import numpy as np, ml_dtypes
CORES = [35,38,43,46]
N = 4
BF = ml_dtypes.bfloat16
L, C, S, F, T, RB = 256, 4096, 2048, 2048, 6, 48
R16 = np.arange(16)[:, None]
def alphabet(rng, A):
    near = rng.integers(0, 256 - A, (8, 16, 1)) + np.arange(A)
    return np.where(rng.random((8, 16, 1)) < 0.5, near, rng.integers(0, 255, (8, 16, A)))
def values(rng, al, n, skew):
    A = al.shape[-1]; ix = np.minimum((A * rng.random((N, 8, 16, n)) ** skew).astype(np.int64), A - 1)
    return np.take_along_axis(np.broadcast_to(al, (N, 8, 16, A)), ix, 3)
def base(rng, A, skew, sizes):
    al = alphabet(rng, A); m = values(rng, al, F, skew); v = values(rng, al, C, skew)
    share = 0.0625 * rng.choice(np.array(sizes), (N, 8, 1, C))
    pt = np.where(rng.random((N, 8, 16, C)) < share, v, 255)
    return rng.integers(0, C, (N, 8, 16, S)), pt, rng.integers(0, C, (N, 8, C)), rng.integers(0, S, (N, 8, C)), m
def keyed(rng):
    h = C // 2; kr = rng.permutation(16)[:8]; b0 = rng.integers(0, 230, 8)
    pt = np.full((N, 8, 16, C), 255); v = rng.integers(0, 255, (N, 8, 16, C - h)); pt[..., h:] = np.where(rng.random(v.shape) < 0.6, v, 255)
    m = rng.integers(0, 255, (N, 8, 16, F))
    for g in range(8):
        pt[:, g, kr[g], :h] = b0[g] + np.arange(h) % 16
        pt[:, g, kr[g], h:] = np.where(rng.random((N, C - h)) < 0.8, b0[g] + np.arange(h, C) % 20, 255)
        m[:, g, kr[g]] = b0[g] + np.arange(F) % 20
    cl = 16 * rng.integers(0, h // 16, (N, 8, 16, S)) + R16
    return cl, pt, rng.integers(h, C, (N, 8, C)), rng.integers(0, S, (N, 8, C)), m
def message(rng, key):
    return key + 20 * rng.integers(0, F // 20, key.shape)
def edge(rng, lo, hi, shape, share):
    return np.where(rng.random(shape) < share, np.where(rng.random(shape) < 0.5, lo, hi), rng.integers(lo, hi + 1, shape))
def boxes(n, ids):
    return np.where(R16 < n[:, :, None, :], ids, 0)
def pack(cl, pt, bo, gs, m, q, n, p, s, w):
    i4 = lambda a: np.ascontiguousarray(a).astype(np.int32)
    bf = lambda a: np.ascontiguousarray(a.reshape(N, 128, -1)).astype(np.float32).astype(BF)
    return {"cl": i4(cl.reshape(N, 128, S)), "pt": bf(pt), "bo": i4(bo), "gs": i4(gs), "m0": bf(m), "q0": i4(q.reshape(N, 128, L)), "n0": i4(n), "p0": i4(p), "s0": i4(s), "w0": i4(w)}
def setup_inputs(rng):
    cl, pt, bo, gs, m = base(rng, 3, 1, [3, 3, 4, 4, 5, 6, 16])
    n = rng.choice(np.array([0, 1, 1, 2, 2, 3, 4, 6, 10, 15, 16, 16]), (N, 8, L))
    p = np.where(rng.random(n.shape) < 0.7, 0, (rng.random(n.shape) * (n + 1)).astype(np.int64)); p = np.minimum(p, n)
    w = np.where(rng.random(n.shape) < 0.6, 0, rng.integers(0, RB + 16, n.shape))
    return pack(cl, pt, bo, gs, m, boxes(n, rng.integers(0, F, (N, 8, 16, L))), n, p, rng.integers(0, S, n.shape), w)
def setup_inputs_spread(rng):
    cl, pt, bo, gs, m = base(rng, 16, 3, [2, 2, 3, 3, 4, 6, 16])
    cl = (C * rng.random(cl.shape) ** 2).astype(np.int64); bo = (C * rng.random(bo.shape) ** 3).astype(np.int64); gs = (S * rng.random(gs.shape) ** 2).astype(np.int64)
    n = np.minimum((17 * rng.random((N, 8, L)) ** 2).astype(np.int64), 16); p = np.minimum((rng.random(n.shape) * (n + 1)).astype(np.int64), n)
    s = np.minimum((S * rng.random(n.shape) ** 4).astype(np.int64), S - 1); w = rng.integers(0, RB + 16, n.shape)
    ids = (F * rng.random((N, 8, 16, L)) ** 2).astype(np.int64)
    return pack(np.minimum(cl, C - 1), pt, np.minimum(bo, C - 1), np.minimum(gs, S - 1), m, boxes(n, np.minimum(ids, F - 1)), n, p, s, w)
def setup_inputs_ends(rng):
    cl = edge(rng, 0, C - 1, (N, 8, 16, S), 0.7); bo = edge(rng, 0, C - 1, (N, 8, C), 0.7); gs = edge(rng, 0, S - 1, (N, 8, C), 0.7); m = edge(rng, 0, 254, (N, 8, 16, F), 0.9)
    v = rng.choice(np.array([0.3, 0.5, 0.6, 0.7, 0.8]), (N, 8, 1, C)); shape = (N, 8, 16, C)
    pt = np.where(rng.random(shape) < v, 255, np.where(rng.random(shape) < 0.5, 0, 254)); pt = np.where(rng.random(shape) < 0.04, rng.integers(0, 256, shape), pt)
    rr = np.array([0, 7, 15]); e0 = rng.choice(np.array([0, 254]), (8, 3)); e1 = rng.choice(np.array([0, 254]), (8, 3)); e1[:, 0] = 254 - e0[:, 0]
    pt[..., 0] = 255; pt[..., C - 1] = 255
    for g in range(8):
        pt[:, g, rr, 0] = e0[g]; pt[:, g, rr, C - 1] = e1[g]
    m[:, 7, rr, 0] = e0[7]; m[:, 7, rr, F - 1] = e1[7]
    cl[:, 7, :, 0] = C - 1; cl[:, 7, :15, S - 1] = 0; cl[:, 7, 15, S - 1] = C - 1; gs[:, 7, C - 1] = S - 1; bo[:, 7, C - 1] = C - 1
    shape = (N, 8, L)
    n = np.where(rng.random(shape) < 0.8, rng.choice(np.array([0, 16, 16]), shape), rng.choice(np.array([1, 2, 15]), shape))
    p = np.where(rng.random(shape) < 0.8, np.where(rng.random(shape) < 0.7, 0, n), np.maximum(n - 1, 0))
    s = edge(rng, 0, S - 1, shape, 0.7)
    w = np.where(rng.random(shape) < 0.75, np.where(rng.random(shape) < 0.6, 0, RB + 15), rng.choice(np.array([RB - 2, RB - 1, RB - 1, RB]), shape))
    ids = edge(rng, 0, F - 1, (N, 8, 16, L), 0.7)
    a = np.array([0, 1, L // 2, L - 2, L - 1]); b = np.array([2, 3, L - 3])
    for z, st, x in ((a, S - 1, F - 1), (b, 0, 0)):
        s[:, 7, z] = st; n[:, 7, z] = 16; p[:, 7, z] = 15; w[:, 7, z] = RB - 1; ids[:, 7, 15, z] = x
    return pack(cl, pt, bo, gs, m, boxes(n, ids), n, p, s, w)
def setup_inputs_corners(rng):
    cl, pt, bo, gs, m = base(rng, 3, 1, [3, 3, 4, 4, 5, 6, 16])
    n = rng.choice(np.array([0, 1, 15, 16]), (N, 8, L)); p = np.choose(rng.integers(0, 3, n.shape), [0 * n, n, np.maximum(n - 1, 0)])
    w = rng.choice(np.array([0, 1, RB - 17, RB - 16, RB - 1, RB, RB + 15]), n.shape); q = boxes(n, rng.integers(0, F, (N, 8, 16, L)))
    s = np.ascontiguousarray(np.argsort(rng.random((N, 8, S)), axis=-1)[..., :L])
    for a in range(N):
        for g in range(8):
            x = np.take_along_axis(q[a, g], np.minimum(p[a, g], 15)[None, :], 0)[0]; o = rng.permutation(C); ex, ne = o[:L], o[L:2 * L]
            v = m[a, g][:, x]; r = rng.integers(0, 16, L); off = np.where(R16 == r, np.where(v < 254, v + 1, v - 1), v)
            hide = (rng.random((16, L)) < 0.5) & (R16 != r) & (rng.random(L) < 0.5)
            pt[a, g][:, ex] = v; pt[a, g][:, ne] = np.where(hide, 255, off)
            first = np.choose(rng.integers(0, 4, L), [16, 15, 0, 1])
            cl[a, g][:, s[a, g]] = np.where(R16 < first, ne, ex)
    return pack(cl, pt, bo, gs, m, q, n, p, s, w)
def setup_inputs_crowd(rng):
    cl, pt, bo, gs, m = keyed(rng); shape = (N, 8, L); a = np.arange(N)
    key = rng.integers(0, 20, (N, 8, 16, L)); key[:, :6] = 0; key[:, 2:4] = 16
    n = rng.integers(0, 17, shape); n[:, :6] = 16; p = np.zeros(shape, np.int64); w = np.zeros(shape, np.int64)
    s = rng.integers(0, S, shape); s[:, :6] = rng.integers(0, S, (N, 6, 1))
    ids = message(rng, key); same = np.array(ids[:, :6, :1, :1]); ids[:, :6] = same
    one = rng.integers(0, L, (N, 8))
    ids[a, 1, :, one[:, 1]] = 19; ids[a, 3, :, one[:, 3]] = 0
    w[:, 4] = RB; w[a, 4, one[:, 4]] = RB - 1
    p[::2, 5] = 16; p[a[::2], 5, one[::2, 5]] = 15; n[a[::2], 5, one[::2, 5]] = 15
    s[:, 6] = rng.choice(np.array([0, S - 1]), (N, L)); ids[:, 6] = rng.choice(np.array([0, 20 * (F // 20) - 20]), (N, 16, L)); gs[:, 6] = rng.choice(np.array([0, S - 1]), (N, C))
    cl[:, 6, :, 0] = 16 * rng.integers(0, C // 32, (N, 1)); cl[:, 6, :, S - 1] = 16 * rng.integers(0, C // 32, (N, 1)); cl[:, 6, 0, S - 1] += 1
    z = (rng.integers(0, N) + np.arange(2)) % N; y = np.array([0, 1, 2, 3, 4, 5, 7])
    n[z] = rng.integers(1, 17, (2, 8, L)); p[z] = 0; w[z] = 0
    ids[z[:, None], y, 0] = message(rng, rng.integers(0, 16, (2, 7, L)))
    for r in range(N):
        if r not in z: pt[r, 7, :, C // 2::4] = 0
    return pack(cl, pt, bo, gs, m, boxes(n, ids), n, p, s, w)
def setup_inputs_calm(rng):
    cl, pt, bo, gs, m = keyed(rng); shape = (N, 8, L); i = np.arange(L)
    e = ((np.arange(8) + np.arange(N)[:, None]) % 4)[:, :, None] + 0 * i
    ty = (i + rng.integers(0, 8, (N, 8, 1))) % 8; j = T - 2 - e % 2
    fj = np.where(R16 < j[:, :, None], 0, 16)
    key = np.choose(ty[:, :, None], [0, fj, fj, 0, 16, 16, 0, rng.integers(0, 20, (N, 8, 16, L))])
    n = np.choose(ty, [16, 16, 16, 16, e + 1, 16, e, rng.integers(14, 17, shape)])
    p = np.choose(ty, [0, 0, 0, 0, 0, 10 + e, 0, np.minimum((rng.random(shape) * (n + 1)).astype(np.int64), n)])
    w = np.choose(ty, [RB - (T - 1 - e), RB - 1 - j, RB - 2 - j, RB - T + e % 2, 0, 0, e, rng.integers(0, RB + 16, shape)])
    return pack(cl, pt, bo, gs, m, boxes(n, message(rng, key)), n, p, rng.integers(0, S, shape), w)
def check_inputs(d):
    bad = []
    for k, lo, hi in (("cl", 0, C - 1), ("pt", 0, 255), ("bo", 0, C - 1), ("gs", 0, S - 1), ("m0", 0, 254), ("q0", 0, F - 1), ("n0", 0, 16), ("p0", 0, 16), ("s0", 0, S - 1), ("w0", 0, RB + 15)):
        v = np.asarray(d[k]).astype(np.float64)
        if not np.all((v >= lo) & (v <= hi)): bad.append("range of " + k)
    for k in ("pt", "m0"):
        v = np.asarray(d[k]).astype(np.float64)
        if np.any(v != np.floor(v)): bad.append("whole numbers of " + k)
    if np.any(d["p0"] > d["n0"]): bad.append("p0 at most n0")
    n = d["n0"].astype(np.int64)[:, :, None, :]; q = d["q0"].astype(np.int64).reshape(N, 8, 16, L)
    if np.any(np.where(R16 >= n, q, 0) != 0): bad.append("0 in empty places of q0")
    return bad
def reference(cl, pt, bo, gs, m0, q0, n0, p0, s0, w0):
    lists_ = cl.astype(np.int64).reshape(N, 8, 16, S); tp = pt.astype(np.float32).astype(np.int64).reshape(N, 8, 16, C)
    M = np.zeros((N, 8, 16, F + T * L), np.int64); M[..., :F] = m0.astype(np.float32).astype(np.int64).reshape(N, 8, 16, F)
    q = q0.astype(np.int64).reshape(N, 8, 16, L); n = n0.astype(np.int64); p = p0.astype(np.int64); s = s0.astype(np.int64); w = w0.astype(np.int64)
    body = bo.astype(np.int64); nxt = gs.astype(np.int64)
    for t in range(T):
        rest = w >= RB; act = ~rest & (p < n)
        x = np.take_along_axis(q, np.minimum(p, 15)[:, :, None, :], 2)
        m = np.take_along_axis(M, x, 3)
        c = np.take_along_axis(lists_, s[:, :, None, :], 3)
        ok = np.ones((N, 8, 16, L), bool)
        for row in range(16):
            g = np.take_along_axis(tp[:, :, row], c.reshape(N, 8, 16 * L), 2).reshape(N, 8, 16, L)
            ok &= (g == 255) | (g == m[:, :, row][:, :, None, :])
        found = act & np.any(ok, axis=2); fail = act & ~found; k = np.argmax(ok, axis=2)
        c1 = np.take_along_axis(c, k[:, :, None, :], 2)[:, :, 0]
        b = np.take_along_axis(tp, np.take_along_axis(body, c1, 2)[:, :, None, :], 3)
        out = np.where(found[:, :, None, :], np.where(b == 255, m, b), 0)
        w = np.where(rest, 0, np.where(found, w + k + 1, np.where(fail, w + 16, w)))
        s = np.where(found, np.take_along_axis(nxt, c1, 2), s)
        up = np.concatenate([q[:, :, 1:], np.zeros((N, 8, 1, L), np.int64)], axis=2)
        q = np.where(found[:, :, None, :] & (R16 >= p[:, :, None, :]), up, q)
        n = n - found; p = np.where(found, 0, np.where(fail, p + 1, p))
        d = 1 + t % (N - 1)
        M[..., F + L * t:F + L * (t + 1)] = np.roll(out, d, axis=0)
        keep = np.roll(found, d, axis=0) & (n < 16)
        q = np.where(keep[:, :, None, :] & (R16 == n[:, :, None, :]), F + L * t + np.arange(L), q)
        n = n + keep
    return {"mn": np.ascontiguousarray(M[..., F:]).reshape(N, 128, T * L).astype(np.float32).astype(BF), "yq": q.reshape(N, 128, L).astype(np.float32),
            "ys": np.concatenate([s, p, n, w], axis=2).astype(np.float32)}

@@ -1,0 +1,760 @@
+import numpy as np
+from concourse.bass import DstId, RemoteDMATransfer
+from concourse.mybir import dt, AluOpType, AxisListType, ActivationFunctionType
+
+AL = AluOpType
+AF = ActivationFunctionType
+NS = 6
+EX = 1
+PIECES = ((0, 128),)
+GP = ((0, 32), (32, 64), (64, 96), (96, 128))
+HH = float(2 ** 40)
+F32, BF, F16, I32, U16 = "float32", "bfloat16", "float16", "int32", "uint16"
+BYTES = {F32: 4, BF: 2, F16: 2, I32: 4, U16: 2}
+
+SCRATCH = {
+    "PW": ("sbuf", [128, 4096], BF), "BW": ("sbuf", [128, 5120], BF), "CW": ("sbuf", [128, 5120], F32),
+    "CLs": ("sbuf", [128, 2048], I32), "MW": ("sbuf", [128, 3584], BF), "GW": ("sbuf", [128, 4864], I32),
+    "SND": ("sbuf", [128, 1536], BF), "MO": ("sbuf", [128, 1536], BF), "CT": ("sbuf", [128, 32 * 12], BF),
+    "BOi": ("sbuf", [128, 256], I32), "GSi": ("sbuf", [128, 256], I32), "BOu": ("sbuf", [128, 256], U16), "GSu": ("sbuf", [128, 256], U16),
+    "Qi": ("sbuf", [128, 256], I32), "STi": ("sbuf", [128, 256], I32), "S0i": ("sbuf", [128, 256], I32), "S0f": ("sbuf", [128, 256], F32),
+    "ONE": ("sbuf", [128, 128], BF), "ZER": ("sbuf", [128, 384], BF), "SHp": ("sbuf", [128, 128], F16), "IDq": ("sbuf", [128, 128], BF), "ID": ("sbuf", [128, 128], BF), "IDh": ("sbuf", [128, 128], F16),
+    "ID16": ("sbuf", [128, 128], F32), "SID": ("sbuf", [128, 128 * 24], BF), "SH0": ("sbuf", [128, 128], BF), "SHh": ("sbuf", [128, 128], F16),
+    "PI": ("sbuf", [128, 16], I32), "CC": ("sbuf", [128, 32], F32), "IO16": ("sbuf", [128, 16], F32), "IOG": ("sbuf", [128, 128], F32),
+    "LR": ("sbuf", [128, 128], F32), "LR2": ("sbuf", [128, 128], F32), "IN8": ("sbuf", [128, 16], F32), "IN16": ("sbuf", [128, 8], F32),
+    "INe": ("sbuf", [128, 8], BF), "INp": ("sbuf", [128, 8], BF), "INh": ("sbuf", [128, 8], F16), "I8f": ("sbuf", [128, 8], F32),
+    "G8": ("sbuf", [128, 128], BF), "BC": ("sbuf", [128, 640], BF), "FW": ("sbuf", [128, 240], F16),
+    "HZ": ("sbuf", [128, 72], F16), "HQ": ("sbuf", [128, 72], F16), "WM": ("sbuf", [128, 360], BF), "WX": ("sbuf", [128, 24], F32),
+    "HI": ("sbuf", [128, 32], F32), "YO": ("sbuf", [128, 8], U16), "YF": ("sbuf", [128, 8], F32), "RST": ("sbuf", [128, 128], F32),
+    "YQ": ("sbuf", [128, 256], F32), "YS": ("sbuf", [128, 256], F32), "YP": ("sbuf", [128, 256], F32),
+}
+for _h in range(2):
+    for _n, _sh, _d in (("P", [128, 2048], BF), ("EQ", [128, 2048], BF), ("CU", [128, 128], U16), ("MS", [128, 256], BF),
+                        ("RS", [128, 128], F32), ("CI", [128, 64], I32), ("CF", [128, 64], F32), ("VC", [128, 32], F32),
+                        ("Y", [128, 128], F16), ("OF", [128, 32], U16), ("R0", [128, 128], BF), ("S1", [128, 128], BF),
+                        ("S2", [128, 128], BF), ("SX", [128, 128], F32), ("Q", [128, 128], F16), ("M1", [128, 128], BF),
+                        ("M2", [128, 128], F16), ("M3", [128, 128], BF), ("T1", [128, 128], F32), ("ZX", [128, 128], F16),
+                        ("QF", [128, 256], F32)):
+        SCRATCH["%s%d" % (_n, _h)] = ("sbuf", _sh, _d)
+    for _n in ("MP", "KY", "XA", "XB"):
+        SCRATCH["%s%d" % (_n, _h)] = ("psum", [128, 512], F32)
+
+SEMAPHORES = ["cV", "cA", "cP", "cG", "loc"] + ["d%d" % i for i in range(48)] + ["ad%d" % i for i in range(12)] + ["af%d" % i for i in range(12)]
+
+CYC, PCYC, GTH, LAT = 1.0, 0.7, 1.56, 90.0
+
+
+def o(b, c0=0, c1=None, st=1, p0=0, p1=128):
+    if c1 is None:
+        c1 = SCRATCH[b][1][1]
+    return (b, p0, p1, c0, c1, st, None)
+
+
+def o3(b, l0, l1, k0, k1):
+    return (b, 0, 128, l0, l1, 1, (k0, k1))
+
+
+def nel(x):
+    n = len(range(x[3], x[4], x[5]))
+    if x[6] is not None:
+        n *= x[6][1] - x[6][0]
+    return n
+
+
+def two(x):
+    return BYTES[SCRATCH[x[0]][2]] == 2
+
+
+def isps(x):
+    return SCRATCH[x[0]][0] == "psum"
+
+
+def span(x):
+    if len(SCRATCH[x[0]][1]) == 3:
+        k = x[6] if x[6] is not None else (0, 16)
+        return (x[1], x[2], x[3], x[4], k[0], k[1])
+    return (x[1], x[2], x[3], x[3] + (len(range(x[3], x[4], x[5])) - 1) * x[5] + 1, 0, 1)
+
+
+def meet(a, b):
+    return a[0] < b[1] and b[0] < a[1] and a[2] < b[3] and b[2] < a[3] and a[4] < b[5] and b[4] < a[5]
+
+
+def build():
+    ops = []
+    hist = {}
+    bank = {}
+    lastpe = {}
+    ctx = ["", {}]
+
+    def add(eng, kind, args, reads, writes, cost, lat=0.0, after=()):
+        i = len(ops)
+        deps = {}
+        dma = kind in ("dma", "rdma")
+
+        def dep(j, raw):
+            if j == i:
+                return
+            pj = ops[j]
+            w = raw or pj["eng"] != eng or dma or pj["kind"] in ("dma", "rdma")
+            if pj["eng"] == "P" and eng == "P":
+                w = False
+            deps[j] = deps.get(j, False) or w
+        for x, wr in [(x, False) for x in reads] + [(x, True) for x in writes]:
+            s = span(x)
+            hl = hist.setdefault(x[0], [])
+            for (j, s2, w2) in hl:
+                if (wr or w2) and meet(s, s2):
+                    dep(j, w2)
+            if isps(x):
+                b = bank.setdefault(x[0], [None, [], []])
+                if b[0] != eng:
+                    b[0], b[2], b[1] = eng, b[1], []
+                for j in b[2]:
+                    dep(j, True)
+                if i not in b[1]:
+                    b[1].append(i)
+                if eng == "P":
+                    if x[0] in lastpe:
+                        dep(lastpe[x[0]], False)
+                    lastpe[x[0]] = i
+        for x in writes:
+            s = span(x)
+            hist[x[0]] = [e for e in hist[x[0]] if not (s[0] <= e[1][0] and e[1][1] <= s[1] and s[2] <= e[1][2] and e[1][3] <= s[3]
+                                                        and s[4] <= e[1][4] and e[1][5] <= s[5] and x[5] == 1)]
+        for x in reads:
+            hist[x[0]].append((i, span(x), False))
+        for x in writes:
+            hist[x[0]].append((i, span(x), True))
+        for j in after:
+            deps[j] = deps.get(j, False)
+        nm = args[0][0] if isinstance(args[0], tuple) else args[0][:2]
+        key = (ctx[0], eng, kind, (nm[:-1] if nm[:-1] + "1" in SCRATCH else nm) if ctx[0] else i)
+        ctx[1][key] = ctx[1].get(key, 0) + 1
+        ops.append({"eng": eng, "kind": kind, "args": args, "deps": deps, "cost": cost, "lat": lat, "cls": key + (ctx[1][key],)})
+        return i
+
+    def aps(*xs):
+        return [x for x in xs if isinstance(x, tuple)]
+
+    def ts(out, a, s1, s2, op0, op1=None, ind=None):
+        n = nel(out)
+        c = 60 + n * GTH if ind else max(64, n * (0.5 if two(out) and two(a) else 1))
+        return add("V", "ts", (out, a, s1, s2, op0, op1, ind), aps(a, s1, s2, ind), [out], c * CYC)
+
+    def tt(out, a, b, op, ind=None, after=()):
+        n = nel(out)
+        c = 60 + n * GTH if ind else max(64, n * (1 if isps(a) or isps(b) else 2))
+        return add("V", "tt", (out, a, b, op, ind), aps(a, b, ind), [out], c * CYC, after=after)
+
+    def cp(out, a, ind=None):
+        n = nel(out)
+        c = 60 + n * GTH if ind else max(64, n * (0.5 if two(out) and two(a) else 1))
+        return add("V", "cp", (out, a, ind), aps(a, ind), [out], c * CYC)
+
+    def ms(out, v):
+        return add("V", "ms", (out, v), [], [out], max(64, nel(out) * (0.5 if two(out) else 1)) * CYC)
+
+    def act(out, a, f, scale=1.0, bias=0.0, ind=None, after=()):
+        n = nel(out)
+        c = 78 + n * GTH if ind else max(64, n)
+        return add("A", "act", (out, a, f, scale, bias, ind), aps(a, ind, bias), [out], c * CYC, after=after)
+
+    def mm(out, l, r, s0=True, s1=True):
+        c = max(min(64, nel(l)), nel(r)) * (1 if two(l) else 4)
+        return add("P", "mm", (out, l, r, s0, s1), [l, r], [out], c * PCYC)
+
+    def iota(out, pat, base, cm):
+        return add("G", "iota", (out, pat, base, cm), [], [out], 160 + 2 * nel(out) * CYC)
+
+    def asel(out, a, pat, base, cm):
+        return add("G", "asel", (out, a, pat, base, cm), [a], [out], 210 + 2 * nel(out) * CYC)
+
+    def dma(eng, out, src, rd, wr, nbytes, after=()):
+        return add(eng, "dma", (out, src, nbytes), rd, wr, 60.0, 1900.0, after)
+
+    def col(b, c):
+        return o(b, c, c + 1)
+
+    for k, nm in enumerate(("p0", "n0", "w0")):
+        x = o("STi", p0=8 * k, p1=8 * k + 8)
+        dma("A", x, ("ext", nm, None), [], [x], 8192)
+    x = o("S0i", p1=8)
+    dma("A", x, ("ext", "s0", None), [], [x], 8192)
+    dma("A", o("Qi"), ("ext", "q0", None), [], [o("Qi")], 131072)
+    ld = [dma("S", o("BOi"), ("ext", "bo", None), [], [o("BOi")], 131072)]
+    for k in range(4):
+        x = o("PW", 1024 * k, 1024 * k + 1024)
+        ld = [dma("S", x, ("ext", "pt", (1024 * k, 1024 * k + 1024)), [], [x], 262144, ld)]
+    ld = [dma("S", o("CLs"), ("ext", "cl", None), [], [o("CLs")], 1048576, ld)]
+    ld = [dma("S", o("GSi"), ("ext", "gs", None), [], [o("GSi")], 131072, ld)]
+    ld = [dma("S", o("MW", 0, 2048), ("ext", "m0", None), [], [o("MW", 0, 2048)], 524288, ld)]
+
+    ms(o("ONE"), 1.0)
+    iota(col("PI", 0), [[0, 1]], 0, 1)
+    asel(o("ID"), o("ONE"), [[-1, 128]], 0, 1)
+    iota(o("IO16"), [[1, 16]], 0, 0)
+    iota(o("IOG"), [[1, 8], [0, 16]], 0, 0)
+    iota(o("LR"), [[1, 128]], 0, 0)
+    asel(o("SH0"), o("ONE"), [[-1, 128]], -1, 1)
+    iota(o("LR2"), [[1, 128]], -256, 0)
+    for c, (s, op) in enumerate(((15, AL.bitwise_and), (4, AL.arith_shift_right), (3, AL.arith_shift_right), (7, AL.bitwise_and), (8, AL.bitwise_and))):
+        ts(col("PI", c + 1), col("PI", 0), s, None, op)
+    cp(o("CC", 0, 6), o("PI", 0, 6))
+    cP, cJ, cP16, cP8, cM8, cQ8 = [col("CC", c) for c in range(6)]
+    cJ1, cK, cN0, cJ0, cJ1e, cEB, cQ16 = [col("CC", c) for c in range(6, 13)]
+    ts(cJ1, cJ, 1.0, None, AL.add)
+    ts(cK, cJ, -4096.0, 61440.5, AL.mult, AL.add)
+    ms(col("CC", 14), 128.5 + 2.0 ** -14)
+    ts(cN0, cJ, 0.0, None, AL.is_gt)
+    ts(cJ0, cJ, 0.0, None, AL.is_equal)
+    ts(cJ1e, cJ, 1.0, None, AL.is_equal)
+    ts(cEB, cP16, cM8, None, AL.is_equal)
+    ts(cQ16, cQ8, -16.0, None, AL.add)
+    cL = {}
+    for par in range(2):
+        for h in range(2):
+            cL[par, h] = col("CC", 16 + 2 * par + h)
+            ts(cL[par, h], cP, 2.0, float((4096 if par == 0 else -512) + 256 * h), AL.mult, AL.add)
+    ts(o("IN8"), o("IO16"), cP8, None, AL.is_equal)
+    ts(o("IN16"), o("IO16", 0, 8), cP16, None, AL.is_equal)
+    ts(o("INe"), o("IN16"), float(2 ** 20), None, AL.mult)
+    ts(o("INp"), o("IN16"), -float(2.0 ** -20), None, AL.mult)
+    cp(o("INh"), o("IN16"))
+    cp(o("IDh"), o("ID"))
+    act(o("ID16"), o("ID"), AF.Copy, 16.0)
+    cp(o("I8f"), o("ID", 0, 8))
+    ts(o("G8"), o("IOG"), cM8, None, AL.is_equal)
+    n8 = lambda s: col("IN8", s)
+    tt(col("CC", 21), n8(0), n8(3), AL.add)
+    tt(col("CC", 20), col("CC", 21), n8(10), AL.subtract)
+    tt(col("CC", 24), n8(6), n8(3), AL.subtract)
+    tt(col("CC", 25), col("CC", 24), n8(8), AL.add)
+    ts(col("CC", 26), col("CC", 25), 64.0, n8(1), AL.mult, AL.add)
+    tt(col("CC", 27), n8(3), n8(10), AL.subtract)
+    ts(col("CC", 28), n8(8), -5.0 * 2 ** 24, None, AL.mult)
+    ts(col("CC", 29), col("CC", 27), 2.0 ** 26, col("CC", 28), AL.mult, AL.add)
+    for k, cc in enumerate((n8(5), col("CC", 26), col("CC", 20), n8(0), col("CC", 29))):
+        ts(o("BC", 128 * k, 128 * k + 128), o("G8"), cc, None, AL.mult)
+    ms(o("FW"), 0.0)
+    ts(o("FW", 112, 128), o("IO16"), cJ, None, AL.is_equal)
+    ts(o("YF"), o("IO16", 0, 8), cQ16, cEB, AL.add, AL.mult)
+    ts(o("YO"), o("YF"), 16.0, None, AL.add)
+    ts(o("SH0"), o("SH0"), cN0, 0.5, AL.mult, AL.mult)
+    ts(o("IDq"), o("ID"), 0.5, None, AL.mult)
+    tt(o("SHh"), o("SH0"), o("IDq"), AL.subtract)
+    tt(o("SHp"), o("SH0"), o("IDq"), AL.add)
+    cJh = col("CC", 13)
+    ts(cJh, cJ, 0.5, None, AL.add)
+    ms(o("RST"), 1.0)
+    ms(o("RST", 0, 128, 16), 0.0)
+    ms(o("HZ"), 0.0)
+    ms(o("HQ"), 0.0)
+    for s in range(2):
+        cp(o("HZ", 8 * s, 8 * s + 8), o("IN16"))
+        ts(o("HQ", 16 + 8 * s, 24 + 8 * s), o("IN16"), cJ0, None, AL.mult)
+        ts(o("HQ", 32 + 8 * s, 40 + 8 * s), o("IN16"), cJ1e, None, AL.mult)
+    cp(o("HZ", 48, 56), o("IN16"))
+    ts(o("HQ", 56, 64), o("IN16"), cJ0, None, AL.mult)
+    ts(o("HQ", 64, 72), o("IN16"), cJ1e, None, AL.mult)
+    tt(col("HI", 16), n8(11), n8(12), AL.add)
+    ts(col("HI", 18), col("HI", 16), -2304.0, None, AL.mult)
+    ts(col("HI", 19), col("HI", 16), -128.0, None, AL.mult)
+    ts(o("HI", 4, 16), o("IO16", 0, 12), col("HI", 19), col("HI", 18), AL.mult, AL.add)
+    WR1, W21, W12, W2X, W1F, WXC = 0, 80, 160, 264, 336, 360
+    N1, N2 = 80, 104
+    TW1, TW2, TWX = {3: 8, 4: 9}, {3: 10, 6: 11, 7: 12}, {0: 6, 2: 7, 4: 8}
+    twin = {WR1: ({}, TW1), W21: (TW2, TW1), W12: (TW1, TW2), W2X: (TW2, TWX), W1F: (TW1, {}), WXC: (TWX, {})}
+    ent = [(W21 + 64, 8, -1), (W21 + 72, 8, -1), (W12 + 80, 6, -1)] + [(W2X + 8 * s, 8, -2048) for s in (6, 7, 8)]
+    for (base, lst) in (
+        (WR1, [(0, 0, 64), (0, 1, 1), (1, 2, -1), (0, 3, -1), (2, 3, -64), (1, 4, 1), (0, 5, 64)]),
+        (W21, [(0, 0, 1), (3, 0, 1), (8, 0, -64), (1, 1, 1), (8, 1, -1), (2, 2, 1), (3, 2, 16), (8, 2, 129), (1, 3, -1), (8, 3, 17),
+               (2, 4, -1), (3, 4, -16), (8, 4, -81), (0, 5, 1), (8, 6, 1), (9, 7, 1)]),
+        (W12, [(0, 0, 1), (1, 1, 1), (3, 1, 1), (2, 2, 1), (4, 2, 64), (6, 2, -64), (1, 3, 1), (3, 3, 1), (0, 3, -1), (4, 3, 64), (6, 3, -64),
+               (0, 5, -1), (6, 5, 1), (1, 6, -4096), (3, 6, -4096), (6, 6, 8192),
+               (1, 7, -4096), (3, 7, -4096), (0, 7, 4096), (4, 7, 4096), (6, 7, 4096), (6, 8, 1), (7, 9, 1)]),
+        (W2X, [(7, 0, 1), (7, 1, 1), (9, 1, 1), (8, 1, -2304), (5, 2, -8192), (9, 3, 1), (8, 3, -2304), (5, 3, -8192),
+               (6, 4, 1), (8, 4, -8192), (5, 4, 8192), (6, 5, 1), (9, 5, 1), (8, 5, -2304), (8, 5, -8192), (5, 5, 8192)]),
+        (W1F, [(0, 0, 1), (1, 1, 1), (3, 1, 1), (2, 2, 1)]),
+        (WXC, [(2, 1, 1), (3, 1, 1), (4, 1, 1), (5, 1, 1), (0, 2, 1), (1, 2, 1), (2, 2, -1), (3, 2, -1), (4, 2, -1), (5, 2, -1)]),
+    ):
+        ti, to = twin[base]
+        lst = lst + [(ti[si], so, -v) for (si, so, v) in lst if si in ti]
+        lst = lst + [(si, to[so], v) for (si, so, v) in lst if so in to]
+        ent += [(base + 8 * so, si, v) for (si, so, v) in lst]
+    vals = sorted(set(e[2] for e in ent) - {1})
+    for k, v in enumerate(vals):
+        act(o("SID", 128 * k, 128 * k + 104), o("ID", 0, 104), AF.Copy, float(v))
+    ms(o("ZER"), 0.0)
+    mm(o("XA0", 0, 384), o("ID"), o("ZER", 0, 384), True, False)
+    for k, (c, si, v) in enumerate(ent):
+        r = o("ID", 8 * si, 8 * si + 8) if v == 1 else o("SID", 128 * vals.index(v) + 8 * si, 128 * vals.index(v) + 8 * si + 8)
+        mm(o("XA0", c, c + 8), o("ID"), r, False, k == len(ent) - 1)
+    act(o("WM"), o("XA0", 0, 360), AF.Copy)
+    cp(o("WX"), o("XA0", 360, 384))
+
+    tmpb = ("MP0", "MP1", "KY0", "KY1")
+    for k in range(8):
+        x = o("PW", 512 * k, 512 * k + 512)
+        act(o(tmpb[k % 4]), x, AF.Relu, HH, -254.0 * HH)
+        tt(x, x, o(tmpb[k % 4]), AL.subtract)
+    for b in ("BW", "CW"):
+        iota(o(b, 4608, 5120), [[0, 512]], 0, 0)
+        iota(o(b, 0, 512), [[0, 512]], 0, 0)
+    for k in range(4):
+        iota(o("GW", 1216 * k, 1216 * k + 1216), [[0, 1216]], 0, 0)
+    cp(o("BOu"), o("BOi"))
+    cp(o("GSu"), o("GSi"))
+
+    def cur(t, h):
+        b = (4608 if t % 2 == 0 else 0) + 256 * h
+        return o("CW", b, b + 256, 2)
+
+    def win(b, t):
+        return o(b, 512, 5120) if t % 2 == 0 else o(b, 0, 4608)
+
+    def to_b(t, h, c0, c1):
+        H = str(h)
+        ts(o("Y" + H), o("VC" + H), -2048.0, None, AL.add, None, o("YO"))
+        for gq in range(8):
+            mm(o("KY" + H, 128, 144), o("FW", 112 - 16 * gq, 240 - 16 * gq), o("Y" + H, 16 * gq, 16 * gq + 16), gq == 0, gq == 7)
+        b = 16 * (t % 2)
+        if c0 == c1:
+            ts(o("OF" + H, b, b + 16), o("KY" + H, 128, 144), c0, None, AL.add)
+        else:
+            ts(o("OF" + H, b, b + 8), o("KY" + H, 128, 136), c0, None, AL.add)
+            ts(o("OF" + H, b + 8, b + 16), o("KY" + H, 136, 144), c1, None, AL.add)
+        return o("OF" + H, b, b + 8), o("OF" + H, b + 8, b + 16)
+
+    def message(t, h, off):
+        H = str(h)
+        m = o("MS" + H, 128 * (t % 2), 128 * (t % 2) + 128)
+        top = 2048 if t == 0 else 2048 + 128 * (2 * (t - 1) + h + 1)
+        act(m, o("MW", 0, top), AF.Abs, ind=off)
+        for e in range(EX):
+            mm(o("MP" + H, e, 128 * EX, EX), o("ID"), m)
+
+    def update(t, h):
+        H = str(h)
+        XA, XB = "XA" + H, "XB" + H
+        r0 = o("R0" + H, p1=24)
+        s1 = o("S1" + H, p1=N1)
+        s2 = o("S2" + H, p1=N2)
+        q = o("Q" + H)
+        if t > 0:
+            i = 2 * (t - 1) + h
+            mm(o(XB, 384, 512), o("SHh"), q)
+            mm(o(XA, 0, 128, p1=24), o("CT", 32 * i, 32 * i + 24), o("ID"))
+            act(r0, o(XA, 0, 128, p1=24), AF.Copy)
+        mm(o(XA, 128, 256, p1=N1), o("WM", W21, W21 + N1, p1=N2), s2, True, False)
+        mm(o(XA, 128, 256, p1=N1), o("WM", WR1, WR1 + N1, p1=24), r0, False, True)
+        act(s1, o(XA, 128, 256, p1=N1), AF.Relu)
+        mm(o(XA, 0, 128, p1=N2), o("WM", W12, W12 + N2, p1=N1), s1)
+        ci = 4 + min(2 * t + h, 11)
+        if t > 0:
+            mm(o(XB, 0, 128), o("BC", 0, 128, p1=N1), s1)
+            mm(o(XB, 128, 256), o("BC", 128, 256, p1=N1), s1)
+        act(s2, o(XA, 0, 128, p1=N2), AF.Relu, 1.0, o("HI", ci, ci + 1, p1=N2))
+        if t == NS:
+            mm(o(XA, 128, 256, p1=24), o("WM", W1F, W1F + 24, p1=N1), s1)
+            act(o("YP", 128 * h, 128 * h + 128, p1=24), o(XA, 128, 256, p1=24), AF.Copy)
+            for k in range(3):
+                x = o("YP", 128 * h, 128 * h + 128, p0=8 * k, p1=8 * k + 8)
+                dma("S", ("ext", "ys", (256 * (k + 1) + 128 * h, 256 * (k + 1) + 128 * h + 128)), x, [x], [], 4096)
+        if t > 0:
+            act(o("M1" + H), o(XB, 0, 128), AF.Sign, -1.0, cJh)
+            ts(o("M2" + H), o(XB, 128, 256), cJ, float(2304 + 128 * (2 * (t - 1) + h)), AL.is_equal, AL.mult)
+            tt(o("T1" + H), o("M1" + H), o(XB, 384, 512), AL.mult)
+        if t < NS - 1:
+            mm(o(XA, 384, 512), o("BC", 256, 384, p1=N2), s2)
+            ts(o("M3" + H), o(XA, 384, 512), cJ, None, AL.is_equal)
+        if t > 0:
+            mm(o(XB, 0, 128), o("SHp"), q, True, False)
+            mm(o(XB, 0, 128), o("IDh"), o("M2" + H), False, True)
+            if t == NS:
+                qf, qt = o("QF" + H, 0, 128), o("QF" + H, 128, 256)
+                y = o("YQ", 128 * h, 128 * h + 128)
+                tt(qf, o("T1" + H), o(XB, 0, 128), AL.add)
+                ts(qt, qf, 2048.0, None, AL.is_ge)
+                tt(qt, qt, o("LR2"), AL.mult)
+                tt(y, qt, qf, AL.add)
+                dma("S", ("ext", "yq", (128 * h, 128 * h + 128)), y, [y], [], 65536)
+                return
+            tt(q, o("T1" + H), o(XB, 0, 128), AL.add)
+        if t < NS - 1:
+            mm(o(XB, 128, 256), o("IDh"), q)
+            tt(o("ZX" + H), o("M3" + H), o(XB, 128, 256), AL.mult)
+            lx = o(XA, 128, 256, p1=72)
+            mm(lx, o("WM", W2X, W2X + 72, p1=N2), s2, True, False)
+            mm(lx, o("HQ"), q, False, False)
+            mm(lx, o("HZ"), o("ZX" + H), False, True)
+            act(o("SX" + H, p1=72), lx, AF.Relu)
+            mm(o(XB, 256, 272), o("SX" + H, p1=72), o("WX", 8, 24, p1=72))
+
+    def start(h):
+        H = str(h)
+        XA, XB = "XA" + H, "XB" + H
+        s2 = o("S2" + H, p1=N2)
+        ts(o("S2" + H), o("LR"), n8(9), n8(8), AL.mult, AL.add)
+        cp(o("S2" + H, p1=24), o("STi", 128 * h, 128 * h + 128, p1=24))
+        ts(col("CC", 22 + h), n8(1), 128.0, 1.0, AL.mult, AL.add)
+        ts(o("R0" + H), o("ONE"), col("CC", 22 + h), None, AL.mult)
+        cp(o("Q" + H), o("Qi", 128 * h, 128 * h + 128))
+        cp(o("S0f", 128 * h, 128 * h + 128, p1=8), o("S0i", 128 * h, 128 * h + 128, p1=8))
+        ms(o("VC" + H, 16, 32), 2048.0)
+        ts(o("CF" + H, 32, 40), o("IO16", 0, 8), 0.0, cL[0, h], AL.mult, AL.add)
+        mm(o(XB, 256, 384), o("BC", 384, 512, p1=N2), s2)
+        mm(o(XB, 128, 256), o("IDh"), o("Q" + H))
+        ts(o("M3" + H), o(XB, 256, 384), cJ, None, AL.is_equal)
+        tt(o("ZX" + H), o("M3" + H), o(XB, 128, 256), AL.mult)
+        mm(o(XA, 256, 264), o("S0f", 128 * h, 128 * h + 128, p1=8), o("I8f", p1=8))
+        mm(o(XA, 264, 272), o("ZX" + H), o("INh"))
+        cp(o("VC" + H, 0, 16), o(XA, 256, 272))
+        f0, f1 = to_b(1, h, 2048.0, 2048.0)
+        ts(cur(0, h), o("CLs"), cK, None, AL.add, None, f0)
+        message(0, h, f1)
+        update(0, h)
+
+    def tables():
+        for k in range(8):
+            x, f = o("CW", 512 + 512 * k, 1024 + 512 * k), o("GSu", 32 * k, 32 * k + 32)
+            chain["V"].append(ts(x, o("CLs"), cK, None, AL.add, None, f))
+            chain["A"].append(act(o("BW", 512 + 512 * k, 1024 + 512 * k), o("PW"), AF.Copy, -1.0, ind=o("BOu", 32 * k, 32 * k + 32)))
+        x = o("GW", 0, 4096)
+        dma("S", ("rows", "GW", 0, 4096), ("ext", "gs", None), [], [x], 131072)
+        x = o("GW", 4608, 4864)
+        dma("S", ("rows", "GW", 4608, 4864), ("ext", "s0", None), [], [x], 8192)
+        cp(o("GW", 4096, 4608, 2), x)
+
+    chain = {"A": [], "V": []}
+
+    def wide(t, h):
+        H = str(h)
+        P, EQ, KY = "P" + H, "EQ" + H, "KY" + H
+        ts(o("CU" + H), cur(t, h), cK, None, AL.subtract)
+        mm(o(KY, 0, 128), cur(t, h), o("ID16"), True, False)
+        for (a, b) in GP:
+            chain["A"] = [act(o(P, 16 * a, 16 * b), o("PW"), AF.Copy, ind=o("CU" + H, a, b), after=chain["A"])]
+        st = 16 // EX
+        for (a, b) in PIECES:
+            for k in range(st):
+                c = 128 * EX * k
+                chain["V"] = [tt(o(EQ, c + EX * a, c + EX * b), o(P, 16 * a + k, 16 * b, st), o("MP" + H, EX * a, EX * b), AL.is_equal, after=chain["V"])]
+        for k in range(16):
+            mm(o(KY, k, 128, 16), o(P, k, 2048, 16), o("INp"), False, False)
+        for k in range(16):
+            kk = k // EX + st * (k % EX)
+            c = 128 * EX * (k // EX)
+            mm(o(KY, kk, 128, 16), o(EQ, c + k % EX, c + 128 * EX, EX), o("INe"), False, False)
+        mm(o(KY, 0, 128), o("S2" + H, p1=N2), o("BC", 512, 640, p1=N2), False, True)
+
+    def choose(t, h):
+        H = str(h)
+        i = 2 * t + h
+        XA = "XA" + H
+        ci = lambda k: o("CI" + H, 8 * k, 8 * k + 8)
+        cf = lambda k: o("CF" + H, 8 * k, 8 * k + 8)
+        add("V", "scan", (o("RS" + H), o("RST"), o("KY" + H, 0, 128)), [o("RST"), o("KY" + H, 0, 128)], [o("RS" + H)], 128 * CYC)
+        rs = o("RS" + H, 15, 128, 16)
+        nf = o("CT", 32 * i, 32 * i + 8)
+        cp(ci(1), rs)
+        ts(nf, rs, 4.0, None, AL.is_lt)
+        ts(cf(0), rs, 4.0, cL[t % 2, h], AL.is_lt, AL.mult)
+        ts(ci(2), ci(1), 4080, None, AL.bitwise_and)
+        ts(ci(3), ci(1), 12, 15, AL.arith_shift_right, AL.bitwise_and)
+        ts(ci(4), ci(1), 4, 4095, AL.arith_shift_right, AL.bitwise_and)
+        land = o("CT", 32 * i + 16, 32 * i + 24)
+        j = add("G", "rdma", (land, nf, t, "af%d" % i), [nf], [], 500.0, 0.0)
+        add("X", "arr", ("af%d" % i,), [], [land], 0.0, 2600.0, after=[j])
+        tt(cf(1), ci(2), cf(0), AL.add)
+        tt(o("VC" + H, 0, 8), ci(3), cf(1), AL.add)
+        tt(cf(3), nf, cf(4), AL.mult)
+        if t < NS - 1:
+            tt(cf(2), nf, o("XB" + H, 264, 272), AL.mult)
+            tt(o("VC" + H, 8, 16), cf(2), o("XB" + H, 256, 264), AL.add)
+            tt(cf(4), cf(3), ci(4), AL.add)
+        else:
+            tt(o("VC" + H, 8, 16), cf(3), ci(4), AL.add)
+        act(o("CT", 32 * i + 8, 32 * i + 16), rs, AF.Identity, 2.0 ** -16, col("CC", 14))
+        f0, f1 = to_b(t, h, 2048.0 if t % 2 == 0 else 2560.0, 2048.0)
+        if t < NS - 1:
+            act(cur(t + 1, h), win("CW", t), AF.Copy, ind=f0)
+        snd = o("SND", 128 * i, 128 * i + 128)
+        tt(snd, win("BW", t), o("MS" + H, 128 * (t % 2), 128 * (t % 2) + 128), AL.min, f0)
+        land = o("MW", 2048 + 128 * i, 2048 + 128 * i + 128)
+        j = add("G", "rdma", (land, snd, t, "ad%d" % i), [snd], [], 500.0, 0.0)
+        add("X", "arr", ("ad%d" % i,), [], [land], 0.0, 3200.0, after=[j])
+        if t < NS - 1:
+            message(t + 1, h, f1)
+        else:
+            y = o("YS", 128 * h, 128 * h + 128)
+            cp(y, o("GW", 0, 4608), f1)
+            dma("S", ("ext", "ys", (128 * h, 128 * h + 128)), ("rows", "YS", 128 * h, 128 * h + 128), [y], [], 4096)
+        if t == NS - 1 or h == 1:
+            a = i if t == NS - 1 else i - 1
+            x = o("MO", 128 * a, 128 * i + 128)
+            act(x, o("MW", 2048 + 128 * a, 2048 + 128 * i + 128), AF.Abs)
+            dma("S", ("ext", "mn", (128 * a, 128 * i + 128)), x, [x], [], 32768 * (i - a + 1))
+
+    start(0)
+    start(1)
+    tables()
+    for t in range(NS):
+        for h in range(2):
+            ctx[0], ctx[1] = ("step" if t < NS - 1 else "last%d" % h), {}
+            wide(t, h)
+            choose(t, h)
+            update(t + 1, h)
+    return ops
+
+
+def plan(ops, rounds=150, climbs=800):
+    n = len(ops)
+    succ = [[] for _ in range(n)]
+    left = [len(p["deps"]) for p in ops]
+    for i, p in enumerate(ops):
+        for j in p["deps"]:
+            succ[j].append(i)
+    dur = [p["cost"] + p["lat"] + (p["args"][2] / 250.0 if p["kind"] == "dma" else 0.0) for p in ops]
+    lvl = [0.0] * n
+    for i in range(n - 1, -1, -1):
+        lvl[i] = dur[i] + max([lvl[k] + (LAT if ops[k]["deps"][i] else 0.0) for k in succ[i]] + [0.0])
+    best = None
+    rng = np.random.default_rng(1)
+    for it in range(rounds):
+        if it < 200 or it % 2 == 0:
+            fa, fv = 1.0 + 0.8 * float(rng.random()), 1.0 + 2.0 * float(rng.random())
+            la = LAT * (1.0 + 3.0 * float(rng.random()))
+            z = rng.random(n) * (0.0, 50.0, 200.0)[it % 3]
+            pr = [0.0] * n
+            for i in range(n - 1, -1, -1):
+                nm = ops[i]["args"][0][0]
+                d = dur[i] * (fa if nm in ("P0", "P1") else fv if nm in ("EQ0", "EQ1") else 1.0)
+                pr[i] = d + max([pr[k] + (la if ops[k]["deps"][i] else 0.0) for k in succ[i]] + [0.0])
+            up = {"BOu": 1e5, "PW": 4000.0}
+            ba, bv = 6000.0 * float(rng.random()), 6000.0 * float(rng.random())
+            for nm in ("R0", "S1", "S2", "M1", "MS", "CW"):
+                up[nm] = ba
+            for nm in ("T1", "M2", "M3", "Q", "ZX", "SX"):
+                up[nm] = bv
+            pr = [pr[i] + float(z[i]) + up.get(ops[i]["cls"][3] if ops[i]["cls"][0] else ops[i]["args"][0][0], 0.0) for i in range(n)]
+        else:
+            o2, beg, fin = best[1:]
+            nxt = {}
+            late = [0.0] * n
+            end = best[0]
+            for i in reversed(o2):
+                p = ops[i]
+                f = min([late[k] - (LAT if ops[k]["deps"][i] or ops[k]["eng"] != p["eng"] else -p["cost"]) for k in succ[i]] + [end])
+                s = f - dur[i]
+                if p["eng"] != "X" and it % 2 == 1:
+                    s = min(s, nxt.get(p["eng"], end) - p["cost"])
+                    nxt[p["eng"]] = s
+                late[i] = s
+            amp = (100.0, 300.0, 800.0)[it % 3]
+            z = rng.random(n)
+            mix = float(rng.random())
+            pr = [-(mix * late[i] + (1 - mix) * (end - lvl[i])) + amp * float(z[i]) for i in range(n)]
+        r = once(ops, succ, list(left), pr, (60.0, 150.0, 300.0)[(it // 3) % 3])
+        if best is None or max(r[2]) < best[0]:
+            best = (max(r[2]),) + r
+            keep = (pr, (60.0, 150.0, 300.0)[(it // 3) % 3])
+    names = {}
+    cls = np.array([names.setdefault(p["cls"], len(names)) for p in ops])
+    small = [k for k in range(len(names)) if any(p["eng"] in "VAG" for p in ops if names[p["cls"]] == k)]
+    rep = [k for k in small if int((cls == k).sum()) > 2]
+    base = np.array(keep[0])
+    delta = np.zeros(len(names))
+    for it in range(climbs):
+        d = delta.copy()
+        pool = rep if it % 3 else small
+        for k in range(1 + it % 4):
+            d[pool[int(rng.integers(len(pool)))]] += float(rng.normal()) * (300.0, 1000.0, 3000.0)[it % 3]
+        r = once(ops, succ, list(left), [float(v) for v in base + d[cls]], keep[1])
+        if max(r[2]) <= best[0]:
+            best = (max(r[2]),) + r
+            delta = d
+    return best[1:]
+
+
+def once(ops, succ, left, lvl, slack):
+    n = len(ops)
+    free = {}
+    fin = [0.0] * n
+    beg = [0.0] * n
+    est = {}
+    order = []
+    bus = 0.0
+    for i in range(n):
+        if left[i] == 0:
+            est[i] = 0.0
+    while est:
+        b = min(est, key=lambda i: (max(est[i], free.get(ops[i]["eng"], 0.0)), i))
+        e = ops[b]["eng"]
+        t0 = max(est[b], free.get(e, 0.0))
+        c = [i for i in est if ops[i]["eng"] == e and est[i] <= t0 + min(slack, 0.5 * ops[b]["cost"] + 40.0)]
+        i = max(c, key=lambda k: (lvl[k], -k))
+        s = max(est[i], free.get(e, 0.0))
+        p = ops[i]
+        beg[i] = s
+        if e != "X":
+            free[e] = s + p["cost"]
+        if p["kind"] == "dma":
+            bus = max(bus, s + p["lat"]) + p["args"][2] / 250.0
+            fin[i] = bus
+        else:
+            fin[i] = s + p["cost"] + p["lat"]
+        del est[i]
+        order.append(i)
+        for k in succ[i]:
+            left[k] -= 1
+            if left[k] == 0:
+                est[k] = max((fin[j] + LAT if w or ops[j]["eng"] != ops[k]["eng"] else beg[j]) for j, w in ops[k]["deps"].items())
+    return order, beg, fin
+
+
+CACHE = {}
+
+
+def rank_program(g, core, T, topo):
+    rank = T.rank_of(core)
+    if rank is None:
+        return
+    if "ops" not in CACHE:
+        CACHE["ops"] = build()
+        CACHE["order"] = plan(CACHE["ops"])[0]
+    ops, order = CACHE["ops"], CACHE["order"]
+    nr = len(T.cores)
+    qs = {"V": g.vector, "A": g.scalar, "P": g.tensor, "G": g, "S": g.sync}
+    dest = [T.cores[(rank + 1 + t % (nr - 1)) % nr] for t in range(NS)]
+    srcs = [T.cores[(rank - 1 - t % (nr - 1)) % nr] for t in range(NS)]
+    engs = set(range(16))
+    for a in T.cores:
+        for b in T.cores:
+            if a != b:
+                assert topo.may_write(a, b)
+                engs &= set(topo.engines(a, b))
+    engs = sorted(engs)
+    ne = len(engs)
+    mask = sum(1 << e for e in engs)
+
+    def ap(x):
+        if not isinstance(x, tuple):
+            return x
+        if x[0] == "ext":
+            return T[x[1]][:] if x[2] is None else T[x[1]][:, x[2][0]:x[2][1]]
+        if x[0] == "rows":
+            return T[x[1]][0:128:16, x[2]:x[3]]
+        if x[6] is not None:
+            if x[6][1] - x[6][0] == 1:
+                return T[x[0]][:, x[3]:x[4], x[6][0]]
+            return T[x[0]][:, x[3]:x[4], x[6][0]:x[6][1]]
+        if x[5] == 1:
+            return T[x[0]][x[1]:x[2], x[3]:x[4]]
+        return T[x[0]][x[1]:x[2], x[3]:x[4]:x[5]]
+
+    def src(x, ind):
+        return ap(x) if ind is None else ap(x).indirect(ap(ind))
+
+    pos = {}
+    for k, i in enumerate(order):
+        pos[i] = k
+    seen = {}
+    need = set()
+    for i in order:
+        e = ops[i]["eng"]
+        if e == "X":
+            continue
+        best = {}
+        for j, w in ops[i]["deps"].items():
+            pj = ops[j]
+            if w and pj["kind"] not in ("dma", "rdma", "arr") and pos[j] > seen.get((e, pj["eng"]), -1):
+                best[pj["eng"]] = max(best.get(pj["eng"], -1), pos[j])
+        for k, v in best.items():
+            seen[e, k] = v
+            need.add(order[v])
+    mark = {}
+    cnt = {}
+    nd = 0
+    for i in order:
+        p = ops[i]
+        if p["kind"] == "dma":
+            mark[i] = ("d%d" % nd, 16)
+            nd += 1
+        elif p["kind"] == "arr":
+            mark[i] = (p["args"][0], ne)
+        elif i in need:
+            cnt[p["eng"]] = cnt.get(p["eng"], 0) + 1
+            mark[i] = ("c" + p["eng"], cnt[p["eng"]])
+    waited = {}
+    seen = {}
+    nloc = 0
+    for i in order:
+        p = ops[i]
+        e, kind, a = p["eng"], p["kind"], p["args"]
+        if e == "X":
+            continue
+        q = qs[e]
+        want = {}
+        for j, w in p["deps"].items():
+            pj = ops[j]
+            if not w or pj["kind"] == "rdma":
+                continue
+            if pj["kind"] in ("dma", "arr"):
+                want[mark[j][0]] = mark[j][1]
+            elif pos[j] > seen.get((e, pj["eng"]), -1):
+                key = "c" + pj["eng"]
+                if key not in want or pos[j] > want[key][0]:
+                    want[key] = (pos[j], pj["eng"])
+        for s, v in sorted(want.items()):
+            if isinstance(v, tuple):
+                seen[e, v[1]] = v[0]
+                v = mark[order[v[0]]][1]
+            if waited.get((e, s), 0) < v:
+                waited[e, s] = v
+                q.wait_ge(T.sem[s], v)
+        if kind == "ts":
+            if a[5] is None:
+                r = q.tensor_scalar(ap(a[0]), src(a[1], a[6]), ap(a[2]), None, a[4])
+            else:
+                r = q.tensor_scalar(ap(a[0]), src(a[1], a[6]), ap(a[2]), ap(a[3]), a[4], a[5])
+        elif kind == "tt":
+            r = q.tensor_tensor(ap(a[0]), src(a[1], a[4]), ap(a[2]), a[3])
+        elif kind == "cp":
+            r = q.tensor_copy(ap(a[0]), src(a[1], a[2]))
+        elif kind == "ms":
+            r = q.memset(ap(a[0]), a[1])
+        elif kind == "scan":
+            r = q.tensor_tensor_scan(ap(a[0]), ap(a[1]), ap(a[2]), 0.0, AL.mult, AL.max)
+        elif kind == "act":
+            if a[4] != 0.0:
+                r = q.activation(ap(a[0]), src(a[1], a[5]), a[2], bias=ap(a[4]), scale=a[3])
+            elif a[3] != 1.0:
+                r = q.activation(ap(a[0]), src(a[1], a[5]), a[2], scale=a[3])
+            else:
+                r = q.activation(ap(a[0]), src(a[1], a[5]), a[2])
+        elif kind == "mm":
+            r = q.matmul(ap(a[0]), ap(a[1]), ap(a[2]), a[3], a[4])
+        elif kind == "iota":
+            if SCRATCH[a[0][0]][2] == I32:
+                r = q.iota(ap(a[0]), a[1], a[2], a[3])
+            else:
+                r = q.iota(ap(a[0]), a[1], a[2], a[3], allow_small_or_imprecise_dtypes=True)
+        elif kind == "asel":
+            r = q.affine_select(ap(a[0]), ap(a[1]), a[2], AL.is_equal, 0.0, a[3], a[4])
+        elif kind == "dma":
+            r = q.dma_start(ap(a[0]), ap(a[1]))
+        elif kind == "rdma":
+            rid, pid, _ = topo.addr(dest[a[2]])
+            q.remote_dma(ap(a[0]), ap(a[1]), T.sem[a[3]], T.sem.loc, pid, rid, mask)
+            nloc += ne
+            continue
+        if i in mark:
+            r.then_inc(T.sem[mark[i][0]], 16 if kind == "dma" else 1)
+    g.wait_ge(T.sem.loc, nloc)
+    top = {}
+    for i, (s, v) in mark.items():
+        top[s] = max(top.get(s, 0), v)
+    for s, v in sorted(top.items()):
+        if ("S", s) not in waited or waited["S", s] < v:
+            g.sync.wait_ge(T.sem[s], v)

@@ -6,8 +6,11 @@ AL = AluOpType
 AF = ActivationFunctionType
 NS = 6
 EX = 1
-PIECES = ((0, 128),)
+PIECES = ((0, 64), (64, 128))
 GP = ((0, 32), (32, 64), (64, 96), (96, 128))
+NM = 1
+FUSE = 2
+TC = 6
 HH = float(2 ** 40)
 F32, BF, F16, I32, U16 = "float32", "bfloat16", "float16", "int32", "uint16"
 BYTES = {F32: 4, BF: 2, F16: 2, I32: 4, U16: 2}
@@ -41,7 +44,7 @@ for _h in range(2):
 
 SEMAPHORES = ["cV", "cA", "cP", "cG", "loc"] + ["d%d" % i for i in range(48)] + ["ad%d" % i for i in range(12)] + ["af%d" % i for i in range(12)]
 
-CYC, PCYC, GTH, LAT = 1.0, 0.7, 1.56, 90.0
+CYC, PCYC, GTH, LAT = 1.0, 0.7 / 0.85, 1.9, 170.0
 
 
 def o(b, c0=0, c1=None, st=1, p0=0, p1=128):
@@ -418,8 +421,11 @@ def build():
     def tables():
         for k in range(8):
             x, f = o("CW", 512 + 512 * k, 1024 + 512 * k), o("GSu", 32 * k, 32 * k + 32)
-            chain["V"].append(ts(x, o("CLs"), cK, None, AL.add, None, f))
-            chain["A"].append(act(o("BW", 512 + 512 * k, 1024 + 512 * k), o("PW"), AF.Copy, -1.0, ind=o("BOu", 32 * k, 32 * k + 32)))
+            j1 = ts(x, o("CLs"), cK, None, AL.add, None, f)
+            j2 = act(o("BW", 512 + 512 * k, 1024 + 512 * k), o("PW"), AF.Copy, -1.0, ind=o("BOu", 32 * k, 32 * k + 32))
+            if k < TC:
+                chain["V"].append(j1)
+                chain["A"].append(j2)
         x = o("GW", 0, 4096)
         dma("S", ("rows", "GW", 0, 4096), ("ext", "gs", None), [], [x], 131072)
         x = o("GW", 4608, 4864)
@@ -431,7 +437,8 @@ def build():
     def wide(t, h):
         H = str(h)
         P, EQ, KY = "P" + H, "EQ" + H, "KY" + H
-        ts(o("CU" + H), cur(t, h), cK, None, AL.subtract)
+        if t == 0 or not FUSE:
+            ts(o("CU" + H), cur(t, h), cK, None, AL.subtract)
         mm(o(KY, 0, 128), cur(t, h), o("ID16"), True, False)
         for (a, b) in GP:
             chain["A"] = [act(o(P, 16 * a, 16 * b), o("PW"), AF.Copy, ind=o("CU" + H, a, b), after=chain["A"])]
@@ -439,14 +446,17 @@ def build():
         for (a, b) in PIECES:
             for k in range(st):
                 c = 128 * EX * k
-                chain["V"] = [tt(o(EQ, c + EX * a, c + EX * b), o(P, 16 * a + k, 16 * b, st), o("MP" + H, EX * a, EX * b), AL.is_equal, after=chain["V"])]
+                m = o("MP" + H, EX * a, EX * b)
+                if k < NM and a == 0 and t > 0:
+                    m = o("MS" + H, 128 * (t % 2) + a, 128 * (t % 2) + b)
+                chain["V"] = [tt(o(EQ, c + EX * a, c + EX * b), o(P, 16 * a + k, 16 * b, st), m, AL.is_equal, after=chain["V"])]
         for k in range(16):
             mm(o(KY, k, 128, 16), o(P, k, 2048, 16), o("INp"), False, False)
+        mm(o(KY, 0, 128), o("S2" + H, p1=N2), o("BC", 512, 640, p1=N2), False, False)
         for k in range(16):
             kk = k // EX + st * (k % EX)
             c = 128 * EX * (k // EX)
-            mm(o(KY, kk, 128, 16), o(EQ, c + k % EX, c + 128 * EX, EX), o("INe"), False, False)
-        mm(o(KY, 0, 128), o("S2" + H, p1=N2), o("BC", 512, 640, p1=N2), False, True)
+            mm(o(KY, kk, 128, 16), o(EQ, c + k % EX, c + 128 * EX, EX), o("INe"), False, k == 15)
 
     def choose(t, h):
         H = str(h)
@@ -478,7 +488,12 @@ def build():
         act(o("CT", 32 * i + 8, 32 * i + 16), rs, AF.Identity, 2.0 ** -16, col("CC", 14))
         f0, f1 = to_b(t, h, 2048.0 if t % 2 == 0 else 2560.0, 2048.0)
         if t < NS - 1:
-            act(cur(t + 1, h), win("CW", t), AF.Copy, ind=f0)
+            if FUSE:
+                ts(o("CU" + H), win("CW", t), cK, None, AL.subtract, None, f0)
+            if FUSE == 2:
+                ts(cur(t + 1, h), o("CU" + H), cK, None, AL.add)
+            else:
+                act(cur(t + 1, h), win("CW", t), AF.Copy, ind=f0)
         snd = o("SND", 128 * i, 128 * i + 128)
         tt(snd, win("BW", t), o("MS" + H, 128 * (t % 2), 128 * (t % 2) + 128), AL.min, f0)
         land = o("MW", 2048 + 128 * i, 2048 + 128 * i + 128)
@@ -508,7 +523,24 @@ def build():
     return ops
 
 
-def plan(ops, rounds=150, climbs=800):
+CASES = ((0.85, 1.4, 200.0, 1.0, 93.0), (1.25, 2.05, 150.0, 1.0, 125.0), (1.2, 1.2, 200.0, 0.8, 112.0), (0.85, 1.1, 130.0, 1.2, 87.0))
+SEED = 1
+
+
+def recost(ops, c, gt):
+    res = []
+    for p in ops:
+        k = {"ts": 6, "tt": 4, "cp": 2, "act": 5}.get(p["kind"])
+        v = p["cost"]
+        if p["eng"] in "VAP" and p["kind"] != "dma":
+            if k is not None and p["args"][k] is not None:
+                v += nel(p["args"][0]) * (gt - GTH) * CYC
+            v *= c / CYC
+        res.append(dict(p, cost=v))
+    return res
+
+
+def plan(ops, rounds=40, climbs=1000):
     n = len(ops)
     succ = [[] for _ in range(n)]
     left = [len(p["deps"]) for p in ops]
@@ -519,8 +551,13 @@ def plan(ops, rounds=150, climbs=800):
     lvl = [0.0] * n
     for i in range(n - 1, -1, -1):
         lvl[i] = dur[i] + max([lvl[k] + (LAT if ops[k]["deps"][i] else 0.0) for k in succ[i]] + [0.0])
+    sets = [(recost(ops, c, gt), l, f, w) for (c, gt, l, f, w) in CASES]
+
+    def score(r):
+        v = [replay(q, r[0], l, f) / w for (q, l, f, w) in sets]
+        return 1000.0 * (sum(v) / len(v) + max(v)) / 2
     best = None
-    rng = np.random.default_rng(1)
+    rng = np.random.default_rng(SEED)
     for it in range(rounds):
         if it < 200 or it % 2 == 0:
             fa, fv = 1.0 + 0.8 * float(rng.random()), 1.0 + 2.0 * float(rng.random())
@@ -556,8 +593,9 @@ def plan(ops, rounds=150, climbs=800):
             mix = float(rng.random())
             pr = [-(mix * late[i] + (1 - mix) * (end - lvl[i])) + amp * float(z[i]) for i in range(n)]
         r = once(ops, succ, list(left), pr, (60.0, 150.0, 300.0)[(it // 3) % 3])
-        if best is None or max(r[2]) < best[0]:
-            best = (max(r[2]),) + r
+        v = score(r)
+        if best is None or v < best[0]:
+            best = (v,) + r
             keep = (pr, (60.0, 150.0, 300.0)[(it // 3) % 3])
     names = {}
     cls = np.array([names.setdefault(p["cls"], len(names)) for p in ops])
@@ -571,8 +609,9 @@ def plan(ops, rounds=150, climbs=800):
         for k in range(1 + it % 4):
             d[pool[int(rng.integers(len(pool)))]] += float(rng.normal()) * (300.0, 1000.0, 3000.0)[it % 3]
         r = once(ops, succ, list(left), [float(v) for v in base + d[cls]], keep[1])
-        if max(r[2]) <= best[0]:
-            best = (max(r[2]),) + r
+        v = score(r)
+        if v <= best[0]:
+            best = (v,) + r
             delta = d
     return best[1:]
 
@@ -611,6 +650,31 @@ def once(ops, succ, left, lvl, slack):
             if left[k] == 0:
                 est[k] = max((fin[j] + LAT if w or ops[j]["eng"] != ops[k]["eng"] else beg[j]) for j, w in ops[k]["deps"].items())
     return order, beg, fin
+
+
+def replay(ops, order, lat, far):
+    n = len(ops)
+    fin = [0.0] * n
+    beg = [0.0] * n
+    free = {}
+    bus = 0.0
+    for i in order:
+        p = ops[i]
+        e = p["eng"]
+        s = free.get(e, 0.0)
+        for j, w in p["deps"].items():
+            v = fin[j] + lat if w or ops[j]["eng"] != e else beg[j]
+            if v > s:
+                s = v
+        beg[i] = s
+        if e != "X":
+            free[e] = s + p["cost"]
+        if p["kind"] == "dma":
+            bus = max(bus, s + p["lat"]) + p["args"][2] / 250.0
+            fin[i] = bus
+        else:
+            fin[i] = s + p["cost"] + p["lat"] * (far if e == "X" else 1.0)
+    return max(fin)
 
 
 CACHE = {}

@@ -5,63 +5,55 @@ from concourse.mybir import dt, AluOpType, AxisListType, ActivationFunctionType
 AL = AluOpType
 AF = ActivationFunctionType
 NS = 6
-EX = 1
 PIECES = ((0, 64), (64, 128))
 GP = ((0, 32), (32, 64), (64, 96), (96, 128))
-NM = 1
-FUSE = 2
-TC = 6
-HH = float(2 ** 40)
+PT = 1
+PV = 16
+BV = 2
+FIXV = (3, 7)
+NM = 0
+M3V = False
+R0V = True
+HH = float(2 ** 60)
+BIG = float(2 ** 20)
+MAG = 1.5 * 2.0 ** 37
 F32, BF, F16, I32, U16 = "float32", "bfloat16", "float16", "int32", "uint16"
 BYTES = {F32: 4, BF: 2, F16: 2, I32: 4, U16: 2}
 
-SCRATCH = {
-    "PW": ("sbuf", [128, 4096], BF), "BW": ("sbuf", [128, 5120], BF), "CW": ("sbuf", [128, 5120], F32),
-    "CLs": ("sbuf", [128, 2048], I32), "MW": ("sbuf", [128, 3584], BF), "GW": ("sbuf", [128, 4864], I32),
-    "SND": ("sbuf", [128, 1536], BF), "MO": ("sbuf", [128, 1536], BF), "CT": ("sbuf", [128, 32 * 12], BF),
-    "BOi": ("sbuf", [128, 256], I32), "GSi": ("sbuf", [128, 256], I32), "BOu": ("sbuf", [128, 256], U16), "GSu": ("sbuf", [128, 256], U16),
-    "Qi": ("sbuf", [128, 256], I32), "STi": ("sbuf", [128, 256], I32), "S0i": ("sbuf", [128, 256], I32), "S0f": ("sbuf", [128, 256], F32),
-    "ONE": ("sbuf", [128, 128], BF), "ZER": ("sbuf", [128, 384], BF), "SHp": ("sbuf", [128, 128], F16), "IDq": ("sbuf", [128, 128], BF), "ID": ("sbuf", [128, 128], BF), "IDh": ("sbuf", [128, 128], F16),
-    "ID16": ("sbuf", [128, 128], F32), "SID": ("sbuf", [128, 128 * 24], BF), "SH0": ("sbuf", [128, 128], BF), "SHh": ("sbuf", [128, 128], F16),
-    "PI": ("sbuf", [128, 16], I32), "CC": ("sbuf", [128, 32], F32), "IO16": ("sbuf", [128, 16], F32), "IOG": ("sbuf", [128, 128], F32),
-    "LR": ("sbuf", [128, 128], F32), "LR2": ("sbuf", [128, 128], F32), "IN8": ("sbuf", [128, 16], F32), "IN16": ("sbuf", [128, 8], F32),
-    "INe": ("sbuf", [128, 8], BF), "INp": ("sbuf", [128, 8], BF), "INh": ("sbuf", [128, 8], F16), "I8f": ("sbuf", [128, 8], F32),
-    "G8": ("sbuf", [128, 128], BF), "BC": ("sbuf", [128, 640], BF), "FW": ("sbuf", [128, 240], F16),
-    "HZ": ("sbuf", [128, 72], F16), "HQ": ("sbuf", [128, 72], F16), "WM": ("sbuf", [128, 360], BF), "WX": ("sbuf", [128, 24], F32),
-    "HI": ("sbuf", [128, 32], F32), "YO": ("sbuf", [128, 8], U16), "YF": ("sbuf", [128, 8], F32), "RST": ("sbuf", [128, 128], F32),
-    "YQ": ("sbuf", [128, 256], F32), "YS": ("sbuf", [128, 256], F32), "YP": ("sbuf", [128, 256], F32),
-}
+SCRATCH = {}
+for _d, _l in (
+        (BF, (("PW", 4096), ("BW", 4624), ("MW", 3584), ("SND", 1536), ("MO", 1536), ("CT", 768), ("ONE", 144), ("WSb", 144), ("ZER", 192), ("ID", 128),
+              ("IXb", 136), ("SID", 1280), ("SH0", 128), ("BU", 272), ("INe", 8), ("INp", 8), ("AL01", 16), ("G8", 128),
+              ("BC", 384), ("BT", 256), ("PN", 136), ("XV", 40), ("WM", 192), ("WO", 80))),
+        (I32, (("CW", 4608), ("CLs", 2048), ("GW", 256), ("BOi", 256), ("GSi", 256), ("Qi", 256), ("STi", 256), ("PI", 16))),
+        (U16, (("BOu", 256), ("GSu", 256), ("L1", 32), ("L2", 16), ("YO", 12), ("SO", 16))),
+        (F16, (("IDh", 128), ("WS", 144), ("S0f", 256), ("IX", 136), ("DM", 128), ("D3", 128), ("E15", 128), ("LN", 128), ("CB", 128), ("LC", 256), ("FW", 48), ("WQ", 16))),
+        (F32, (("X2", 512), ("X3", 512), ("LF", 32), ("CC", 40), ("I1f", 8), ("IO16", 16), ("IOG", 128), ("IOH", 136),
+               ("IOK", 136), ("IOJ", 128), ("IOT", 40), ("LP", 256), ("IN8", 16), ("IN16", 8), ("D8", 8), ("I8f", 8), ("WZ", 16),
+               ("YT", 24), ("YF", 24), ("YQ", 256), ("YS", 256), ("YP", 256)))):
+    for _n, _c in _l:
+        SCRATCH[_n] = ("sbuf", [128, _c], _d)
 for _h in range(2):
-    for _n, _sh, _d in (("P", [128, 2048], BF), ("EQ", [128, 2048], BF), ("CU", [128, 128], U16), ("MS", [128, 256], BF),
-                        ("RS", [128, 128], F32), ("CI", [128, 64], I32), ("CF", [128, 64], F32), ("VC", [128, 32], F32),
-                        ("Y", [128, 128], F16), ("OF", [128, 32], U16), ("R0", [128, 128], BF), ("S1", [128, 128], BF),
-                        ("S2", [128, 128], BF), ("SX", [128, 128], F32), ("Q", [128, 128], F16), ("M1", [128, 128], BF),
-                        ("M2", [128, 128], F16), ("M3", [128, 128], BF), ("T1", [128, 128], F32), ("ZX", [128, 128], F16),
-                        ("QF", [128, 256], F32)):
-        SCRATCH["%s%d" % (_n, _h)] = ("sbuf", _sh, _d)
+    for _n, _c, _d in (("P", 2048, BF), ("EQ", 2048, BF), ("CU", 128, U16), ("CH", 128, F16), ("MS", 256, BF), ("RS", 144, F32),
+                       ("VC", 168, F32), ("VB", 168, F32), ("Y", 192, F16), ("OF", 48, U16), ("S", 128, BF), ("Q", 128, F16), ("M", 256, BF),
+                       ("M3", 128, BF), ("T1", 128, F32), ("ZX", 128, F32), ("QF", 128, F32)):
+        SCRATCH["%s%d" % (_n, _h)] = ("sbuf", [128, _c], _d)
     for _n in ("MP", "KY", "XA", "XB"):
         SCRATCH["%s%d" % (_n, _h)] = ("psum", [128, 512], F32)
 
 SEMAPHORES = ["cV", "cA", "cP", "cG", "loc"] + ["d%d" % i for i in range(48)] + ["ad%d" % i for i in range(12)] + ["af%d" % i for i in range(12)]
 
-CYC, PCYC, GTH, LAT = 1.0, 0.7 / 0.85, 1.9, 170.0
+CYC, PCYC, GTH = 1.0, 0.8, 1.9
 
 
 def o(b, c0=0, c1=None, st=1, p0=0, p1=128):
     if c1 is None:
         c1 = SCRATCH[b][1][1]
-    return (b, p0, p1, c0, c1, st, None)
-
-
-def o3(b, l0, l1, k0, k1):
-    return (b, 0, 128, l0, l1, 1, (k0, k1))
+    return (b, p0, p1, c0, c1, st)
 
 
 def nel(x):
-    n = len(range(x[3], x[4], x[5]))
-    if x[6] is not None:
-        n *= x[6][1] - x[6][0]
-    return n
+    return len(range(x[3], x[4], x[5]))
 
 
 def two(x):
@@ -73,14 +65,13 @@ def isps(x):
 
 
 def span(x):
-    if len(SCRATCH[x[0]][1]) == 3:
-        k = x[6] if x[6] is not None else (0, 16)
-        return (x[1], x[2], x[3], x[4], k[0], k[1])
-    return (x[1], x[2], x[3], x[3] + (len(range(x[3], x[4], x[5])) - 1) * x[5] + 1, 0, 1)
+    return (x[1], x[2], x[3], x[3] + (nel(x) - 1) * x[5] + 1, x[5])
 
 
 def meet(a, b):
-    return a[0] < b[1] and b[0] < a[1] and a[2] < b[3] and b[2] < a[3] and a[4] < b[5] and b[4] < a[5]
+    if a[4] == b[4] and (a[2] - b[2]) % a[4]:
+        return False
+    return a[0] < b[1] and b[0] < a[1] and a[2] < b[3] and b[2] < a[3]
 
 
 def build():
@@ -88,7 +79,7 @@ def build():
     hist = {}
     bank = {}
     lastpe = {}
-    ctx = ["", {}]
+    ctx = ["", {}, None]
 
     def add(eng, kind, args, reads, writes, cost, lat=0.0, after=()):
         i = len(ops)
@@ -99,9 +90,7 @@ def build():
             if j == i:
                 return
             pj = ops[j]
-            w = raw or pj["eng"] != eng or dma or pj["kind"] in ("dma", "rdma")
-            if pj["eng"] == "P" and eng == "P":
-                w = False
+            w = not (pj["eng"] == "P" and eng == "P")
             deps[j] = deps.get(j, False) or w
         for x, wr in [(x, False) for x in reads] + [(x, True) for x in writes]:
             s = span(x)
@@ -124,7 +113,7 @@ def build():
         for x in writes:
             s = span(x)
             hist[x[0]] = [e for e in hist[x[0]] if not (s[0] <= e[1][0] and e[1][1] <= s[1] and s[2] <= e[1][2] and e[1][3] <= s[3]
-                                                        and s[4] <= e[1][4] and e[1][5] <= s[5] and x[5] == 1)]
+                                                        and (s[4] == 1 or (s[4] == e[1][4] and (s[2] - e[1][2]) % s[4] == 0)))]
         for x in reads:
             hist[x[0]].append((i, span(x), False))
         for x in writes:
@@ -132,9 +121,9 @@ def build():
         for j in after:
             deps[j] = deps.get(j, False)
         nm = args[0][0] if isinstance(args[0], tuple) else args[0][:2]
-        key = (ctx[0], eng, kind, (nm[:-1] if nm[:-1] + "1" in SCRATCH else nm) if ctx[0] else i)
+        key = (ctx[0], eng, nm[:-1] if nm[-1] in "01" and nm[:-1] + "1" in SCRATCH and nm[:-1] + "0" in SCRATCH and ctx[0] else nm)
         ctx[1][key] = ctx[1].get(key, 0) + 1
-        ops.append({"eng": eng, "kind": kind, "args": args, "deps": deps, "cost": cost, "lat": lat, "cls": key + (ctx[1][key],)})
+        ops.append({"eng": eng, "kind": kind, "args": args, "deps": deps, "cost": cost, "lat": lat, "cls": key + (ctx[1][key],), "at": ctx[2]})
         return i
 
     def aps(*xs):
@@ -158,17 +147,30 @@ def build():
     def ms(out, v):
         return add("V", "ms", (out, v), [], [out], max(64, nel(out) * (0.5 if two(out) else 1)) * CYC)
 
+    def red(out, a):
+        return add("V", "red", (out, a), [a], [out], max(64, nel(a)) * CYC)
+
+    def scan(out, a, b, init, op0, op1):
+        return add("V", "scan", (out, a, b, init, op0, op1), [a, b], [out], max(64, nel(out)) * CYC)
+
     def act(out, a, f, scale=1.0, bias=0.0, ind=None, after=()):
         n = nel(out)
         c = 78 + n * GTH if ind else max(64, n)
-        return add("A", "act", (out, a, f, scale, bias, ind), aps(a, ind, bias), [out], c * CYC, after=after)
+        return add("A", "act", (out, a, f, scale, bias, ind), aps(a, ind, bias, scale), [out], c * CYC, after=after)
+
+    def lin(out, a, scale=1.0, bias=0.0):
+        return act(out, a, AF.Copy if bias == 0.0 else AF.Identity, scale, bias)
 
     def mm(out, l, r, s0=True, s1=True):
-        c = max(min(64, nel(l)), nel(r)) * (1 if two(l) else 4)
+        same = ops[-1]["kind"] == "mm" and ops[-1]["args"][1] == l and ops[-1]["args"][0][0] == out[0]
+        c = max(16 if same else min(64, nel(l)), nel(r)) * (1 if two(l) else 4)
         return add("P", "mm", (out, l, r, s0, s1), [l, r], [out], c * PCYC)
 
     def iota(out, pat, base, cm):
         return add("G", "iota", (out, pat, base, cm), [], [out], 160 + 2 * nel(out) * CYC)
+
+    def fill(out, v):
+        return iota(out, [[0, nel(out)]], v, 0)
 
     def asel(out, a, pat, base, cm):
         return add("G", "asel", (out, a, pat, base, cm), [a], [out], 210 + 2 * nel(out) * CYC)
@@ -179,331 +181,338 @@ def build():
     def col(b, c):
         return o(b, c, c + 1)
 
-    for k, nm in enumerate(("p0", "n0", "w0")):
+    la = [dma("A", o("BOi"), ("ext", "bo", None), [], [o("BOi")], 131072)]
+    for k, nm in ((0, "p0"), (1, "s0"), (2, "n0"), (4, "w0")):
         x = o("STi", p0=8 * k, p1=8 * k + 8)
-        dma("A", x, ("ext", nm, None), [], [x], 8192)
-    x = o("S0i", p1=8)
-    dma("A", x, ("ext", "s0", None), [], [x], 8192)
-    dma("A", o("Qi"), ("ext", "q0", None), [], [o("Qi")], 131072)
-    ld = [dma("S", o("BOi"), ("ext", "bo", None), [], [o("BOi")], 131072)]
+        la = [dma("A", x, ("ext", nm, None), [], [x], 8192, la)]
+    ld = []
     for k in range(4):
         x = o("PW", 1024 * k, 1024 * k + 1024)
         ld = [dma("S", x, ("ext", "pt", (1024 * k, 1024 * k + 1024)), [], [x], 262144, ld)]
+        if k < 2:
+            la = [dma("A", o(("Qi", "GSi")[k]), ("ext", ("q0", "gs")[k], None), [], [o(("Qi", "GSi")[k])], 131072, la)]
     ld = [dma("S", o("CLs"), ("ext", "cl", None), [], [o("CLs")], 1048576, ld)]
-    ld = [dma("S", o("GSi"), ("ext", "gs", None), [], [o("GSi")], 131072, ld)]
     ld = [dma("S", o("MW", 0, 2048), ("ext", "m0", None), [], [o("MW", 0, 2048)], 524288, ld)]
 
     ms(o("ONE"), 1.0)
+    one = o("ONE", 0, 128)
     iota(col("PI", 0), [[0, 1]], 0, 1)
-    asel(o("ID"), o("ONE"), [[-1, 128]], 0, 1)
+    asel(o("ID"), one, [[-1, 128]], 0, 1)
     iota(o("IO16"), [[1, 16]], 0, 0)
+    iota(o("LF"), [[16, 16], [0, 2]], 0, 0)
+    for (c, n, b, s) in ((0, 4, 136, 2), (4, 8, 0, 17), (12, 4, 137, 2), (16, 8, 145, 2)):
+        iota(o("YT", c, c + n), [[s, n]], b, 0)
     iota(o("IOG"), [[1, 8], [0, 16]], 0, 0)
-    iota(o("LR"), [[1, 128]], 0, 0)
-    asel(o("SH0"), o("ONE"), [[-1, 128]], -1, 1)
-    iota(o("LR2"), [[1, 128]], -256, 0)
-    for c, (s, op) in enumerate(((15, AL.bitwise_and), (4, AL.arith_shift_right), (3, AL.arith_shift_right), (7, AL.bitwise_and), (8, AL.bitwise_and))):
+    iota(o("IOH"), [[1, 8], [0, 17]], 0, 0)
+    iota(o("IOK"), [[0, 8], [-1, 17]], 16, 0)
+    iota(o("IOJ"), [[0, 8], [2, 16]], 1, 0)
+    iota(o("IOT"), [[256, 5], [0, 8]], 384, 0)
+    iota(o("AL01"), [[0, 8], [1, 2]], 0, 0)
+    iota(o("LP", p1=1), [[1, 256]], 1664, 0)
+    asel(o("SH0"), one, [[-1, 128]], -1, 1)
+    asel(o("IXb"), o("ONE", 0, 136), [[-16, 8], [-1, 17]], 0, 1)
+    for c, (s, op) in enumerate(((15, AL.bitwise_and), (4, AL.arith_shift_right), (3, AL.arith_shift_right), (7, AL.bitwise_and),
+                                 (8, AL.bitwise_and), (31, AL.bitwise_and))):
         ts(col("PI", c + 1), col("PI", 0), s, None, op)
-    cp(o("CC", 0, 6), o("PI", 0, 6))
-    cP, cJ, cP16, cP8, cM8, cQ8 = [col("CC", c) for c in range(6)]
-    cJ1, cK, cN0, cJ0, cJ1e, cEB, cQ16 = [col("CC", c) for c in range(6, 13)]
-    ts(cJ1, cJ, 1.0, None, AL.add)
-    ts(cK, cJ, -4096.0, 61440.5, AL.mult, AL.add)
-    ms(col("CC", 14), 128.5 + 2.0 ** -14)
-    ts(cN0, cJ, 0.0, None, AL.is_gt)
+    cp(o("CC", 0, 7), o("PI", 0, 7))
+    cP, cJ, cP16, cP8, cM8, cQ8, cP32 = [col("CC", c) for c in range(7)]
+    cJ16, cBias, cN0, cJ15, cJd, cEB, cE1, cE0, cE2 = [col("CC", c) for c in range(7, 16)]
+    vp, vn, vr, vw, c1, c2a, c3, c3b, cpn, cA, cB, cBa, cJ0, cCB, cS1, cBG = [col("CC", c) for c in range(16, 32)]
+    lin(cJ16, cJ, 31.0, cP32)
+    ts(o("L1"), o("LF"), cJ, None, AL.add)
+    ts(o("L2"), o("IO16"), cJ16, None, AL.add)
+    lin(cBias, cJ, 256.0, 128.0)
     ts(cJ0, cJ, 0.0, None, AL.is_equal)
-    ts(cJ1e, cJ, 1.0, None, AL.is_equal)
+    ts(cJ15, cJ, 15.0, None, AL.is_equal)
+    lin(cN0, cJ0, -1.0, 1.0)
+    lin(cJd, cJ0, -1.0, cJ15)
     ts(cEB, cP16, cM8, None, AL.is_equal)
-    ts(cQ16, cQ8, -16.0, None, AL.add)
-    cL = {}
-    for par in range(2):
-        for h in range(2):
-            cL[par, h] = col("CC", 16 + 2 * par + h)
-            ts(cL[par, h], cP, 2.0, float((4096 if par == 0 else -512) + 256 * h), AL.mult, AL.add)
+    ts(cE1, cQ8, 0.125, cEB, AL.mult, AL.mult)
+    lin(cE0, cE1, -1.0, cEB)
+    lin(cE2, cEB, -160.0, 160.0)
+    lin(o("YF", 0, 12), o("YT", 0, 12), cE0, cE2)
+    lin(o("YF", 12, 24), o("YT", 12, 24), cE1)
+    tt(o("YF", 0, 12), o("YF", 0, 12), o("YF", 12, 24), AL.add)
+    cp(o("YO"), o("YF", 0, 12))
     ts(o("IN8"), o("IO16"), cP8, None, AL.is_equal)
     ts(o("IN16"), o("IO16", 0, 8), cP16, None, AL.is_equal)
-    ts(o("INe"), o("IN16"), float(2 ** 20), None, AL.mult)
-    ts(o("INp"), o("IN16"), -float(2.0 ** -20), None, AL.mult)
-    cp(o("INh"), o("IN16"))
-    cp(o("IDh"), o("ID"))
-    act(o("ID16"), o("ID"), AF.Copy, 16.0)
-    cp(o("I8f"), o("ID", 0, 8))
+    ts(o("D8"), o("IO16", 0, 8), cM8, None, AL.is_equal)
+    lin(o("INe"), o("IN16"), float(2 ** 19))
+    lin(o("INp"), o("IN16"), -float(2.0 ** -41))
+    lin(o("IDh"), o("ID"))
+    lin(o("IX"), o("IXb"))
+    lin(o("LC", p1=1), o("LP", p1=1))
+    asel(o("WSb", p1=16), o("ONE", p1=16), [[1, 144]], 113, -16)
+    lin(o("WS", p1=16), o("WSb", p1=16))
+    lin(o("I1f"), o("ID", 120, 128))
+    e120, e121, e122 = [col("I1f", c) for c in range(3)]
+    lin(o("LN", p1=1), o("ONE", 0, 128, p1=1))
+    ts(cS1, cP8, 1.0, None, AL.not_equal)
     ts(o("G8"), o("IOG"), cM8, None, AL.is_equal)
-    n8 = lambda s: col("IN8", s)
-    tt(col("CC", 21), n8(0), n8(3), AL.add)
-    tt(col("CC", 20), col("CC", 21), n8(10), AL.subtract)
-    tt(col("CC", 24), n8(6), n8(3), AL.subtract)
-    tt(col("CC", 25), col("CC", 24), n8(8), AL.add)
-    ts(col("CC", 26), col("CC", 25), 64.0, n8(1), AL.mult, AL.add)
-    tt(col("CC", 27), n8(3), n8(10), AL.subtract)
-    ts(col("CC", 28), n8(8), -5.0 * 2 ** 24, None, AL.mult)
-    ts(col("CC", 29), col("CC", 27), 2.0 ** 26, col("CC", 28), AL.mult, AL.add)
-    for k, cc in enumerate((n8(5), col("CC", 26), col("CC", 20), n8(0), col("CC", 29))):
-        ts(o("BC", 128 * k, 128 * k + 128), o("G8"), cc, None, AL.mult)
     ms(o("FW"), 0.0)
-    ts(o("FW", 112, 128), o("IO16"), cJ, None, AL.is_equal)
-    ts(o("YF"), o("IO16", 0, 8), cQ16, cEB, AL.add, AL.mult)
-    ts(o("YO"), o("YF"), 16.0, None, AL.add)
-    ts(o("SH0"), o("SH0"), cN0, 0.5, AL.mult, AL.mult)
-    ts(o("IDq"), o("ID"), 0.5, None, AL.mult)
-    tt(o("SHh"), o("SH0"), o("IDq"), AL.subtract)
-    tt(o("SHp"), o("SH0"), o("IDq"), AL.add)
-    cJh = col("CC", 13)
-    ts(cJh, cJ, 0.5, None, AL.add)
-    ms(o("RST"), 1.0)
-    ms(o("RST", 0, 128, 16), 0.0)
-    ms(o("HZ"), 0.0)
-    ms(o("HQ"), 0.0)
-    for s in range(2):
-        cp(o("HZ", 8 * s, 8 * s + 8), o("IN16"))
-        ts(o("HQ", 16 + 8 * s, 24 + 8 * s), o("IN16"), cJ0, None, AL.mult)
-        ts(o("HQ", 32 + 8 * s, 40 + 8 * s), o("IN16"), cJ1e, None, AL.mult)
-    cp(o("HZ", 48, 56), o("IN16"))
-    ts(o("HQ", 56, 64), o("IN16"), cJ0, None, AL.mult)
-    ts(o("HQ", 64, 72), o("IN16"), cJ1e, None, AL.mult)
-    tt(col("HI", 16), n8(11), n8(12), AL.add)
-    ts(col("HI", 18), col("HI", 16), -2304.0, None, AL.mult)
-    ts(col("HI", 19), col("HI", 16), -128.0, None, AL.mult)
-    ts(o("HI", 4, 16), o("IO16", 0, 12), col("HI", 19), col("HI", 18), AL.mult, AL.add)
-    WR1, W21, W12, W2X, W1F, WXC = 0, 80, 160, 264, 336, 360
-    N1, N2 = 80, 104
-    TW1, TW2, TWX = {3: 8, 4: 9}, {3: 10, 6: 11, 7: 12}, {0: 6, 2: 7, 4: 8}
-    twin = {WR1: ({}, TW1), W21: (TW2, TW1), W12: (TW1, TW2), W2X: (TW2, TWX), W1F: (TW1, {}), WXC: (TWX, {})}
-    ent = [(W21 + 64, 8, -1), (W21 + 72, 8, -1), (W12 + 80, 6, -1)] + [(W2X + 8 * s, 8, -2048) for s in (6, 7, 8)]
-    for (base, lst) in (
-        (WR1, [(0, 0, 64), (0, 1, 1), (1, 2, -1), (0, 3, -1), (2, 3, -64), (1, 4, 1), (0, 5, 64)]),
-        (W21, [(0, 0, 1), (3, 0, 1), (8, 0, -64), (1, 1, 1), (8, 1, -1), (2, 2, 1), (3, 2, 16), (8, 2, 129), (1, 3, -1), (8, 3, 17),
-               (2, 4, -1), (3, 4, -16), (8, 4, -81), (0, 5, 1), (8, 6, 1), (9, 7, 1)]),
-        (W12, [(0, 0, 1), (1, 1, 1), (3, 1, 1), (2, 2, 1), (4, 2, 64), (6, 2, -64), (1, 3, 1), (3, 3, 1), (0, 3, -1), (4, 3, 64), (6, 3, -64),
-               (0, 5, -1), (6, 5, 1), (1, 6, -4096), (3, 6, -4096), (6, 6, 8192),
-               (1, 7, -4096), (3, 7, -4096), (0, 7, 4096), (4, 7, 4096), (6, 7, 4096), (6, 8, 1), (7, 9, 1)]),
-        (W2X, [(7, 0, 1), (7, 1, 1), (9, 1, 1), (8, 1, -2304), (5, 2, -8192), (9, 3, 1), (8, 3, -2304), (5, 3, -8192),
-               (6, 4, 1), (8, 4, -8192), (5, 4, 8192), (6, 5, 1), (9, 5, 1), (8, 5, -2304), (8, 5, -8192), (5, 5, 8192)]),
-        (W1F, [(0, 0, 1), (1, 1, 1), (3, 1, 1), (2, 2, 1)]),
-        (WXC, [(2, 1, 1), (3, 1, 1), (4, 1, 1), (5, 1, 1), (0, 2, 1), (1, 2, 1), (2, 2, -1), (3, 2, -1), (4, 2, -1), (5, 2, -1)]),
-    ):
-        ti, to = twin[base]
-        lst = lst + [(ti[si], so, -v) for (si, so, v) in lst if si in ti]
-        lst = lst + [(si, to[so], v) for (si, so, v) in lst if so in to]
-        ent += [(base + 8 * so, si, v) for (si, so, v) in lst]
-    vals = sorted(set(e[2] for e in ent) - {1})
-    for k, v in enumerate(vals):
-        act(o("SID", 128 * k, 128 * k + 104), o("ID", 0, 104), AF.Copy, float(v))
+    ts(o("FW", 16, 32), o("IO16"), cJ, None, AL.is_equal)
+    n8 = lambda s: col("IN8", s)
+    lin(vp, n8(0), 1.0, n8(1))
+    lin(vn, n8(3), -1.0, n8(2))
+    lin(vr, n8(6), -1.0, n8(5))
+    red(vw, o("IN8", 7, 12))
+    for k, v in enumerate((vp, vn, n8(4), vr, vw)):
+        lin(o("XV", 8 * k, 8 * k + 8), o("D8"), v)
+    lin(c1, n8(12), 64.0, vp)
+    ts(c2a, n8(13), n8(12), vn, AL.subtract, AL.subtract)
+    ts(c3, n8(15), vp, vr, AL.add, AL.subtract)
+    lin(c3b, n8(15), 15.0, vp)
+    ts(cpn, vr, vw, -2.0 ** 23, AL.add, AL.mult)
+    lin(o("BC", 0, 128), o("G8"), c1)
+    lin(o("BT", 0, 128), o("G8"), c2a)
+    lin(o("BT", 128, 256), o("IOJ"), e120)
+    tt(o("BC", 128, 256), o("BT", 0, 128), o("BT", 128, 256), AL.add)
+    lin(o("BC", 256, 384), o("G8"), c3)
+    lin(o("BC", 271, 384, 16), o("D8"), c3b)
+    lin(cA, e121, 16384.0)
+    lin(cBa, e120, -2.0 ** 23)
+    lin(cB, e122, 2048.0, cBa)
+    lin(cBG, e121, BIG)
+    ts(o("BU", 0, 136), o("IOH"), cM8, cpn, AL.is_equal, AL.mult)
+    lin(o("BU", 136, 272), o("IOK"), cA, cB)
+    tt(o("PN"), o("BU", 0, 136), o("BU", 136, 272), AL.add)
+    lin(o("PN", 16, 136, 17), o("ONE", 0, 8), cBG)
+    lin(o("CB", p1=1), o("ONE", 0, 128, p1=1), 1664.0)
+    lin(o("SH0"), o("SH0"), cN0)
+    tt(o("DM"), o("SH0"), o("ID"), AL.subtract)
+    cp(o("D3"), o("DM"))
+    cp(o("D3", 15, 128, 16), o("DM", 0, 128, 16))
+    ms(o("E15", p1=1), 0.0)
+    ms(o("E15", 15, 128, 16, p1=1), 1.0)
+    lin(o("WZ", 0, 16, 2), o("IN16"), -1.0)
+    lin(o("WZ", 1, 16, 2), o("IN16"), cJ15)
+    lin(o("WQ", 0, 16, 2), o("IN16"), cJd)
+    lin(o("WQ", 1, 16, 2), o("IN16"), cJ0)
+    fill(o("WO"), 0)
+    lin(o("WO", 1, 80, 2), o("IOT"), e120)
+    var = {"p": o("XV", 0, 8), "n": o("XV", 8, 16), "w": o("XV", 16, 24), "r": o("XV", 24, 32), "a": o("XV", 32, 40),
+           "f": o("ID", 96, 104), "s": o("ID", 104, 112), "u": o("ID", 112, 120), "1": o("ID", 120, 128)}
+    ell = [("w", 1), ("a", -16), ("f", -1), ("u", -2.0 ** -14), ("r", -128)]
+    layer = ([("p", 1), ("f", 64), ("1", -64)], [("r", -1), ("a", -1), ("f", 64), ("1", -63)],
+             [("n", 1), ("f", 1), ("s", -1)], [("n", 1), ("f", 1), ("s", -1), ("1", -16)],
+             ell + [("1", 17)], ell + [("1", -30)], ell + [("1", -31)],
+             [("1", 1), ("n", -1), ("f", -65), ("s", 1)],
+             [("p", 1), ("r", -1), ("n", -1), ("f", 63), ("s", 1), ("a", -64), ("1", -62)],
+             [("a", 1), ("s", 1), ("1", -1)],
+             [("p", 1), ("n", 1), ("f", 65), ("s", -1), ("r", -1), ("a", -64), ("1", -95)],
+             [("p", 1), ("n", 1), ("f", 1), ("s", -1), ("1", -32)],
+             [("p", 1)], [], [("n", 1)], [], [("w", 1)], [("w", 1), ("1", -31), ("1", -16)], [("w", 1), ("1", -32), ("1", -16)],
+             [("p", 1), ("n", -1), ("1", 1)], [], [], [], [])
+    parts = {-128: (-64, -64), 17: (16, 1), -30: (-16, -16, 1, 1), -31: (-16, -16, 1), -32: (-16, -16), -63: (-64, 1), -65: (-64, -1),
+             63: (64, -1), 65: (64, 1), -62: (-64, 1, 1), -95: (-64, -16, -16, 1)}
+    ent = sorted([(v != 1, v, 8 * so, nm) for so, lst in enumerate(layer) for (nm, v0) in lst for v in parts.get(v0, (v0,))])
+    vals = sorted(set(e[1] for e in ent) - {1}) + [-256, -4096]
+    sid = lambda v: o("ID") if v == 1 else o("SID", 128 * vals.index(v), 128 * vals.index(v) + 128)
+    for v in vals:
+        lin(sid(v), o("ID"), float(v))
     ms(o("ZER"), 0.0)
-    mm(o("XA0", 0, 384), o("ID"), o("ZER", 0, 384), True, False)
-    for k, (c, si, v) in enumerate(ent):
-        r = o("ID", 8 * si, 8 * si + 8) if v == 1 else o("SID", 128 * vals.index(v) + 8 * si, 128 * vals.index(v) + 8 * si + 8)
-        mm(o("XA0", c, c + 8), o("ID"), r, False, k == len(ent) - 1)
-    act(o("WM"), o("XA0", 0, 360), AF.Copy)
-    cp(o("WX"), o("XA0", 360, 384))
+    mm(o("KY1", 0, 192), o("ID"), o("ZER"), True, False)
+    for k, (_, v, c, nm) in enumerate(ent):
+        mm(o("KY1", c, c + 8), sid(v), var[nm], False, k == len(ent) - 1)
+    lin(o("WM"), o("KY1", 0, 192))
+    for i in range(2 * NS):
+        fill(o("CT", 64 * i, 64 * i + 16), 0)
 
-    tmpb = ("MP0", "MP1", "KY0", "KY1")
     for k in range(8):
-        x = o("PW", 512 * k, 512 * k + 512)
-        act(o(tmpb[k % 4]), x, AF.Relu, HH, -254.0 * HH)
-        tt(x, x, o(tmpb[k % 4]), AL.subtract)
-    for b in ("BW", "CW"):
-        iota(o(b, 4608, 5120), [[0, 512]], 0, 0)
-        iota(o(b, 0, 512), [[0, 512]], 0, 0)
-    for k in range(4):
-        iota(o("GW", 1216 * k, 1216 * k + 1216), [[0, 1216]], 0, 0)
-    cp(o("BOu"), o("BOi"))
-    cp(o("GSu"), o("GSi"))
-
-    def cur(t, h):
-        b = (4608 if t % 2 == 0 else 0) + 256 * h
-        return o("CW", b, b + 256, 2)
-
-    def win(b, t):
-        return o(b, 512, 5120) if t % 2 == 0 else o(b, 0, 4608)
-
-    def to_b(t, h, c0, c1):
-        H = str(h)
-        ts(o("Y" + H), o("VC" + H), -2048.0, None, AL.add, None, o("YO"))
-        for gq in range(8):
-            mm(o("KY" + H, 128, 144), o("FW", 112 - 16 * gq, 240 - 16 * gq), o("Y" + H, 16 * gq, 16 * gq + 16), gq == 0, gq == 7)
-        b = 16 * (t % 2)
-        if c0 == c1:
-            ts(o("OF" + H, b, b + 16), o("KY" + H, 128, 144), c0, None, AL.add)
+        x, y, z = o("PW", 512 * k, 512 * k + 512), o(("MP0", "MP1", "XA1", "XB1")[k % 4]), o("EQ%d" % (k // 4), 512 * (k % 4), 512 * (k % 4) + 512)
+        if k in FIXV:
+            act(y, x, AF.Relu, HH, -254.0 * HH)
+            tt(x, x, y, AL.subtract)
         else:
-            ts(o("OF" + H, b, b + 8), o("KY" + H, 128, 136), c0, None, AL.add)
-            ts(o("OF" + H, b + 8, b + 16), o("KY" + H, 136, 144), c1, None, AL.add)
-        return o("OF" + H, b, b + 8), o("OF" + H, b + 8, b + 16)
+            ts(z, x, 255.0, -HH, AL.is_equal, AL.mult)
+            mm(y, o("ID"), x, True, False)
+            mm(y, o("ID"), z, False, True)
+            lin(x, y)
+    fill(o("BW", 4096, 4624), 0)
+    fill(o("CW", 4096, 4608), 0)
+    fill(o("GW"), 0)
+    for (a, b) in (("BOi", "BOu"), ("GSi", "GSu")):
+        cp(o("X2"), o(a), o("L1"))
+        add("V", "tr", (o("X3"), o("X2")), [o("X2")], [o("X3")], 512 * CYC)
+        cp(o(b), o("X3"), o("L2"))
+
+    def to_b(t, h, body):
+        H = str(h)
+        n, y0, ps, win = (8, 0, "KY" + H, o("VB" + H)) if body else (16, 64, "MP" + H, o("VC" + H))
+        ts(o("Y" + H, y0, y0 + 8 * n), win, -2048.0, None, AL.add, None, o("YO", y0 // 16, (y0 + 8 * n) // 16))
+        for gq in range(8):
+            x = o(ps, 144, 144 + n, p0=32 * (gq // 2), p1=32 * (gq // 2) + 32)
+            mm(x, o("FW", 16 - 16 * (gq % 2), 48 - 16 * (gq % 2)), o("Y" + H, y0 + n * gq, y0 + n * gq + n), gq % 2 == 0, gq % 2 == 1)
+        b = 24 * (t % 2) + y0 // 8
+        ts(o("OF" + H, b, b + n), o(ps, 144, 144 + n), 2048.0, None, AL.add)
+        return [o("OF" + H, b + k, b + k + 8) for k in range(0, n, 8)]
 
     def message(t, h, off):
         H = str(h)
         m = o("MS" + H, 128 * (t % 2), 128 * (t % 2) + 128)
         top = 2048 if t == 0 else 2048 + 128 * (2 * (t - 1) + h + 1)
         act(m, o("MW", 0, top), AF.Abs, ind=off)
-        for e in range(EX):
-            mm(o("MP" + H, e, 128 * EX, EX), o("ID"), m)
+        mm(o("MP" + H, 0, 128), o("ID"), m)
+
+    def mask(out, x):
+        act(out, x, AF.Sigmoid, -256.0, cBias)
+
+    def offers(t, h, m):
+        H = str(h)
+        XB = "XB" + H
+        mm(o(XB, 128, 256), o("D3"), o("Q" + H))
+        tt(o("ZX" + H), m, o(XB, 128, 256), AL.mult)
+        x = o(XB, 384, 400)
+        mm(x, o("S" + H), o("WO", 16 * t, 16 * t + 16), True, False)
+        mm(x, o("Q" + H), o("WQ"), False, False)
+        mm(x, o("ZX" + H), o("WZ"), False, True)
 
     def update(t, h):
         H = str(h)
         XA, XB = "XA" + H, "XB" + H
-        r0 = o("R0" + H, p1=24)
-        s1 = o("S1" + H, p1=N1)
-        s2 = o("S2" + H, p1=N2)
-        q = o("Q" + H)
-        if t > 0:
-            i = 2 * (t - 1) + h
-            mm(o(XB, 384, 512), o("SHh"), q)
-            mm(o(XA, 0, 128, p1=24), o("CT", 32 * i, 32 * i + 24), o("ID"))
-            act(r0, o(XA, 0, 128, p1=24), AF.Copy)
-        mm(o(XA, 128, 256, p1=N1), o("WM", W21, W21 + N1, p1=N2), s2, True, False)
-        mm(o(XA, 128, 256, p1=N1), o("WM", WR1, WR1 + N1, p1=24), r0, False, True)
-        act(s1, o(XA, 128, 256, p1=N1), AF.Relu)
-        mm(o(XA, 0, 128, p1=N2), o("WM", W12, W12 + N2, p1=N1), s1)
-        ci = 4 + min(2 * t + h, 11)
-        if t > 0:
-            mm(o(XB, 0, 128), o("BC", 0, 128, p1=N1), s1)
-            mm(o(XB, 128, 256), o("BC", 128, 256, p1=N1), s1)
-        act(s2, o(XA, 0, 128, p1=N2), AF.Relu, 1.0, o("HI", ci, ci + 1, p1=N2))
+        s, q = o("S" + H), o("Q" + H)
+        i = 2 * (t - 1) + h
+        mm(o(XB, 0, 128), o("DM"), q, True, False)
+        mm(o(XB, 0, 128), o("E15", p1=1), o("LC", 128 * h, 128 * h + 128, p1=1), False, True)
+        mm(o(XA, 0, 128, p0=96, p1=120), o("CT", 64 * i + 1, 64 * i + 48, 2), o("ID"))
+        (cp if R0V else lin)(o("S" + H, p0=96, p1=120), o(XA, 0, 128, p0=96, p1=120))
+        mm(o(XA, 0, 128, p1=96), o("WM", 0, 96), s)
+        mm(o(XA, 128, 256), o("BC", 0, 128), s)
+        mm(o(XA, 256, 384), o("BC", 128, 256), s)
+        act(o("S" + H, p1=96), o(XA, 0, 128, p1=96), AF.Relu)
+        mask(o("M" + H), o(XA, 128, 384))
+        m1, m2 = o("M" + H, 0, 128), o("M" + H, 128, 256)
         if t == NS:
-            mm(o(XA, 128, 256, p1=24), o("WM", W1F, W1F + 24, p1=N1), s1)
-            act(o("YP", 128 * h, 128 * h + 128, p1=24), o(XA, 128, 256, p1=24), AF.Copy)
+            mm(o(XB, 256, 384), o("IDh"), q, True, False)
+            mm(o(XB, 256, 384), o("LN", p1=1), o("CB", p1=1), False, True)
+            tt(o("T1" + H), m1, o(XB, 0, 128), AL.mult)
+            mm(o(XA, 384, 512, p1=24), o("XV", 0, 24), s)
+            lin(o("YP", 128 * h, 128 * h + 128, p1=24), o(XA, 384, 512, p1=24))
             for k in range(3):
                 x = o("YP", 128 * h, 128 * h + 128, p0=8 * k, p1=8 * k + 8)
                 dma("S", ("ext", "ys", (256 * (k + 1) + 128 * h, 256 * (k + 1) + 128 * h + 128)), x, [x], [], 4096)
-        if t > 0:
-            act(o("M1" + H), o(XB, 0, 128), AF.Sign, -1.0, cJh)
-            ts(o("M2" + H), o(XB, 128, 256), cJ, float(2304 + 128 * (2 * (t - 1) + h)), AL.is_equal, AL.mult)
-            tt(o("T1" + H), o("M1" + H), o(XB, 384, 512), AL.mult)
+            y = o("YQ", 128 * h, 128 * h + 128)
+            tt(o("QF" + H), o("T1" + H), o(XB, 256, 384), AL.add)
+            tt(y, o("QF" + H), m2, AL.mult)
+            dma("S", ("ext", "yq", (128 * h, 128 * h + 128)), y, [y], [], 65536)
+            return
+        mm(o(XB, 256, 384), o("IDh"), q, True, False)
+        mm(o(XB, 256, 384), sid(-256), m2, False, True)
+        tt(o("T1" + H), m1, o(XB, 0, 128), AL.mult)
+        tt(q, o("T1" + H), o(XB, 256, 384), AL.add)
         if t < NS - 1:
-            mm(o(XA, 384, 512), o("BC", 256, 384, p1=N2), s2)
-            ts(o("M3" + H), o(XA, 384, 512), cJ, None, AL.is_equal)
-        if t > 0:
-            mm(o(XB, 0, 128), o("SHp"), q, True, False)
-            mm(o(XB, 0, 128), o("IDh"), o("M2" + H), False, True)
-            if t == NS:
-                qf, qt = o("QF" + H, 0, 128), o("QF" + H, 128, 256)
-                y = o("YQ", 128 * h, 128 * h + 128)
-                tt(qf, o("T1" + H), o(XB, 0, 128), AL.add)
-                ts(qt, qf, 2048.0, None, AL.is_ge)
-                tt(qt, qt, o("LR2"), AL.mult)
-                tt(y, qt, qf, AL.add)
-                dma("S", ("ext", "yq", (128 * h, 128 * h + 128)), y, [y], [], 65536)
-                return
-            tt(q, o("T1" + H), o(XB, 0, 128), AL.add)
-        if t < NS - 1:
-            mm(o(XB, 128, 256), o("IDh"), q)
-            tt(o("ZX" + H), o("M3" + H), o(XB, 128, 256), AL.mult)
-            lx = o(XA, 128, 256, p1=72)
-            mm(lx, o("WM", W2X, W2X + 72, p1=N2), s2, True, False)
-            mm(lx, o("HQ"), q, False, False)
-            mm(lx, o("HZ"), o("ZX" + H), False, True)
-            act(o("SX" + H, p1=72), lx, AF.Relu)
-            mm(o(XB, 256, 272), o("SX" + H, p1=72), o("WX", 8, 24, p1=72))
+            mm(o(XA, 384, 512), o("BC", 256, 384), s)
+            if M3V:
+                ts(o("M3" + H), o(XA, 384, 512), cJ, None, AL.is_le)
+            else:
+                mask(o("M3" + H), o(XA, 384, 512))
+            offers(t, h, o("M3" + H))
 
     def start(h):
         H = str(h)
-        XA, XB = "XA" + H, "XB" + H
-        s2 = o("S2" + H, p1=N2)
-        ts(o("S2" + H), o("LR"), n8(9), n8(8), AL.mult, AL.add)
-        cp(o("S2" + H, p1=24), o("STi", 128 * h, 128 * h + 128, p1=24))
-        ts(col("CC", 22 + h), n8(1), 128.0, 1.0, AL.mult, AL.add)
-        ts(o("R0" + H), o("ONE"), col("CC", 22 + h), None, AL.mult)
-        cp(o("Q" + H), o("Qi", 128 * h, 128 * h + 128))
-        cp(o("S0f", 128 * h, 128 * h + 128, p1=8), o("S0i", 128 * h, 128 * h + 128, p1=8))
-        ms(o("VC" + H, 16, 32), 2048.0)
-        ts(o("CF" + H, 32, 40), o("IO16", 0, 8), 0.0, cL[0, h], AL.mult, AL.add)
-        mm(o(XB, 256, 384), o("BC", 384, 512, p1=N2), s2)
-        mm(o(XB, 128, 256), o("IDh"), o("Q" + H))
-        ts(o("M3" + H), o(XB, 256, 384), cJ, None, AL.is_equal)
-        tt(o("ZX" + H), o("M3" + H), o(XB, 128, 256), AL.mult)
-        mm(o(XA, 256, 264), o("S0f", 128 * h, 128 * h + 128, p1=8), o("I8f", p1=8))
-        mm(o(XA, 264, 272), o("ZX" + H), o("INh"))
-        cp(o("VC" + H, 0, 16), o(XA, 256, 272))
-        f0, f1 = to_b(1, h, 2048.0, 2048.0)
-        ts(cur(0, h), o("CLs"), cK, None, AL.add, None, f0)
-        message(0, h, f1)
-        update(0, h)
+        XA, XB, VC = "XA" + H, "XB" + H, "VC" + H
+        s, q = o("S" + H), o("Q" + H)
+        hs = lambda b, **k: o(b, 128 * h, 128 * h + 128, **k)
+        lin(s, one, n8(15))
+        ts(o("S" + H, p1=24), hs("STi", p1=24), cS1[:2] + (24,) + cS1[3:], None, AL.mult)
+        cp(o("S" + H, p0=32, p1=40), hs("STi", p0=32, p1=40))
+        if h == 0:
+            cp(o("S0f", p1=16), o("STi", p1=16))
+            for a in range(16):
+                mm(o("KY0", 0, 16), o("WS", 15 - a, 143 - a, p1=16), o("S0f", a, 256, 16, p1=16), a == 0, a == 15)
+            cp(o("SO"), o("KY0", 0, 16))
+        cp(o("CU" + H), o("CLs"), o("SO", 8 * h, 8 * h + 8))
+        cp(o("CW", 4096 + 256 * h, 4352 + 256 * h, 2), o("CU" + H))
+        fill(o(VC, 0, 136), 2 ** 20)
+        fill(o(VC, 136, 168), 2048)
+        fill(o("VB" + H), 2048)
+        iota(o(VC, 0, 136, 17), [[0, 8]], 4096 + 256 * h, 2)
+        mm(o(XA, 128, 256), o("BC", 0, 128), s)
+        mm(o(XA, 256, 384), o("BC", 128, 256), s)
+        mask(o("M" + H), o(XA, 128, 384))
+        mm(o(XB, 0, 128), o("LN", p1=1), hs("LC", p1=1), True, False)
+        mm(o(XB, 0, 128), sid(-4096), o("M" + H, 128, 256), False, True)
+        ts(o("CH" + H), hs("Qi"), -384.0, None, AL.add)
+        tt(q, o("CH" + H), o(XB, 0, 128), AL.max)
+        offers(0, h, o("M" + H, 0, 128))
+        scan(o(VC, 144, 160), o("AL01"), o(XB, 384, 400), 0.0, AL.mult, AL.add)
+        ts(o(VC, 144, 160), o(VC, 144, 160), 2047.0, None, AL.min)
+        message(0, h, to_b(1, h, False)[1])
+        mm(o(XA, 0, 128, p1=96), o("WM", 96, 192), s)
+        act(o("S" + H, p1=96), o(XA, 0, 128, p1=96), AF.Relu)
+        mm(o(XA, 384, 512), o("BC", 256, 384), s)
+        mask(o("M3" + H), o(XA, 384, 512))
+        offers(0, h, o("M3" + H))
 
     def tables():
-        for k in range(8):
-            x, f = o("CW", 512 + 512 * k, 1024 + 512 * k), o("GSu", 32 * k, 32 * k + 32)
-            j1 = ts(x, o("CLs"), cK, None, AL.add, None, f)
-            j2 = act(o("BW", 512 + 512 * k, 1024 + 512 * k), o("PW"), AF.Copy, -1.0, ind=o("BOu", 32 * k, 32 * k + 32))
-            if k < TC:
-                chain["V"].append(j1)
-                chain["A"].append(j2)
-        x = o("GW", 0, 4096)
-        dma("S", ("rows", "GW", 0, 4096), ("ext", "gs", None), [], [x], 131072)
-        x = o("GW", 4608, 4864)
-        dma("S", ("rows", "GW", 4608, 4864), ("ext", "s0", None), [], [x], 8192)
-        cp(o("GW", 4096, 4608, 2), x)
+        for r in range(8):
+            cp(o("CW", 512 * r, 512 * r + 512), o("CLs"), o("GSu", 32 * r, 32 * r + 32))
+            x, f = o("BW", 512 * r, 512 * r + 512), o("BOu", 32 * r, 32 * r + 32)
+            if r < BV:
+                ts(x, o("PW"), -1.0, None, AL.mult, None, f)
+            else:
+                act(x, o("PW"), AF.Copy, -1.0, ind=f)
+        dma("S", ("rows", "GW", 0, 256), ("ext", "s0", None), [], [o("GW")], 8192)
 
     chain = {"A": [], "V": []}
 
     def wide(t, h):
         H = str(h)
         P, EQ, KY = "P" + H, "EQ" + H, "KY" + H
-        if t == 0 or not FUSE:
-            ts(o("CU" + H), cur(t, h), cK, None, AL.subtract)
-        mm(o(KY, 0, 128), cur(t, h), o("ID16"), True, False)
+        ts(o("CH" + H), o("CU" + H), -2048.0, None, AL.add)
+        mm(o(KY, 0, 136), o("CH" + H), o("IX"), True, False)
+        pv = PV if t >= PT else 0
+        if pv:
+            cp(o(P, 16 * (128 - pv), 2048), o("PW"), o("CU" + H, 128 - pv, 128))
         for (a, b) in GP:
+            b = min(b, 128 - pv)
             chain["A"] = [act(o(P, 16 * a, 16 * b), o("PW"), AF.Copy, ind=o("CU" + H, a, b), after=chain["A"])]
-        st = 16 // EX
         for (a, b) in PIECES:
-            for k in range(st):
-                c = 128 * EX * k
-                m = o("MP" + H, EX * a, EX * b)
-                if k < NM and a == 0 and t > 0:
+            for k in range(16):
+                m = o("MP" + H, a, b)
+                if k < NM and a == 0:
                     m = o("MS" + H, 128 * (t % 2) + a, 128 * (t % 2) + b)
-                chain["V"] = [tt(o(EQ, c + EX * a, c + EX * b), o(P, 16 * a + k, 16 * b, st), m, AL.is_equal, after=chain["V"])]
+                chain["V"] = [tt(o(EQ, 128 * k + a, 128 * k + b), o(P, 16 * a + k, 16 * b, 16), m, AL.is_equal, after=chain["V"])]
         for k in range(16):
-            mm(o(KY, k, 128, 16), o(P, k, 2048, 16), o("INp"), False, False)
-        mm(o(KY, 0, 128), o("S2" + H, p1=N2), o("BC", 512, 640, p1=N2), False, False)
+            mm(o(KY, k, 136, 17), o(P, k, 2048, 16), o("INp"), False, False)
+        mm(o(KY, 0, 136), o("S" + H), o("PN"), False, False)
         for k in range(16):
-            kk = k // EX + st * (k % EX)
-            c = 128 * EX * (k // EX)
-            mm(o(KY, kk, 128, 16), o(EQ, c + k % EX, c + 128 * EX, EX), o("INe"), False, k == 15)
+            mm(o(KY, k, 136, 17), o(EQ, 128 * k, 128 * k + 128), o("INe"), False, k == 15)
 
     def choose(t, h):
         H = str(h)
         i = 2 * t + h
-        XA = "XA" + H
-        ci = lambda k: o("CI" + H, 8 * k, 8 * k + 8)
-        cf = lambda k: o("CF" + H, 8 * k, 8 * k + 8)
-        add("V", "scan", (o("RS" + H), o("RST"), o("KY" + H, 0, 128)), [o("RST"), o("KY" + H, 0, 128)], [o("RS" + H)], 128 * CYC)
-        rs = o("RS" + H, 15, 128, 16)
-        nf = o("CT", 32 * i, 32 * i + 8)
-        cp(ci(1), rs)
-        ts(nf, rs, 4.0, None, AL.is_lt)
-        ts(cf(0), rs, 4.0, cL[t % 2, h], AL.is_lt, AL.mult)
-        ts(ci(2), ci(1), 4080, None, AL.bitwise_and)
-        ts(ci(3), ci(1), 12, 15, AL.arith_shift_right, AL.bitwise_and)
-        ts(ci(4), ci(1), 4, 4095, AL.arith_shift_right, AL.bitwise_and)
-        land = o("CT", 32 * i + 16, 32 * i + 24)
-        j = add("G", "rdma", (land, nf, t, "af%d" % i), [nf], [], 500.0, 0.0)
-        add("X", "arr", ("af%d" % i,), [], [land], 0.0, 2600.0, after=[j])
-        tt(cf(1), ci(2), cf(0), AL.add)
-        tt(o("VC" + H, 0, 8), ci(3), cf(1), AL.add)
-        tt(cf(3), nf, cf(4), AL.mult)
+        VC = "VC" + H
+        scan(o("RS" + H, 0, 136), o(VC, 0, 136), o("KY" + H, 0, 136), BIG, AL.min, AL.max)
+        rs, z = o("RS" + H, 15, 136, 17), o("RS" + H, 136, 144)
+        nf, u = o("CT", 64 * i + 1, 64 * i + 16, 2), o("CT", 64 * i + 33, 64 * i + 48, 2)
+        ts(u, rs, MAG, MAG, AL.add, AL.subtract)
+        ts(z, rs, 4608.0, None, AL.max)
+        ts(nf, rs, 8192.0, None, AL.is_lt)
+        tt(o("VB" + H, 136, 144), z, u, AL.subtract)
+        fb = to_b(t, h, True)
+        land, x = o("CT", 64 * i + 16, 64 * i + 32), o("CT", 64 * i, 64 * i + 16)
+        j = add("G", "rdma", (land, x, t, "af%d" % i), [x], [], 500.0, 0.0)
+        add("X", "arr", ("af%d" % i, j), [], [land], 0.0, 2600.0, after=[j])
+        tt(o(VC, 0, 136, 17), rs, u, AL.subtract)
         if t < NS - 1:
-            tt(cf(2), nf, o("XB" + H, 264, 272), AL.mult)
-            tt(o("VC" + H, 8, 16), cf(2), o("XB" + H, 256, 264), AL.add)
-            tt(cf(4), cf(3), ci(4), AL.add)
-        else:
-            tt(o("VC" + H, 8, 16), cf(3), ci(4), AL.add)
-        act(o("CT", 32 * i + 8, 32 * i + 16), rs, AF.Identity, 2.0 ** -16, col("CC", 14))
-        f0, f1 = to_b(t, h, 2048.0 if t % 2 == 0 else 2560.0, 2048.0)
+            scan(o(VC, 144, 160), x, o("XB" + H, 384, 400), 0.0, AL.mult, AL.add)
+        f = to_b(t, h, False)
         if t < NS - 1:
-            if FUSE:
-                ts(o("CU" + H), win("CW", t), cK, None, AL.subtract, None, f0)
-            if FUSE == 2:
-                ts(cur(t + 1, h), o("CU" + H), cK, None, AL.add)
-            else:
-                act(cur(t + 1, h), win("CW", t), AF.Copy, ind=f0)
+            cp(o("CU" + H), o("CW"), f[0])
+        if i == 2 * NS - 3:
+            dma("S", ("rows", "CW", 0, 4096), ("ext", "gs", None), [], [o("CW", 0, 4096)], 131072)
+            cp(o("CW", 4096, 4608, 2), o("GW"))
         snd = o("SND", 128 * i, 128 * i + 128)
-        tt(snd, win("BW", t), o("MS" + H, 128 * (t % 2), 128 * (t % 2) + 128), AL.min, f0)
+        tt(snd, o("BW"), o("MS" + H, 128 * (t % 2), 128 * (t % 2) + 128), AL.min, fb[0])
         land = o("MW", 2048 + 128 * i, 2048 + 128 * i + 128)
         j = add("G", "rdma", (land, snd, t, "ad%d" % i), [snd], [], 500.0, 0.0)
-        add("X", "arr", ("ad%d" % i,), [], [land], 0.0, 3200.0, after=[j])
+        add("X", "arr", ("ad%d" % i, j), [], [land], 0.0, 3200.0, after=[j])
         if t < NS - 1:
-            message(t + 1, h, f1)
+            message(t + 1, h, f[1])
         else:
             y = o("YS", 128 * h, 128 * h + 128)
-            cp(y, o("GW", 0, 4608), f1)
+            cp(y, o("CW"), f[0])
             dma("S", ("ext", "ys", (128 * h, 128 * h + 128)), ("rows", "YS", 128 * h, 128 * h + 128), [y], [], 4096)
         if t == NS - 1 or h == 1:
             a = i if t == NS - 1 else i - 1
@@ -516,19 +525,36 @@ def build():
     tables()
     for t in range(NS):
         for h in range(2):
-            ctx[0], ctx[1] = ("step" if t < NS - 1 else "last%d" % h), {}
+            ctx[0], ctx[1], ctx[2] = ("step" if t < NS - 1 else "last%d" % h), {}, (t, h)
             wide(t, h)
             choose(t, h)
             update(t + 1, h)
+    prune(ops)
     return ops
 
 
-CASES = ((0.85, 1.4, 200.0, 1.0, 93.0), (1.25, 2.05, 150.0, 1.0, 125.0), (1.2, 1.2, 200.0, 0.8, 112.0), (0.85, 1.1, 130.0, 1.2, 87.0))
-SEED = 1
+CASES = ((0.83, 1.1, 160.0, 0.7, 77.0), (0.85, 1.45, 190.0, 0.8, 83.0), (0.9, 2.0, 170.0, 0.7, 91.0), (1.2, 1.1, 190.0, 0.7, 102.0),
+         (1.2, 2.0, 150.0, 0.75, 116.0), (0.9, 1.3, 160.0, 1.2, 88.0))
+MID = (0.87, 1.45, 180.0, 0.85)
+PERIOD, FIRST, BUS = 8300.0, 14000.0, 250.0
+SEED, HEAT, AHEAD = 1, 2.0, 5000.0
+SHIFT = {}
+DUE = {("V", "CH"): -1870, ("P", "KY", 1): -1600, ("A", "P", 1): -3900, ("A", "P", 2): -3250, ("A", "P", 3): -2600, ("A", "P", 4): -1950,
+       ("V", "RS", 1): 2200, ("V", "CT", 1): 2500, ("V", "RS", 2): 2510, ("V", "CT", 2): 2520, ("G", "CT"): 2700, ("V", "VB"): 2750,
+       ("V", "VC"): 2760, ("V", "Y", 1): 2980, ("V", "Y", 2): 3120, ("V", "OF", 1): 3650, ("V", "SND"): 3880, ("V", "OF", 2): 3900,
+       ("G", "MW"): 4250, ("V", "CU"): 4150, ("A", "MS"): 7350, ("P", "MP"): 3500, ("P", "MP", 9): 7700,
+       ("P", "XB", 1): 5000, ("P", "XB", 2): 5100, ("P", "XA", 1): 5600, ("A", "S", 1): 7000, ("P", "XA", 2): 6350, ("P", "XA", 3): 6400,
+       ("P", "XA", 4): 6450, ("A", "S", 2): 7000, ("A", "M"): 6800, ("V", "T1"): 7500, ("P", "XB", 3): 5200, ("P", "XB", 4): 7200,
+       ("V", "Q"): 7850, ("P", "XA", 5): 7300, ("A", "M3"): 7750, ("P", "XB", 5): 8250, ("V", "ZX"): 10100, ("P", "XB"): 10350,
+       ("A", "MO"): 7900, ("S", "ext"): 9000, ("V", "S"): 6050, ("V", "M3"): 7300, ("V", "P"): -2200}
+EARLY = {"PI": 0, "L1": 500, "L2": 600, "LF": 300, "X2": 6000, "X3": 6000, "GSu": 6000, "BOu": 6000, "CW": 16000, "PW": 3500, "EQ0": 3400,
+         "EQ1": 3400, "BW": 13400, "MS0": 12000, "MS1": 14500, "OF0": 9000, "OF1": 11000, "SO": 5000, "CU0": 7100, "CU1": 10100}
 
 
-def recost(ops, c, gt):
-    res = []
+def graph(ops, c, gt, l, f):
+    cost = []
+    lat = []
+    bus = 0.0
     for p in ops:
         k = {"ts": 6, "tt": 4, "cp": 2, "act": 5}.get(p["kind"])
         v = p["cost"]
@@ -536,145 +562,229 @@ def recost(ops, c, gt):
             if k is not None and p["args"][k] is not None:
                 v += nel(p["args"][0]) * (gt - GTH) * CYC
             v *= c / CYC
-        res.append(dict(p, cost=v))
-    return res
+        cost.append(v)
+        v = p["lat"] * (f if p["eng"] == "X" else 1.0)
+        if p["kind"] == "dma":
+            bus = p["args"][2] / BUS + (bus - 60.0 if p["args"][1][0] == "ext" and p["args"][0][0] != "rows" else 0.0)
+            v += bus
+        lat.append(v)
+    fw = [[(j, cost[j] + (lat[j] + l if p["deps"][j] or ops[j]["eng"] != p["eng"] else 0.0)) for j in p["near"]] for p in ops]
+    return cost, lat, fw
 
 
-def plan(ops, rounds=40, climbs=1000):
-    n = len(ops)
-    succ = [[] for _ in range(n)]
-    left = [len(p["deps"]) for p in ops]
-    for i, p in enumerate(ops):
-        for j in p["deps"]:
-            succ[j].append(i)
-    dur = [p["cost"] + p["lat"] + (p["args"][2] / 250.0 if p["kind"] == "dma" else 0.0) for p in ops]
-    lvl = [0.0] * n
-    for i in range(n - 1, -1, -1):
-        lvl[i] = dur[i] + max([lvl[k] + (LAT if ops[k]["deps"][i] else 0.0) for k in succ[i]] + [0.0])
-    sets = [(recost(ops, c, gt), l, f, w) for (c, gt, l, f, w) in CASES]
-
-    def score(r):
-        v = [replay(q, r[0], l, f) / w for (q, l, f, w) in sets]
-        return 1000.0 * (sum(v) / len(v) + max(v)) / 2
-    best = None
-    rng = np.random.default_rng(SEED)
-    for it in range(rounds):
-        if it < 200 or it % 2 == 0:
-            fa, fv = 1.0 + 0.8 * float(rng.random()), 1.0 + 2.0 * float(rng.random())
-            la = LAT * (1.0 + 3.0 * float(rng.random()))
-            z = rng.random(n) * (0.0, 50.0, 200.0)[it % 3]
-            pr = [0.0] * n
-            for i in range(n - 1, -1, -1):
-                nm = ops[i]["args"][0][0]
-                d = dur[i] * (fa if nm in ("P0", "P1") else fv if nm in ("EQ0", "EQ1") else 1.0)
-                pr[i] = d + max([pr[k] + (la if ops[k]["deps"][i] else 0.0) for k in succ[i]] + [0.0])
-            up = {"BOu": 1e5, "PW": 4000.0}
-            ba, bv = 6000.0 * float(rng.random()), 6000.0 * float(rng.random())
-            for nm in ("R0", "S1", "S2", "M1", "MS", "CW"):
-                up[nm] = ba
-            for nm in ("T1", "M2", "M3", "Q", "ZX", "SX"):
-                up[nm] = bv
-            pr = [pr[i] + float(z[i]) + up.get(ops[i]["cls"][3] if ops[i]["cls"][0] else ops[i]["args"][0][0], 0.0) for i in range(n)]
-        else:
-            o2, beg, fin = best[1:]
-            nxt = {}
-            late = [0.0] * n
-            end = best[0]
-            for i in reversed(o2):
-                p = ops[i]
-                f = min([late[k] - (LAT if ops[k]["deps"][i] or ops[k]["eng"] != p["eng"] else -p["cost"]) for k in succ[i]] + [end])
-                s = f - dur[i]
-                if p["eng"] != "X" and it % 2 == 1:
-                    s = min(s, nxt.get(p["eng"], end) - p["cost"])
-                    nxt[p["eng"]] = s
-                late[i] = s
-            amp = (100.0, 300.0, 800.0)[it % 3]
-            z = rng.random(n)
-            mix = float(rng.random())
-            pr = [-(mix * late[i] + (1 - mix) * (end - lvl[i])) + amp * float(z[i]) for i in range(n)]
-        r = once(ops, succ, list(left), pr, (60.0, 150.0, 300.0)[(it // 3) % 3])
-        v = score(r)
-        if best is None or v < best[0]:
-            best = (v,) + r
-            keep = (pr, (60.0, 150.0, 300.0)[(it // 3) % 3])
-    names = {}
-    cls = np.array([names.setdefault(p["cls"], len(names)) for p in ops])
-    small = [k for k in range(len(names)) if any(p["eng"] in "VAG" for p in ops if names[p["cls"]] == k)]
-    rep = [k for k in small if int((cls == k).sum()) > 2]
-    base = np.array(keep[0])
-    delta = np.zeros(len(names))
-    for it in range(climbs):
-        d = delta.copy()
-        pool = rep if it % 3 else small
-        for k in range(1 + it % 4):
-            d[pool[int(rng.integers(len(pool)))]] += float(rng.normal()) * (300.0, 1000.0, 3000.0)[it % 3]
-        r = once(ops, succ, list(left), [float(v) for v in base + d[cls]], keep[1])
-        v = score(r)
-        if v <= best[0]:
-            best = (v,) + r
-            delta = d
-    return best[1:]
+def prune(ops):
+    anc = []
+    for p in ops:
+        hard = 0
+        a = 0
+        for j, w in p["deps"].items():
+            a |= anc[j] | (1 << j)
+            if w or ops[j]["eng"] != p["eng"]:
+                hard |= anc[j]
+        anc.append(a)
+        p["near"] = [j for j in p["deps"] if ops[j]["lat"] or not hard >> j & 1]
 
 
-def once(ops, succ, left, lvl, slack):
-    n = len(ops)
+def replay(eng, g, order):
+    cost, lat, fw = g
+    beg = [0.0] * len(eng)
     free = {}
-    fin = [0.0] * n
-    beg = [0.0] * n
-    est = {}
-    order = []
-    bus = 0.0
-    for i in range(n):
-        if left[i] == 0:
-            est[i] = 0.0
-    while est:
-        b = min(est, key=lambda i: (max(est[i], free.get(ops[i]["eng"], 0.0)), i))
-        e = ops[b]["eng"]
-        t0 = max(est[b], free.get(e, 0.0))
-        c = [i for i in est if ops[i]["eng"] == e and est[i] <= t0 + min(slack, 0.5 * ops[b]["cost"] + 40.0)]
-        i = max(c, key=lambda k: (lvl[k], -k))
-        s = max(est[i], free.get(e, 0.0))
-        p = ops[i]
+    end = 0.0
+    for i in order:
+        e = eng[i]
+        s = free.get(e, 0.0)
+        for j, d in fw[i]:
+            if beg[j] + d > s:
+                s = beg[j] + d
         beg[i] = s
         if e != "X":
-            free[e] = s + p["cost"]
-        if p["kind"] == "dma":
-            bus = max(bus, s + p["lat"]) + p["args"][2] / 250.0
-            fin[i] = bus
-        else:
-            fin[i] = s + p["cost"] + p["lat"]
-        del est[i]
+            free[e] = s + cost[i]
+        if s + cost[i] + lat[i] > end:
+            end = s + cost[i] + lat[i]
+    return end
+
+
+def once(eng, g, succ, due, slack):
+    cost, lat, fw = g
+    n = len(eng)
+    left = [len(x) for x in fw]
+    beg = [0.0] * n
+    ready = {e: {} for e in "VAPGSX"}
+    free = {e: 0.0 for e in ready}
+    nxt = {}
+    order = []
+    for i in range(n):
+        if left[i] == 0:
+            ready[eng[i]][i] = 0.0
+            nxt[eng[i]] = 0.0
+    while nxt:
+        e = min(nxt, key=nxt.get)
+        r = ready[e]
+        lim = nxt[e] + slack[e]
+        i = min([k for k in r if r[k] <= lim], key=lambda k: due[k])
+        s = max(r.pop(i), free[e])
+        beg[i] = s
+        if e != "X":
+            free[e] = s + cost[i]
         order.append(i)
+        if r:
+            nxt[e] = max(min(r.values()), free[e])
+        else:
+            del nxt[e]
         for k in succ[i]:
             left[k] -= 1
             if left[k] == 0:
-                est[k] = max((fin[j] + LAT if w or ops[j]["eng"] != ops[k]["eng"] else beg[j]) for j, w in ops[k]["deps"].items())
-    return order, beg, fin
+                v = max([beg[j] + d for j, d in fw[k]])
+                x = eng[k]
+                ready[x][k] = v
+                v = max(v, free[x])
+                if v < nxt.get(x, 1e18):
+                    nxt[x] = v
+    return order
 
 
-def replay(ops, order, lat, far):
+def plan(ops, climbs=2500, tries=0, polish=4500):
     n = len(ops)
-    fin = [0.0] * n
-    beg = [0.0] * n
-    free = {}
-    bus = 0.0
-    for i in order:
-        p = ops[i]
-        e = p["eng"]
-        s = free.get(e, 0.0)
-        for j, w in p["deps"].items():
-            v = fin[j] + lat if w or ops[j]["eng"] != e else beg[j]
-            if v > s:
-                s = v
-        beg[i] = s
-        if e != "X":
-            free[e] = s + p["cost"]
-        if p["kind"] == "dma":
-            bus = max(bus, s + p["lat"]) + p["args"][2] / 250.0
-            fin[i] = bus
+    eng = [p["eng"] for p in ops]
+    sets = [(graph(ops, c, gt, l, f), w) for (c, gt, l, f, w) in CASES]
+    mid = graph(ops, *MID)
+    succ = [[] for _ in range(n)]
+    for i, p in enumerate(ops):
+        for j in p["near"]:
+            succ[j].append(i)
+    names = {}
+    cls = []
+    base = [None] * n
+    for i, p in enumerate(ops):
+        c, e, nm, k = p["cls"]
+        if not c:
+            cls.append(names.setdefault(("", e, nm), len(names)))
+            if p["kind"] == "dma" and nm != "rows":
+                base[i] = -20000.0
+            elif nm in EARLY:
+                base[i] = EARLY[nm] + 0.1 * i
+            continue
+        t, h = p["at"]
+        if (e, nm) == ("V", "EQ"):
+            v, k = 1700.0 * k / (16 * len(PIECES)), (k - 1) // 4
+        elif (e, nm) == ("P", "KY") and k > 1:
+            v, k = (-250.0 + k, 2) if k < 18 else (300.0, 3) if k == 18 else (53.0 * k + 100.0, 4 + (k - 19) // 4) if k < 35 else (3300.0 + k, 9)
+        elif (e, nm) == ("P", "MP") and k < 9:
+            v, k = DUE[e, nm] + k, 1
         else:
-            fin[i] = s + p["cost"] + p["lat"] * (far if e == "X" else 1.0)
-    return max(fin)
+            v = DUE.get((e, nm, k), DUE.get((e, nm), 7000.0)) + k
+        base[i] = FIRST + PERIOD * (t + 0.5 * h) + v
+        cls.append(names.setdefault((c, e, nm, k), len(names)))
+    for i in range(n - 1, -1, -1):
+        if base[i] is None:
+            base[i] = min([base[k] - d - (AHEAD if ops[k]["at"] else 0.0) for k in succ[i] for j, d in mid[2][k] if j == i] + [60000.0])
+    cls = np.array(cls)
+    base = np.array(base) + 0.001 * np.arange(n)
+    slack = {"V": 150.0, "A": 500.0, "P": 300.0, "G": 200.0, "S": 0.0, "X": 0.0}
+
+    def score(d):
+        r = once(eng, mid, succ, (base + d[cls]).tolist(), slack)
+        v = [replay(eng, g, r) / w for (g, w) in sets]
+        return (sum(v) / len(v) + max(v)) / 2, r
+    rng = np.random.default_rng(SEED)
+    delta = np.array([float(SHIFT.get(" ".join(str(x) for x in c), 0)) for c in names])
+    first = best = cur = score(delta) + (delta,)
+    rep = [k for c, k in names.items() if c[0] == "step"]
+    for it in range(climbs * (tries + 1)):
+        if it % climbs == 0:
+            cur = first if it < climbs * tries else best
+        d = cur[2].copy()
+        if it % 2:
+            held = waits(ops, eng, sets[int(rng.integers(len(sets)))][0], cur[1])
+            held = [(i, y) for (i, y) in held if cls[i] != cls[y]]
+            i, y = held[int(rng.integers(len(held)))]
+            gap = max(0.0, base[i] + d[cls[i]] - base[y] - d[cls[y]]) + 10.0 + 300.0 * float(rng.random()) ** 2
+            if it % 4 == 1:
+                d[cls[i]] -= gap
+            else:
+                d[cls[y]] += gap
+        else:
+            for k in range(1 + it % 3):
+                x = rep[int(rng.integers(len(rep)))] if it % 4 else int(rng.integers(len(names)))
+                d[x] += float(rng.normal()) * (200.0, 700.0, 2500.0)[(it // 4) % 3]
+        v = score(d)
+        if v[0] <= cur[0] + HEAT * float(rng.random()) * (1.0 - it % climbs / climbs):
+            cur = v + (d,)
+            if v[0] < best[0]:
+                best = cur
+    beg = starts(eng, mid, best[1])
+    per = [i for i in range(n) if ops[i]["at"] == (2, 0) and ops[i]["cls"][1:] == ("V", "RS", 1)][0]
+    nxt = [i for i in range(n) if ops[i]["at"] == (2, 1) and ops[i]["cls"][1:] == ("V", "RS", 1)][0]
+    half = beg[nxt] - beg[per]
+    names = {}
+    cls = np.array([names.setdefault(p["cls"] if p["at"] and 1 <= p["at"][0] < NS - 1 else i, len(names)) for i, p in enumerate(ops)])
+    ref = {p["cls"]: beg[i] for i, p in enumerate(ops) if p["at"] == (2, 0)}
+    base = np.array([ref[p["cls"]] + half * (2 * p["at"][0] + p["at"][1] - 4) if p["at"] and 1 <= p["at"][0] < NS - 1 and p["cls"] in ref
+                     else beg[i] for i, p in enumerate(ops)])
+    near = [p["near"] for p in ops]
+
+    def rank(d):
+        due = (base + d[cls]).tolist()
+        for i in range(n):
+            for j in near[i]:
+                if due[j] >= due[i]:
+                    due[i] = due[j] + 0.01
+        r = sorted(range(n), key=lambda i: due[i])
+        v = [replay(eng, g, r) / w for (g, w) in sets]
+        return (sum(v) / len(v) + max(v)) / 2, r, d, due
+    cur = rank(np.zeros(len(names)))
+    top = cur if cur[0] < best[0] else best
+    for it in range(polish):
+        held = [(i, y) for (i, y) in waits(ops, eng, sets[int(rng.integers(len(sets)))][0], cur[1]) if cls[i] != cls[y]]
+        i, y = held[int(rng.integers(len(held)))]
+        d = cur[2].copy()
+        far = 1.0 + (0.0, 60.0, 300.0)[it % 3] * float(rng.random())
+        if it % 2:
+            d[cls[i]] = cur[3][y] - far - base[i]
+        else:
+            d[cls[y]] = cur[3][i] + far - base[y]
+        v = rank(d)
+        if v[0] <= cur[0] + HEAT * float(rng.random()) * (1.0 - it / polish):
+            cur = v
+            if v[0] < top[0]:
+                top = v
+    return top[1], top[0], best[0]
+
+
+def starts(eng, g, order):
+    cost, lat, fw = g
+    beg = [0.0] * len(eng)
+    free = {}
+    for i in order:
+        s = max([free.get(eng[i], 0.0)] + [beg[j] + d for j, d in fw[i]])
+        beg[i] = s
+        if eng[i] != "X":
+            free[eng[i]] = s + cost[i]
+    return beg
+
+
+def waits(ops, eng, g, order):
+    cost, lat, fw = g
+    beg = [0.0] * len(eng)
+    why = [-1] * len(eng)
+    last = {}
+    for i in order:
+        e = eng[i]
+        y = last.get(e, -1)
+        s = beg[y] + cost[y] if y >= 0 else 0.0
+        for j, d in fw[i]:
+            if beg[j] + d >= s:
+                s, y = beg[j] + d, j
+        beg[i], why[i] = s, y
+        if e != "X":
+            last[e] = i
+    i = max(order, key=lambda k: beg[k] + cost[k] + lat[k])
+    res = []
+    while why[i] >= 0:
+        if why[i] not in ops[i]["deps"]:
+            res.append((i, why[i]))
+        i = why[i]
+    return res
 
 
 CACHE = {}
@@ -691,7 +801,6 @@ def rank_program(g, core, T, topo):
     nr = len(T.cores)
     qs = {"V": g.vector, "A": g.scalar, "P": g.tensor, "G": g, "S": g.sync}
     dest = [T.cores[(rank + 1 + t % (nr - 1)) % nr] for t in range(NS)]
-    srcs = [T.cores[(rank - 1 - t % (nr - 1)) % nr] for t in range(NS)]
     engs = set(range(16))
     for a in T.cores:
         for b in T.cores:
@@ -709,10 +818,6 @@ def rank_program(g, core, T, topo):
             return T[x[1]][:] if x[2] is None else T[x[1]][:, x[2][0]:x[2][1]]
         if x[0] == "rows":
             return T[x[1]][0:128:16, x[2]:x[3]]
-        if x[6] is not None:
-            if x[6][1] - x[6][0] == 1:
-                return T[x[0]][:, x[3]:x[4], x[6][0]]
-            return T[x[0]][:, x[3]:x[4], x[6][0]:x[6][1]]
         if x[5] == 1:
             return T[x[0]][x[1]:x[2], x[3]:x[4]]
         return T[x[0]][x[1]:x[2], x[3]:x[4]:x[5]]
@@ -788,13 +893,17 @@ def rank_program(g, core, T, topo):
             r = q.tensor_copy(ap(a[0]), src(a[1], a[2]))
         elif kind == "ms":
             r = q.memset(ap(a[0]), a[1])
+        elif kind == "red":
+            r = q.tensor_reduce(ap(a[0]), ap(a[1]), AxisListType.X, AL.add)
+        elif kind == "tr":
+            r = q.transpose(ap(a[0]), ap(a[1]))
         elif kind == "scan":
-            r = q.tensor_tensor_scan(ap(a[0]), ap(a[1]), ap(a[2]), 0.0, AL.mult, AL.max)
+            r = q.tensor_tensor_scan(ap(a[0]), ap(a[1]), ap(a[2]), a[3], a[4], a[5])
         elif kind == "act":
             if a[4] != 0.0:
-                r = q.activation(ap(a[0]), src(a[1], a[5]), a[2], bias=ap(a[4]), scale=a[3])
+                r = q.activation(ap(a[0]), src(a[1], a[5]), a[2], bias=ap(a[4]), scale=ap(a[3]))
             elif a[3] != 1.0:
-                r = q.activation(ap(a[0]), src(a[1], a[5]), a[2], scale=a[3])
+                r = q.activation(ap(a[0]), src(a[1], a[5]), a[2], scale=ap(a[3]))
             else:
                 r = q.activation(ap(a[0]), src(a[1], a[5]), a[2])
         elif kind == "mm":

@@ -5,12 +5,19 @@ from concourse.mybir import dt, AluOpType, AxisListType, ActivationFunctionType
 AL = AluOpType
 AF = ActivationFunctionType
 NS = 6
-PIECES = ((0, 64), (64, 128))
-GP = ((0, 32), (32, 64), (64, 96), (96, 128))
+PIECES = ((0, 128),)
+GP = ((0, 56), (56, 128))
 PT = 1
+CA = 2
+CUA = True
+LV = ("SID", "BC", "BT", "S0", "S1", "ZP", "SH0", "IDh", "IX", "WS")
+PS = 16
+CHA = False
+Y2A = False
+O2A = False
 PV = 16
-BV = 2
-FIXV = (3, 7)
+BV = 3
+FIXV = (1, 3, 5, 7)
 NM = 0
 M3V = False
 R0V = True
@@ -22,13 +29,13 @@ BYTES = {F32: 4, BF: 2, F16: 2, I32: 4, U16: 2}
 
 SCRATCH = {}
 for _d, _l in (
-        (BF, (("PW", 4096), ("BW", 4624), ("MW", 3584), ("SND", 1536), ("MO", 1536), ("CT", 768), ("ONE", 144), ("WSb", 144), ("ZER", 192), ("ID", 128),
+        (BF, (("PW", 4096), ("BW", 4624), ("MW", 3584), ("SND", 1536), ("MO", 1536), ("CT", 768), ("ONE", 160), ("WSb", 144), ("ZB", 160), ("ZER", 192), ("ID", 128),
               ("IXb", 136), ("SID", 1280), ("SH0", 128), ("BU", 272), ("INe", 8), ("INp", 8), ("AL01", 16), ("G8", 128),
               ("BC", 384), ("BT", 256), ("PN", 136), ("XV", 40), ("WM", 192), ("WO", 80))),
         (I32, (("CW", 4608), ("CLs", 2048), ("GW", 256), ("BOi", 256), ("GSi", 256), ("Qi", 256), ("STi", 256), ("PI", 16))),
-        (U16, (("BOu", 256), ("GSu", 256), ("L1", 32), ("L2", 16), ("YO", 12), ("SO", 16))),
-        (F16, (("IDh", 128), ("WS", 144), ("S0f", 256), ("IX", 136), ("DM", 128), ("D3", 128), ("E15", 128), ("LN", 128), ("CB", 128), ("LC", 256), ("FW", 48), ("WQ", 16))),
-        (F32, (("X2", 512), ("X3", 512), ("LF", 32), ("CC", 40), ("I1f", 8), ("IO16", 16), ("IOG", 128), ("IOH", 136),
+        (U16, (("BOu", 256), ("GSu", 256), ("YO", 12), ("SO", 16))),
+        (F16, (("IDh", 128), ("X2", 256), ("X3", 256), ("ZP", 320), ("ZF", 256), ("WS", 144), ("S0f", 256), ("IX", 136), ("DM", 128), ("D3", 128), ("E15", 128), ("LN", 128), ("CB", 128), ("LC", 256), ("FW", 48), ("WQ", 16))),
+        (F32, (("CC", 40), ("I1f", 8), ("IO16", 16), ("IOG", 128), ("IOH", 136),
                ("IOK", 136), ("IOJ", 128), ("IOT", 40), ("LP", 256), ("IN8", 16), ("IN16", 8), ("D8", 8), ("I8f", 8), ("WZ", 16),
                ("YT", 24), ("YF", 24), ("YQ", 256), ("YS", 256), ("YP", 256)))):
     for _n, _c in _l:
@@ -79,7 +86,7 @@ def build():
     hist = {}
     bank = {}
     lastpe = {}
-    ctx = ["", {}, None]
+    ctx = ["", {}, None, "constants"]
 
     def add(eng, kind, args, reads, writes, cost, lat=0.0, after=()):
         i = len(ops)
@@ -123,7 +130,8 @@ def build():
         nm = args[0][0] if isinstance(args[0], tuple) else args[0][:2]
         key = (ctx[0], eng, nm[:-1] if nm[-1] in "01" and nm[:-1] + "1" in SCRATCH and nm[:-1] + "0" in SCRATCH and ctx[0] else nm)
         ctx[1][key] = ctx[1].get(key, 0) + 1
-        ops.append({"eng": eng, "kind": kind, "args": args, "deps": deps, "cost": cost, "lat": lat, "cls": key + (ctx[1][key],), "at": ctx[2]})
+        ops.append({"eng": eng, "kind": kind, "args": args, "deps": deps, "cost": cost, "lat": lat, "cls": key + (ctx[1][key],), "at": ctx[2],
+                    "part": ctx[3]})
         return i
 
     def aps(*xs):
@@ -159,6 +167,8 @@ def build():
         return add("A", "act", (out, a, f, scale, bias, ind), aps(a, ind, bias, scale), [out], c * CYC, after=after)
 
     def lin(out, a, scale=1.0, bias=0.0):
+        if out[0] in LV and not ctx[0] and not isps(a):
+            return ts(out, a, scale, bias, AL.mult, AL.add)
         return act(out, a, AF.Copy if bias == 0.0 else AF.Identity, scale, bias)
 
     def mm(out, l, r, s0=True, s1=True):
@@ -199,7 +209,6 @@ def build():
     iota(col("PI", 0), [[0, 1]], 0, 1)
     asel(o("ID"), one, [[-1, 128]], 0, 1)
     iota(o("IO16"), [[1, 16]], 0, 0)
-    iota(o("LF"), [[16, 16], [0, 2]], 0, 0)
     for (c, n, b, s) in ((0, 4, 136, 2), (4, 8, 0, 17), (12, 4, 137, 2), (16, 8, 145, 2)):
         iota(o("YT", c, c + n), [[s, n]], b, 0)
     iota(o("IOG"), [[1, 8], [0, 16]], 0, 0)
@@ -212,15 +221,18 @@ def build():
     asel(o("SH0"), one, [[-1, 128]], -1, 1)
     asel(o("IXb"), o("ONE", 0, 136), [[-16, 8], [-1, 17]], 0, 1)
     for c, (s, op) in enumerate(((15, AL.bitwise_and), (4, AL.arith_shift_right), (3, AL.arith_shift_right), (7, AL.bitwise_and),
-                                 (8, AL.bitwise_and), (31, AL.bitwise_and))):
+                                 (8, AL.bitwise_and), (16, AL.bitwise_and))):
         ts(col("PI", c + 1), col("PI", 0), s, None, op)
     cp(o("CC", 0, 7), o("PI", 0, 7))
     cP, cJ, cP16, cP8, cM8, cQ8, cP32 = [col("CC", c) for c in range(7)]
     cJ16, cBias, cN0, cJ15, cJd, cEB, cE1, cE0, cE2 = [col("CC", c) for c in range(7, 16)]
     vp, vn, vr, vw, c1, c2a, c3, c3b, cpn, cA, cB, cBa, cJ0, cCB, cS1, cBG = [col("CC", c) for c in range(16, 32)]
-    lin(cJ16, cJ, 31.0, cP32)
-    ts(o("L1"), o("LF"), cJ, None, AL.add)
-    ts(o("L2"), o("IO16"), cJ16, None, AL.add)
+    lin(cJ16, cP32, -1.0 / 16, 1.0)
+    asel(o("ZB"), o("ONE"), [[1, 160]], -16, -1)
+    lin(o("ZP", 0, 160), o("ZB"), cJ16)
+    lin(o("ZP", 160, 320), o("ZB"), cP32)
+    lin(o("ZP", 160, 320), o("ZP", 160, 320), 1.0 / 16)
+    ms(o("ZF"), 0.0)
     lin(cBias, cJ, 256.0, 128.0)
     ts(cJ0, cJ, 0.0, None, AL.is_equal)
     ts(cJ15, cJ, 15.0, None, AL.is_equal)
@@ -242,7 +254,7 @@ def build():
     lin(o("IDh"), o("ID"))
     lin(o("IX"), o("IXb"))
     lin(o("LC", p1=1), o("LP", p1=1))
-    asel(o("WSb", p1=16), o("ONE", p1=16), [[1, 144]], 113, -16)
+    asel(o("WSb", p1=16), o("ONE", 0, 144, p1=16), [[1, 144]], 113, -16)
     lin(o("WS", p1=16), o("WSb", p1=16))
     lin(o("I1f"), o("ID", 120, 128))
     e120, e121, e122 = [col("I1f", c) for c in range(3)]
@@ -318,6 +330,7 @@ def build():
     for i in range(2 * NS):
         fill(o("CT", 64 * i, 64 * i + 16), 0)
 
+    ctx[3] = "variables"
     for k in range(8):
         x, y, z = o("PW", 512 * k, 512 * k + 512), o(("MP0", "MP1", "XA1", "XB1")[k % 4]), o("EQ%d" % (k // 4), 512 * (k % 4), 512 * (k % 4) + 512)
         if k in FIXV:
@@ -328,23 +341,38 @@ def build():
             mm(y, o("ID"), x, True, False)
             mm(y, o("ID"), z, False, True)
             lin(x, y)
+    ctx[3] = "fills"
     fill(o("BW", 4096, 4624), 0)
     fill(o("CW", 4096, 4608), 0)
     fill(o("GW"), 0)
-    for (a, b) in (("BOi", "BOu"), ("GSi", "GSu")):
-        cp(o("X2"), o(a), o("L1"))
-        add("V", "tr", (o("X3"), o("X2")), [o("X2")], [o("X3")], 512 * CYC)
-        cp(o(b), o("X3"), o("L2"))
+    for (a, b, ps) in (("BOi", "BOu", "KY0"), ("GSi", "GSu", "KY1")):
+        ctx[3] = b
+        lin(o("X2"), o(a), 1.0, -2048.0)
+        add("V", "tr", (o("X3"), o("X2")), [o("X2")], [o("X3")], 128 * CYC)
+        mm(o(ps, 0, 256), o("IDh"), o("ZF"), True, False)
+        for m0 in range(2):
+            for g0 in range(2):
+                c = 160 * m0 + 16 + 16 * (m0 - g0)
+                for m in range(8):
+                    mm(o(ps, 2 * m + m0, 256, 16), o("ZP", c, c + 128), o("X3", 32 * m + 16 * g0, 32 * m + 16 * g0 + 16), False,
+                       m0 + g0 + m == 9)
+        ts(o(b), o(ps, 0, 256), 2048.0, None, AL.add)
 
     def to_b(t, h, body):
         H = str(h)
         n, y0, ps, win = (8, 0, "KY" + H, o("VB" + H)) if body else (16, 64, "MP" + H, o("VC" + H))
-        ts(o("Y" + H, y0, y0 + 8 * n), win, -2048.0, None, AL.add, None, o("YO", y0 // 16, (y0 + 8 * n) // 16))
+        if Y2A and not body:
+            act(o("Y" + H, y0, y0 + 8 * n), win, AF.Identity, 1.0, -2048.0, ind=o("YO", y0 // 16, (y0 + 8 * n) // 16))
+        else:
+            ts(o("Y" + H, y0, y0 + 8 * n), win, -2048.0, None, AL.add, None, o("YO", y0 // 16, (y0 + 8 * n) // 16))
         for gq in range(8):
             x = o(ps, 144, 144 + n, p0=32 * (gq // 2), p1=32 * (gq // 2) + 32)
             mm(x, o("FW", 16 - 16 * (gq % 2), 48 - 16 * (gq % 2)), o("Y" + H, y0 + n * gq, y0 + n * gq + n), gq % 2 == 0, gq % 2 == 1)
         b = 24 * (t % 2) + y0 // 8
-        ts(o("OF" + H, b, b + n), o(ps, 144, 144 + n), 2048.0, None, AL.add)
+        if O2A and not body:
+            lin(o("OF" + H, b, b + n), o(ps, 144, 144 + n), 1.0, 2048.0)
+        else:
+            ts(o("OF" + H, b, b + n), o(ps, 144, 144 + n), 2048.0, None, AL.add)
         return [o("OF" + H, b + k, b + k + 8) for k in range(0, n, 8)]
 
     def message(t, h, off):
@@ -410,6 +438,7 @@ def build():
 
     def start(h):
         H = str(h)
+        ctx[3] = "start" + H
         XA, XB, VC = "XA" + H, "XB" + H, "VC" + H
         s, q = o("S" + H), o("Q" + H)
         hs = lambda b, **k: o(b, 128 * h, 128 * h + 128, **k)
@@ -446,7 +475,10 @@ def build():
 
     def tables():
         for r in range(8):
-            cp(o("CW", 512 * r, 512 * r + 512), o("CLs"), o("GSu", 32 * r, 32 * r + 32))
+            if r < CA:
+                act(o("CW", 512 * r, 512 * r + 512), o("CLs"), AF.Copy, ind=o("GSu", 32 * r, 32 * r + 32))
+            else:
+                cp(o("CW", 512 * r, 512 * r + 512), o("CLs"), o("GSu", 32 * r, 32 * r + 32))
             x, f = o("BW", 512 * r, 512 * r + 512), o("BOu", 32 * r, 32 * r + 32)
             if r < BV:
                 ts(x, o("PW"), -1.0, None, AL.mult, None, f)
@@ -459,11 +491,14 @@ def build():
     def wide(t, h):
         H = str(h)
         P, EQ, KY = "P" + H, "EQ" + H, "KY" + H
-        ts(o("CH" + H), o("CU" + H), -2048.0, None, AL.add)
+        if CHA:
+            lin(o("CH" + H), o("CU" + H), 1.0, -2048.0)
+        else:
+            ts(o("CH" + H), o("CU" + H), -2048.0, None, AL.add)
         mm(o(KY, 0, 136), o("CH" + H), o("IX"), True, False)
         pv = PV if t >= PT else 0
-        if pv:
-            cp(o(P, 16 * (128 - pv), 2048), o("PW"), o("CU" + H, 128 - pv, 128))
+        for a in range(128 - pv, 128, PS):
+            cp(o(P, 16 * a, 16 * (a + PS)), o("PW"), o("CU" + H, a, a + PS))
         for (a, b) in GP:
             b = min(b, 128 - pv)
             chain["A"] = [act(o(P, 16 * a, 16 * b), o("PW"), AF.Copy, ind=o("CU" + H, a, b), after=chain["A"])]
@@ -499,7 +534,10 @@ def build():
             scan(o(VC, 144, 160), x, o("XB" + H, 384, 400), 0.0, AL.mult, AL.add)
         f = to_b(t, h, False)
         if t < NS - 1:
-            cp(o("CU" + H), o("CW"), f[0])
+            if CUA:
+                act(o("CU" + H), o("CW"), AF.Copy, ind=f[0])
+            else:
+                cp(o("CU" + H), o("CW"), f[0])
         if i == 2 * NS - 3:
             dma("S", ("rows", "CW", 0, 4096), ("ext", "gs", None), [], [o("CW", 0, 4096)], 131072)
             cp(o("CW", 4096, 4608, 2), o("GW"))
@@ -533,22 +571,23 @@ def build():
     return ops
 
 
-CASES = ((0.83, 1.1, 160.0, 0.7, 77.0), (0.85, 1.45, 190.0, 0.8, 83.0), (0.9, 2.0, 170.0, 0.7, 91.0), (1.2, 1.1, 190.0, 0.7, 102.0),
-         (1.2, 2.0, 150.0, 0.75, 116.0), (0.9, 1.3, 160.0, 1.2, 88.0))
+CASES = ((0.83, 1.1, 160.0, 0.7, 71.8), (0.85, 1.45, 190.0, 0.8, 79.0), (0.9, 2.0, 170.0, 0.7, 86.4), (1.2, 1.1, 190.0, 0.7, 94.9),
+         (1.2, 2.0, 150.0, 0.75, 108.4), (0.9, 1.3, 160.0, 1.2, 85.0))
 MID = (0.87, 1.45, 180.0, 0.85)
-PERIOD, FIRST, BUS = 8300.0, 14000.0, 250.0
-SEED, HEAT, AHEAD = 1, 2.0, 5000.0
+PERIOD, FIRST, BUS = 8200.0, 13000.0, 250.0
+HAND = True
+SEED, HEAT, AHEAD = 1, 2.0, 8000.0
 SHIFT = {}
-DUE = {("V", "CH"): -1870, ("P", "KY", 1): -1600, ("A", "P", 1): -3900, ("A", "P", 2): -3250, ("A", "P", 3): -2600, ("A", "P", 4): -1950,
-       ("V", "RS", 1): 2200, ("V", "CT", 1): 2500, ("V", "RS", 2): 2510, ("V", "CT", 2): 2520, ("G", "CT"): 2700, ("V", "VB"): 2750,
-       ("V", "VC"): 2760, ("V", "Y", 1): 2980, ("V", "Y", 2): 3120, ("V", "OF", 1): 3650, ("V", "SND"): 3880, ("V", "OF", 2): 3900,
-       ("G", "MW"): 4250, ("V", "CU"): 4150, ("A", "MS"): 7350, ("P", "MP"): 3500, ("P", "MP", 9): 7700,
-       ("P", "XB", 1): 5000, ("P", "XB", 2): 5100, ("P", "XA", 1): 5600, ("A", "S", 1): 7000, ("P", "XA", 2): 6350, ("P", "XA", 3): 6400,
-       ("P", "XA", 4): 6450, ("A", "S", 2): 7000, ("A", "M"): 6800, ("V", "T1"): 7500, ("P", "XB", 3): 5200, ("P", "XB", 4): 7200,
-       ("V", "Q"): 7850, ("P", "XA", 5): 7300, ("A", "M3"): 7750, ("P", "XB", 5): 8250, ("V", "ZX"): 10100, ("P", "XB"): 10350,
-       ("A", "MO"): 7900, ("S", "ext"): 9000, ("V", "S"): 6050, ("V", "M3"): 7300, ("V", "P"): -2200}
-EARLY = {"PI": 0, "L1": 500, "L2": 600, "LF": 300, "X2": 6000, "X3": 6000, "GSu": 6000, "BOu": 6000, "CW": 16000, "PW": 3500, "EQ0": 3400,
-         "EQ1": 3400, "BW": 13400, "MS0": 12000, "MS1": 14500, "OF0": 9000, "OF1": 11000, "SO": 5000, "CU0": 7100, "CU1": 10100}
+DUE = {("V", "CH"): -2100, ("P", "KY", 1): -1900, ("A", "P", 1): -3750, ("A", "P", 2): -3090, ("A", "P", 3): -2430, ("A", "P", 4): -1200,
+       ("V", "P", 1): -700, ("V", "P", 2): -700, ("V", "RS", 1): 2150, ("V", "CT", 1): 2440, ("V", "RS", 2): 2490, ("V", "CT", 2): 2545,
+       ("G", "CT"): 2750, ("V", "VB"): 2730, ("V", "VC", 1): 2780, ("V", "VC", 2): 2840, ("V", "Y", 1): 2960, ("V", "Y", 2): 3090,
+       ("V", "OF", 1): 3610, ("V", "OF", 2): 3790, ("V", "SND"): 3850, ("G", "MW"): 4230, ("A", "CU"): 4100, ("P", "MP"): 3470,
+       ("P", "XB", 1): 4600, ("P", "XB", 2): 4650, ("P", "XB", 3): 4700, ("P", "XA", 1): 5450, ("V", "S"): 5900, ("P", "XA", 2): 6180,
+       ("P", "XA", 3): 6200, ("P", "XA", 4): 6220, ("A", "M"): 6680, ("A", "S"): 6890, ("P", "XB", 4): 7010, ("P", "XA", 5): 7080,
+       ("A", "MS"): 7360, ("V", "T1"): 7400, ("A", "M3"): 7580, ("V", "M3"): 7420, ("A", "MO"): 7690, ("P", "MP", 9): 7700, ("V", "Q"): 7770,
+       ("P", "XB", 5): 8050, ("V", "ZX"): 9900, ("P", "XB"): 10180, ("S", "ext"): 9000, ("X", "af"): 2800, ("X", "ad"): 4300}
+EARLY = {"variables": 500, "BOu": 3000, "start0": 4000, "GSu": 5000, "start1": 6000, "CT": 9000, "CW": 15500, "BW": 11500, "GW": 12000,
+         "MS1": 13200, "CU0": 100, "CU1": 200}
 
 
 def graph(ops, c, gt, l, f):
@@ -643,7 +682,7 @@ def once(eng, g, succ, due, slack):
     return order
 
 
-def plan(ops, climbs=2500, tries=0, polish=4500):
+def plan(ops, climbs=1000, tries=0, polish=(9500, 3000)):
     n = len(ops)
     eng = [p["eng"] for p in ops]
     sets = [(graph(ops, c, gt, l, f), w) for (c, gt, l, f, w) in CASES]
@@ -655,32 +694,34 @@ def plan(ops, climbs=2500, tries=0, polish=4500):
     names = {}
     cls = []
     base = [None] * n
+    table = {}
     for i, p in enumerate(ops):
         c, e, nm, k = p["cls"]
         if not c:
-            cls.append(names.setdefault(("", e, nm), len(names)))
+            cls.append(names.setdefault((p["part"], e, nm), len(names)))
             if p["kind"] == "dma" and nm != "rows":
                 base[i] = -20000.0
-            elif nm in EARLY:
-                base[i] = EARLY[nm] + 0.1 * i
+            elif nm in EARLY or p["part"] in EARLY:
+                base[i] = EARLY.get(nm, EARLY.get(p["part"])) + 0.1 * i
             continue
         t, h = p["at"]
         if (e, nm) == ("V", "EQ"):
             v, k = 1700.0 * k / (16 * len(PIECES)), (k - 1) // 4
         elif (e, nm) == ("P", "KY") and k > 1:
-            v, k = (-250.0 + k, 2) if k < 18 else (300.0, 3) if k == 18 else (53.0 * k + 100.0, 4 + (k - 19) // 4) if k < 35 else (3300.0 + k, 9)
+            v, k = (-400.0 + 42 * k, 2) if k < 18 else (450.0, 3) if k == 18 else (53.0 * k + 80.0, 4 + (k - 19) // 4) if k < 35 else (3220.0 + k, 9)
         elif (e, nm) == ("P", "MP") and k < 9:
             v, k = DUE[e, nm] + k, 1
         else:
             v = DUE.get((e, nm, k), DUE.get((e, nm), 7000.0)) + k
         base[i] = FIRST + PERIOD * (t + 0.5 * h) + v
+        table[p["cls"]] = v
         cls.append(names.setdefault((c, e, nm, k), len(names)))
     for i in range(n - 1, -1, -1):
         if base[i] is None:
             base[i] = min([base[k] - d - (AHEAD if ops[k]["at"] else 0.0) for k in succ[i] for j, d in mid[2][k] if j == i] + [60000.0])
     cls = np.array(cls)
     base = np.array(base) + 0.001 * np.arange(n)
-    slack = {"V": 150.0, "A": 500.0, "P": 300.0, "G": 200.0, "S": 0.0, "X": 0.0}
+    slack = {"V": 150.0, "A": 250.0, "P": 300.0, "G": 200.0, "S": 0.0, "X": 0.0}
 
     def score(d):
         r = once(eng, mid, succ, (base + d[cls]).tolist(), slack)
@@ -719,35 +760,47 @@ def plan(ops, climbs=2500, tries=0, polish=4500):
     names = {}
     cls = np.array([names.setdefault(p["cls"] if p["at"] and 1 <= p["at"][0] < NS - 1 else i, len(names)) for i, p in enumerate(ops)])
     ref = {p["cls"]: beg[i] for i, p in enumerate(ops) if p["at"] == (2, 0)}
+    if HAND:
+        ref = {c: beg[per] + (table[c] - DUE["V", "RS", 1]) * 2 * half / PERIOD for c in ref}
     base = np.array([ref[p["cls"]] + half * (2 * p["at"][0] + p["at"][1] - 4) if p["at"] and 1 <= p["at"][0] < NS - 1 and p["cls"] in ref
                      else beg[i] for i, p in enumerate(ops)])
     near = [p["near"] for p in ops]
 
-    def rank(d):
-        due = (base + d[cls]).tolist()
+    def rank(due, d, c, bound):
         for i in range(n):
             for j in near[i]:
                 if due[j] >= due[i]:
                     due[i] = due[j] + 0.01
         r = sorted(range(n), key=lambda i: due[i])
-        v = [replay(eng, g, r) / w for (g, w) in sets]
-        return (sum(v) / len(v) + max(v)) / 2, r, d, due
-    cur = rank(np.zeros(len(names)))
-    top = cur if cur[0] < best[0] else best
-    for it in range(polish):
-        held = [(i, y) for (i, y) in waits(ops, eng, sets[int(rng.integers(len(sets)))][0], cur[1]) if cls[i] != cls[y]]
-        i, y = held[int(rng.integers(len(held)))]
-        d = cur[2].copy()
-        far = 1.0 + (0.0, 60.0, 300.0)[it % 3] * float(rng.random())
-        if it % 2:
-            d[cls[i]] = cur[3][y] - far - base[i]
-        else:
-            d[cls[y]] = cur[3][i] + far - base[y]
-        v = rank(d)
-        if v[0] <= cur[0] + HEAT * float(rng.random()) * (1.0 - it / polish):
-            cur = v
-            if v[0] < top[0]:
-                top = v
+        x = replay(eng, sets[c][0], r) / sets[c][1]
+        if x > bound:
+            return None
+        v = [x if k == c else replay(eng, g, r) / w for k, (g, w) in enumerate(sets)]
+        return (sum(v) / len(v) + max(v)) / 2, r, d, due, v, {}
+    cur = top = rank(base.tolist(), np.zeros(len(names)), 0, 1e9)
+    for stage in range(2):
+        if stage:
+            base, cls = np.array(starts(eng, mid, top[1] if top[0] < best[0] else best[1])), np.arange(n)
+            cur = top = rank(base.tolist(), np.zeros(n), 0, 1e9)
+        for it in range(polish[stage]):
+            c = int(rng.integers(len(sets)))
+            if c not in cur[5]:
+                cur[5][c] = [(i, y) for (i, y) in waits(ops, eng, sets[c][0], cur[1]) if cls[i] != cls[y]]
+            i, y = cur[5][c][int(rng.integers(len(cur[5][c])))]
+            d = cur[2].copy()
+            far = 1.0 + (0.0, 60.0, 300.0)[it % 3] * float(rng.random())
+            if it % 7 == 0:
+                d[cls[y]] = cur[3][y] + 1500.0 * float(rng.normal()) - base[y]
+            elif it % 2:
+                d[cls[i]] = cur[3][y] - far - base[i]
+            else:
+                d[cls[y]] = cur[3][i] + far - base[y]
+            heat = HEAT * float(rng.random()) * (1.0 - it / polish[stage]) / (1 + 3 * stage)
+            v = rank((base + d[cls]).tolist(), d, c, cur[4][c] + 2.0 * heat + 1.0)
+            if v and v[0] <= cur[0] + heat:
+                cur = v
+                if v[0] < top[0]:
+                    top = v
     return top[1], top[0], best[0]
 
 

@@ -1,3 +1,4 @@
+import math
 import numpy as np
 from concourse.bass import DstId, RemoteDMATransfer
 from concourse.mybir import dt, AluOpType, AxisListType, ActivationFunctionType
@@ -6,43 +7,38 @@ AL = AluOpType
 AF = ActivationFunctionType
 NS = 6
 PIECES = ((0, 128),)
-GP = ((0, 56), (56, 128))
-PT = 1
-CA = 2
-CUA = True
+GP = (0, 0.45, 0.85, 1)
+CC = (0, 32, 64, 96, 128, 160, 192, 208, 224, 240, 256)
+CA = 128
 LV = ("SID", "BC", "BT", "S0", "S1", "ZP", "SH0", "IDh", "IX", "WS")
-PS = 16
-CHA = False
-Y2A = False
-O2A = False
-PV = 16
-BV = 3
-FIXV = (1, 3, 5, 7)
-NM = 0
-M3V = False
-R0V = True
+PS = 10
+ON = {"CH": "V", "OM": "V", "S": "V", "BOu": "V", "GSu": "V"}
+PV = (30, 20, 20, 20, 20, 20)
+BV = 4
+FIXV = (5, 7)
 HH = float(2 ** 60)
-BIG = float(2 ** 20)
+BIG = 2 ** 20
 MAG = 1.5 * 2.0 ** 37
 F32, BF, F16, I32, U16 = "float32", "bfloat16", "float16", "int32", "uint16"
 BYTES = {F32: 4, BF: 2, F16: 2, I32: 4, U16: 2}
 
 SCRATCH = {}
 for _d, _l in (
-        (BF, (("PW", 4096), ("BW", 4624), ("MW", 3584), ("SND", 1536), ("MO", 1536), ("CT", 768), ("ONE", 160), ("WSb", 144), ("ZB", 160), ("ZER", 192), ("ID", 128),
-              ("IXb", 136), ("SID", 1280), ("SH0", 128), ("BU", 272), ("INe", 8), ("INp", 8), ("AL01", 16), ("G8", 128),
-              ("BC", 384), ("BT", 256), ("PN", 136), ("XV", 40), ("WM", 192), ("WO", 80))),
-        (I32, (("CW", 4608), ("CLs", 2048), ("GW", 256), ("BOi", 256), ("GSi", 256), ("Qi", 256), ("STi", 256), ("PI", 16))),
-        (U16, (("BOu", 256), ("GSu", 256), ("YO", 12), ("SO", 16))),
-        (F16, (("IDh", 128), ("X2", 256), ("X3", 256), ("ZP", 320), ("ZF", 256), ("WS", 144), ("S0f", 256), ("IX", 136), ("DM", 128), ("D3", 128), ("E15", 128), ("LN", 128), ("CB", 128), ("LC", 256), ("FW", 48), ("WQ", 16))),
-        (F32, (("CC", 40), ("I1f", 8), ("IO16", 16), ("IOG", 128), ("IOH", 136),
-               ("IOK", 136), ("IOJ", 128), ("IOT", 40), ("LP", 256), ("IN8", 16), ("IN16", 8), ("D8", 8), ("I8f", 8), ("WZ", 16),
-               ("YT", 24), ("YF", 24), ("YQ", 256), ("YS", 256), ("YP", 256)))):
+        (BF, (("PW", 4096), ("BW", 4624), ("MW", 3584), ("SND", 1536), ("MO", 1536), ("CT", 2880), ("ONE", 160), ("ZB", 160), ("ZER", 192),
+              ("IXb", 136), ("SID", 1280), ("SH0", 128), ("INe", 8), ("INp", 8), ("F2", 160), ("FT", 160), ("G8", 128), ("RD", 136),
+              ("BC", 384), ("BS", 128), ("PN", 136), ("XV", 40), ("WM", 192), ("WO", 400), ("IOG", 128), ("IOH", 136), ("IOK", 136))),
+        (I32, (("CW", 4608), ("CLs", 2048), ("GW", 256), ("BOi", 288), ("GSi", 256), ("Qi", 256), ("STi", 256), ("PI", 16))),
+        (U16, (("BOu", 272), ("GSu", 256))),
+        (F16, (("IDh", 128), ("X2", 288), ("X3", 288), ("ZP", 320), ("ZF", 272), ("IX", 136), ("DM", 256), ("D3", 128), ("E15", 128),
+               ("LN", 128), ("CB", 384), ("LC", 256), ("FW", 48), ("WQ", 80))),
+        (F32, (("CC", 40), ("IO16", 16), ("LP", 256), ("IN8", 16), ("IN16", 8), ("D8", 8), ("WZ", 80),
+               ("YQ", 256), ("YS", 256), ("YP", 256)))):
     for _n, _c in _l:
         SCRATCH[_n] = ("sbuf", [128, _c], _d)
 for _h in range(2):
-    for _n, _c, _d in (("P", 2048, BF), ("EQ", 2048, BF), ("CU", 128, U16), ("CH", 128, F16), ("MS", 256, BF), ("RS", 144, F32),
-                       ("VC", 168, F32), ("VB", 168, F32), ("Y", 192, F16), ("OF", 48, U16), ("S", 128, BF), ("Q", 128, F16), ("M", 256, BF),
+    for _n, _c, _d in (("P", 2048, BF), ("EQ", 2048, BF), ("CU", 128, U16), ("CH", 128, F16), ("MS", 256, BF), ("RS", 1488, F32),
+                       ("VB", 80, F32), ("Y", 80, F16), ("Z", 80, F16), ("OF", 16, U16), ("OM", 16, U16), ("S", 896, BF),
+                       ("Q", 128, F16), ("M", 256, BF),
                        ("M3", 128, BF), ("T1", 128, F32), ("ZX", 128, F32), ("QF", 128, F32)):
         SCRATCH["%s%d" % (_n, _h)] = ("sbuf", [128, _c], _d)
     for _n in ("MP", "KY", "XA", "XB"):
@@ -54,6 +50,8 @@ CYC, PCYC, GTH = 1.0, 0.8, 1.9
 
 
 def o(b, c0=0, c1=None, st=1, p0=0, p1=128):
+    if b == "ID":
+        return ("ZB", p0, p1, 16 + c0, 16 + (c1 or 128), st)
     if c1 is None:
         c1 = SCRATCH[b][1][1]
     return (b, p0, p1, c0, c1, st)
@@ -76,7 +74,7 @@ def span(x):
 
 
 def meet(a, b):
-    if a[4] == b[4] and (a[2] - b[2]) % a[4]:
+    if (a[2] - b[2]) % math.gcd(a[4], b[4]):
         return False
     return a[0] < b[1] and b[0] < a[1] and a[2] < b[3] and b[2] < a[3]
 
@@ -159,7 +157,8 @@ def build():
         return add("V", "red", (out, a), [a], [out], max(64, nel(a)) * CYC)
 
     def scan(out, a, b, init, op0, op1):
-        return add("V", "scan", (out, a, b, init, op0, op1), [a, b], [out], max(64, nel(out)) * CYC)
+        return add("V", "scan", (out, a, b, init, op0, op1), [a, b], [out],
+                   max(64, nel(out) * (0.5 if two(out) and two(a) and two(b) else 1)) * CYC)
 
     def act(out, a, f, scale=1.0, bias=0.0, ind=None, after=()):
         n = nel(out)
@@ -182,84 +181,78 @@ def build():
     def fill(out, v):
         return iota(out, [[0, nel(out)]], v, 0)
 
-    def asel(out, a, pat, base, cm):
-        return add("G", "asel", (out, a, pat, base, cm), [a], [out], 210 + 2 * nel(out) * CYC)
+    def asel(out, a, pat, base, cm, op=AL.is_equal, v=0.0):
+        return add("G", "asel", (out, a, pat, base, cm, op, v), [a], [out], 210 + 2 * nel(out) * CYC)
+
+    def shift(e, out, a, v):
+        return ts(out, a, v, None, AL.add) if e == "V" else act(out, a, AF.Identity, 1.0, v)
 
     def dma(eng, out, src, rd, wr, nbytes, after=()):
-        return add(eng, "dma", (out, src, nbytes), rd, wr, 60.0, 1900.0, after)
+        return add(eng, "dma", (out, src, nbytes), rd, wr, 60.0, 1300.0, after)
 
     def col(b, c):
         return o(b, c, c + 1)
 
-    la = [dma("A", o("BOi"), ("ext", "bo", None), [], [o("BOi")], 131072)]
-    for k, nm in ((0, "p0"), (1, "s0"), (2, "n0"), (4, "w0")):
-        x = o("STi", p0=8 * k, p1=8 * k + 8)
+    la = [dma("A", o("BOi", 0, 256), ("ext", "bo", None), [], [o("BOi", 0, 256)], 131072)]
+    for x, nm in [(o("BOi", 256 + 16 * k, 272 + 16 * k), "s0") for k in range(2)] + [
+            (o("STi", p0=8 * k, p1=8 * k + 8), nm) for k, nm in enumerate(("p0", "p0", "n0", "n0", "w0"))]:
         la = [dma("A", x, ("ext", nm, None), [], [x], 8192, la)]
     ld = []
     for k in range(4):
         x = o("PW", 1024 * k, 1024 * k + 1024)
         ld = [dma("S", x, ("ext", "pt", (1024 * k, 1024 * k + 1024)), [], [x], 262144, ld)]
-        if k < 2:
-            la = [dma("A", o(("Qi", "GSi")[k]), ("ext", ("q0", "gs")[k], None), [], [o(("Qi", "GSi")[k])], 131072, la)]
+    for (b, nm) in (("Qi", "q0"), ("GSi", "gs")):
+        ld = [dma("S", o(b), ("ext", nm, None), [], [o(b)], 131072, ld)]
     ld = [dma("S", o("CLs"), ("ext", "cl", None), [], [o("CLs")], 1048576, ld)]
     ld = [dma("S", o("MW", 0, 2048), ("ext", "m0", None), [], [o("MW", 0, 2048)], 524288, ld)]
 
     ms(o("ONE"), 1.0)
     one = o("ONE", 0, 128)
     iota(col("PI", 0), [[0, 1]], 0, 1)
-    asel(o("ID"), one, [[-1, 128]], 0, 1)
+    asel(o("ZB"), o("ONE"), [[1, 160]], -16, -1)
     iota(o("IO16"), [[1, 16]], 0, 0)
-    for (c, n, b, s) in ((0, 4, 136, 2), (4, 8, 0, 17), (12, 4, 137, 2), (16, 8, 145, 2)):
-        iota(o("YT", c, c + n), [[s, n]], b, 0)
     iota(o("IOG"), [[1, 8], [0, 16]], 0, 0)
     iota(o("IOH"), [[1, 8], [0, 17]], 0, 0)
     iota(o("IOK"), [[0, 8], [-1, 17]], 16, 0)
-    iota(o("IOJ"), [[0, 8], [2, 16]], 1, 0)
-    iota(o("IOT"), [[256, 5], [0, 8]], 384, 0)
-    iota(o("AL01"), [[0, 8], [1, 2]], 0, 0)
     iota(o("LP", p1=1), [[1, 256]], 1664, 0)
-    asel(o("SH0"), one, [[-1, 128]], -1, 1)
     asel(o("IXb"), o("ONE", 0, 136), [[-16, 8], [-1, 17]], 0, 1)
+    fill(o("RD"), 0)
+    fill(o("RD", 0, 136, 17), -BIG)
+    asel(o("FT"), o("ONE"), [[0, 16], [-16, 10]], 16, 1, AL.is_ge, 2.0 ** 40)
+    asel(o("F2"), o("FT"), [[0, 16], [-16, 10]], 32, 1, AL.is_ge)
+    ms(o("F2", 0, 160, 10), 0.0)
+    ts(o("F2", 2, 160, 10), o("F2", 2, 160, 10), 2.0 ** -40, None, AL.mult)
     for c, (s, op) in enumerate(((15, AL.bitwise_and), (4, AL.arith_shift_right), (3, AL.arith_shift_right), (7, AL.bitwise_and),
-                                 (8, AL.bitwise_and), (16, AL.bitwise_and))):
+                                 (16, AL.bitwise_and), (8, AL.bitwise_and))):
         ts(col("PI", c + 1), col("PI", 0), s, None, op)
     cp(o("CC", 0, 7), o("PI", 0, 7))
-    cP, cJ, cP16, cP8, cM8, cQ8, cP32 = [col("CC", c) for c in range(7)]
-    cJ16, cBias, cN0, cJ15, cJd, cEB, cE1, cE0, cE2 = [col("CC", c) for c in range(7, 16)]
-    vp, vn, vr, vw, c1, c2a, c3, c3b, cpn, cA, cB, cBa, cJ0, cCB, cS1, cBG = [col("CC", c) for c in range(16, 32)]
+    cP, cJ, cP16, cP8, cM8, cP32, cQ8 = [col("CC", c) for c in range(7)]
+    cJ16, cBias, cN0, cJ15, cJd, cBS, cJe, cJ1, cB2 = [col("CC", c) for c in range(7, 16)]
+    vp, vn, vr, vw, c1, c2a, c3, c3b, cpn, cA, cK, cJ0, cS1 = [col("CC", c) for c in range(16, 29)]
     lin(cJ16, cP32, -1.0 / 16, 1.0)
-    asel(o("ZB"), o("ONE"), [[1, 160]], -16, -1)
     lin(o("ZP", 0, 160), o("ZB"), cJ16)
-    lin(o("ZP", 160, 320), o("ZB"), cP32)
-    lin(o("ZP", 160, 320), o("ZP", 160, 320), 1.0 / 16)
+    ts(o("ZP", 160, 320), o("ZB"), cP32, 1.0 / 16, AL.mult, AL.mult)
     ms(o("ZF"), 0.0)
-    lin(cBias, cJ, 256.0, 128.0)
+    lin(cBias, cJ, 1.0, 0.5)
+    lin(cB2, cJ, -1.0, -0.5)
+    lin(cK, cP, 2.0)
     ts(cJ0, cJ, 0.0, None, AL.is_equal)
+    ts(cJ1, cJ, 1.0, None, AL.is_equal)
     ts(cJ15, cJ, 15.0, None, AL.is_equal)
-    lin(cN0, cJ0, -1.0, 1.0)
-    lin(cJd, cJ0, -1.0, cJ15)
-    ts(cEB, cP16, cM8, None, AL.is_equal)
-    ts(cE1, cQ8, 0.125, cEB, AL.mult, AL.mult)
-    lin(cE0, cE1, -1.0, cEB)
-    lin(cE2, cEB, -160.0, 160.0)
-    lin(o("YF", 0, 12), o("YT", 0, 12), cE0, cE2)
-    lin(o("YF", 12, 24), o("YT", 12, 24), cE1)
-    tt(o("YF", 0, 12), o("YF", 0, 12), o("YF", 12, 24), AL.add)
-    cp(o("YO"), o("YF", 0, 12))
+    lin(cN0, cJ0, -0.5, 0.5)
+    ts(cJd, cJ15, cJ1, 0.5, AL.subtract, AL.mult)
+    ts(cJe, cJ0, cJ1, 0.5, AL.add, AL.mult)
     ts(o("IN8"), o("IO16"), cP8, None, AL.is_equal)
     ts(o("IN16"), o("IO16", 0, 8), cP16, None, AL.is_equal)
     ts(o("D8"), o("IO16", 0, 8), cM8, None, AL.is_equal)
-    lin(o("INe"), o("IN16"), float(2 ** 19))
+    lin(o("INe"), o("IN16"), -float(2 ** 19))
     lin(o("INp"), o("IN16"), -float(2.0 ** -41))
     lin(o("IDh"), o("ID"))
     lin(o("IX"), o("IXb"))
+    ms(o("IX", 16, 136, 17), 0.0)
     lin(o("LC", p1=1), o("LP", p1=1))
-    asel(o("WSb", p1=16), o("ONE", 0, 144, p1=16), [[1, 144]], 113, -16)
-    lin(o("WS", p1=16), o("WSb", p1=16))
-    lin(o("I1f"), o("ID", 120, 128))
-    e120, e121, e122 = [col("I1f", c) for c in range(3)]
     lin(o("LN", p1=1), o("ONE", 0, 128, p1=1))
-    ts(cS1, cP8, 1.0, None, AL.not_equal)
+    ts(cS1, cQ8, 0.0, None, AL.is_equal)
     ts(o("G8"), o("IOG"), cM8, None, AL.is_equal)
     ms(o("FW"), 0.0)
     ts(o("FW", 16, 32), o("IO16"), cJ, None, AL.is_equal)
@@ -271,39 +264,35 @@ def build():
     for k, v in enumerate((vp, vn, n8(4), vr, vw)):
         lin(o("XV", 8 * k, 8 * k + 8), o("D8"), v)
     lin(c1, n8(12), 64.0, vp)
-    ts(c2a, n8(13), n8(12), vn, AL.subtract, AL.subtract)
+    ts(c2a, n8(14), n8(12), vn, AL.subtract, AL.subtract)
     ts(c3, n8(15), vp, vr, AL.add, AL.subtract)
     lin(c3b, n8(15), 15.0, vp)
     ts(cpn, vr, vw, -2.0 ** 23, AL.add, AL.mult)
     lin(o("BC", 0, 128), o("G8"), c1)
-    lin(o("BT", 0, 128), o("G8"), c2a)
-    lin(o("BT", 128, 256), o("IOJ"), e120)
-    tt(o("BC", 128, 256), o("BT", 0, 128), o("BT", 128, 256), AL.add)
+    lin(o("BC", 128, 256), o("G8"), c2a)
     lin(o("BC", 256, 384), o("G8"), c3)
     lin(o("BC", 271, 384, 16), o("D8"), c3b)
-    lin(cA, e121, 16384.0)
-    lin(cBa, e120, -2.0 ** 23)
-    lin(cB, e122, 2048.0, cBa)
-    lin(cBG, e121, BIG)
-    ts(o("BU", 0, 136), o("IOH"), cM8, cpn, AL.is_equal, AL.mult)
-    lin(o("BU", 136, 272), o("IOK"), cA, cB)
-    tt(o("PN"), o("BU", 0, 136), o("BU", 136, 272), AL.add)
-    lin(o("PN", 16, 136, 17), o("ONE", 0, 8), cBG)
-    lin(o("CB", p1=1), o("ONE", 0, 128, p1=1), 1664.0)
-    lin(o("SH0"), o("SH0"), cN0)
-    tt(o("DM"), o("SH0"), o("ID"), AL.subtract)
-    cp(o("D3"), o("DM"))
-    cp(o("D3", 15, 128, 16), o("DM", 0, 128, 16))
+    lin(cA, o("ID", 121, 122), 16384.0)
+    ts(o("PN"), o("IOH"), cM8, cpn, AL.is_equal, AL.mult)
+    ms(o("PN", 16, 136, 17), 0.0)
+    lin(o("PN", p0=96), o("IOK", p0=96), o("CC", 25, 26, p0=96))
+    ts(cBS, n8(15), n8(14), 256.0, AL.subtract, AL.mult)
+    lin(o("BS"), o("G8"), cBS)
+    for k, v in enumerate((-128.0, 1664.0, -2048.0)):
+        ms(o("CB", 128 * k, 128 * k + 128, p1=1), v)
+    lin(o("SH0"), o("ZB", 17, 145), cN0)
     ms(o("E15", p1=1), 0.0)
-    ms(o("E15", 15, 128, 16, p1=1), 1.0)
-    lin(o("WZ", 0, 16, 2), o("IN16"), -1.0)
-    lin(o("WZ", 1, 16, 2), o("IN16"), cJ15)
-    lin(o("WQ", 0, 16, 2), o("IN16"), cJd)
-    lin(o("WQ", 1, 16, 2), o("IN16"), cJ0)
-    fill(o("WO"), 0)
-    lin(o("WO", 1, 80, 2), o("IOT"), e120)
+    ms(o("E15", 15, 128, 16, p1=1), 0.5)
+    ms(o("WZ"), 0.0)
+    ms(o("WQ"), 0.0)
+    lin(o("WZ", 0, 80, 10), o("IN16"), -1.0)
+    lin(o("WZ", 1, 80, 10), o("IN16"), cJ15)
+    lin(o("WQ", 0, 80, 10), o("IN16"), cJd)
+    lin(o("WQ", 1, 80, 10), o("IN16"), cJe)
+    fill(o("WO", p1=1), 0)
+    iota(o("WO", 1, 400, 10, p1=1), [[256, 5], [0, 8]], 384 - 2048, 0)
     var = {"p": o("XV", 0, 8), "n": o("XV", 8, 16), "w": o("XV", 16, 24), "r": o("XV", 24, 32), "a": o("XV", 32, 40),
-           "f": o("ID", 96, 104), "s": o("ID", 104, 112), "u": o("ID", 112, 120), "1": o("ID", 120, 128)}
+           "f": o("ID", 96, 104), "u": o("ID", 104, 112), "s": o("ID", 112, 120), "1": o("ID", 120, 128)}
     ell = [("w", 1), ("a", -16), ("f", -1), ("u", -2.0 ** -14), ("r", -128)]
     layer = ([("p", 1), ("f", 64), ("1", -64)], [("r", -1), ("a", -1), ("f", 64), ("1", -63)],
              [("n", 1), ("f", 1), ("s", -1)], [("n", 1), ("f", 1), ("s", -1), ("1", -16)],
@@ -315,10 +304,10 @@ def build():
              [("p", 1), ("n", 1), ("f", 1), ("s", -1), ("1", -32)],
              [("p", 1)], [], [("n", 1)], [], [("w", 1)], [("w", 1), ("1", -31), ("1", -16)], [("w", 1), ("1", -32), ("1", -16)],
              [("p", 1), ("n", -1), ("1", 1)], [], [], [], [])
-    parts = {-128: (-64, -64), 17: (16, 1), -30: (-16, -16, 1, 1), -31: (-16, -16, 1), -32: (-16, -16), -63: (-64, 1), -65: (-64, -1),
+    parts = {17: (16, 1), -30: (-16, -16, 1, 1), -31: (-16, -16, 1), -32: (-16, -16), -63: (-64, 1), -65: (-64, -1),
              63: (64, -1), 65: (64, 1), -62: (-64, 1, 1), -95: (-64, -16, -16, 1)}
     ent = sorted([(v != 1, v, 8 * so, nm) for so, lst in enumerate(layer) for (nm, v0) in lst for v in parts.get(v0, (v0,))])
-    vals = sorted(set(e[1] for e in ent) - {1}) + [-256, -4096]
+    vals = sorted(set(e[1] for e in ent) - {1}) + [-2048, 0.5, -0.5]
     sid = lambda v: o("ID") if v == 1 else o("SID", 128 * vals.index(v), 128 * vals.index(v) + 128)
     for v in vals:
         lin(sid(v), o("ID"), float(v))
@@ -327,8 +316,17 @@ def build():
     for k, (_, v, c, nm) in enumerate(ent):
         mm(o("KY1", c, c + 8), sid(v), var[nm], False, k == len(ent) - 1)
     lin(o("WM"), o("KY1", 0, 192))
+    for k, v in enumerate((-0.5, 0.5)):
+        mm(o("XB0", 128 * k, 128 * k + 128), o("ID"), o("SH0"), True, False)
+        mm(o("XB0", 128 * k, 128 * k + 128), sid(v), o("ID"), False, True)
+    lin(o("DM"), o("XB0", 0, 256))
+    cp(o("D3"), o("DM", 0, 128))
+    cp(o("D3", 15, 128, 16), o("DM", 0, 128, 16))
     for i in range(2 * NS):
-        fill(o("CT", 64 * i, 64 * i + 16), 0)
+        asel(o("CT", 240 * i, 240 * i + 160), o("F2"), [[0, 160]], 0, 0)
+    for k in range(3):
+        for h in range(2):
+            fill(o("S%d" % h, 128 + 256 * k, 384 + 256 * k), 1)
 
     ctx[3] = "variables"
     for k in range(8):
@@ -345,35 +343,32 @@ def build():
     fill(o("BW", 4096, 4624), 0)
     fill(o("CW", 4096, 4608), 0)
     fill(o("GW"), 0)
-    for (a, b, ps) in (("BOi", "BOu", "KY0"), ("GSi", "GSu", "KY1")):
+    for (a, b, ps, n) in (("BOi", "BOu", "KY0", 288), ("GSi", "GSu", "KY1", 256)):
         ctx[3] = b
-        lin(o("X2"), o(a), 1.0, -2048.0)
-        add("V", "tr", (o("X3"), o("X2")), [o("X2")], [o("X3")], 128 * CYC)
-        mm(o(ps, 0, 256), o("IDh"), o("ZF"), True, False)
+        lin(o("X2", 0, n), o(a), 1.0, -2048.0)
+        add("V", "tr", (o("X3", 0, n), o("X2", 0, n)), [o("X2", 0, n)], [o("X3", 0, n)], n / 2 * CYC)
+        mm(o(ps, 0, nel(o(b))), o("IDh"), o("ZF", 0, nel(o(b))), True, False)
         for m0 in range(2):
             for g0 in range(2):
                 c = 160 * m0 + 16 + 16 * (m0 - g0)
-                for m in range(8):
-                    mm(o(ps, 2 * m + m0, 256, 16), o("ZP", c, c + 128), o("X3", 32 * m + 16 * g0, 32 * m + 16 * g0 + 16), False,
-                       m0 + g0 + m == 9)
-        ts(o(b), o(ps, 0, 256), 2048.0, None, AL.add)
+                for m in range(8 if m0 else n // 32):
+                    mm(o(ps, 2 * m + m0, 256, 16) if m < 8 else o(ps, 256, 272), o("ZP", c, c + 128),
+                       o("X3", 32 * m + 16 * g0, 32 * m + 16 * g0 + 16), False, m0 + g0 + m == 9 and m0 == 1)
+        shift(ON[b], o(b), o(ps, 0, nel(o(b))), 2048.0)
 
-    def to_b(t, h, body):
+    def to_b(t, h, first, fac, x, top=None):
         H = str(h)
-        n, y0, ps, win = (8, 0, "KY" + H, o("VB" + H)) if body else (16, 64, "MP" + H, o("VC" + H))
-        if Y2A and not body:
-            act(o("Y" + H, y0, y0 + 8 * n), win, AF.Identity, 1.0, -2048.0, ind=o("YO", y0 // 16, (y0 + 8 * n) // 16))
-        else:
-            ts(o("Y" + H, y0, y0 + 8 * n), win, -2048.0, None, AL.add, None, o("YO", y0 // 16, (y0 + 8 * n) // 16))
+        y, ps, f = ("Y" + H, "KY" + H, "OF" + H) if first else ("Z" + H, "MP" + H, "OM" + H)
+        scan(o(y), fac, x, 0.0, AL.mult, AL.add)
         for gq in range(8):
-            x = o(ps, 144, 144 + n, p0=32 * (gq // 2), p1=32 * (gq // 2) + 32)
-            mm(x, o("FW", 16 - 16 * (gq % 2), 48 - 16 * (gq % 2)), o("Y" + H, y0 + n * gq, y0 + n * gq + n), gq % 2 == 0, gq % 2 == 1)
-        b = 24 * (t % 2) + y0 // 8
-        if O2A and not body:
-            lin(o("OF" + H, b, b + n), o(ps, 144, 144 + n), 1.0, 2048.0)
+            mm(o(ps, 160, 168, p0=32 * (gq // 2), p1=32 * (gq // 2) + 32), o("FW", 16 - 16 * (gq % 2), 48 - 16 * (gq % 2)),
+               o(y, 10 * gq + 2, 10 * gq + 10), gq % 2 == 0, gq % 2 == 1)
+        f = o(f, 8 * (t % 2), 8 * (t % 2) + 8)
+        if top:
+            ts(f, o(ps, 160, 168), 2048.0, top, AL.add, AL.min)
         else:
-            ts(o("OF" + H, b, b + n), o(ps, 144, 144 + n), 2048.0, None, AL.add)
-        return [o("OF" + H, b + k, b + k + 8) for k in range(0, n, 8)]
+            shift("V" if first else ON["OM"], f, o(ps, 160, 168), 2048.0)
+        return f
 
     def message(t, h, off):
         H = str(h)
@@ -382,37 +377,46 @@ def build():
         act(m, o("MW", 0, top), AF.Abs, ind=off)
         mm(o("MP" + H, 0, 128), o("ID"), m)
 
-    def mask(out, x):
-        act(out, x, AF.Sigmoid, -256.0, cBias)
+    def tile(t, h, **k):
+        return o("S%d" % h, 128 * t, 128 * t + 128, **k)
+
+    def mask(out, x, b=cBias):
+        act(out, x, AF.Sign, -1.0, b)
 
     def offers(t, h, m):
         H = str(h)
         XB = "XB" + H
         mm(o(XB, 128, 256), o("D3"), o("Q" + H))
         tt(o("ZX" + H), m, o(XB, 128, 256), AL.mult)
-        x = o(XB, 384, 400)
-        mm(x, o("S" + H), o("WO", 16 * t, 16 * t + 16), True, False)
+        x = o(XB, 384, 464)
+        mm(x, o("ONE", 0, 128, p1=1), o("WO", 80 * t, 80 * t + 80, p1=1), True, False)
         mm(x, o("Q" + H), o("WQ"), False, False)
         mm(x, o("ZX" + H), o("WZ"), False, True)
 
     def update(t, h):
         H = str(h)
         XA, XB = "XA" + H, "XB" + H
-        s, q = o("S" + H), o("Q" + H)
+        s, q = tile(t - 1, h), o("Q" + H)
         i = 2 * (t - 1) + h
-        mm(o(XB, 0, 128), o("DM"), q, True, False)
+        c = 128 if t == NS else 0
+        mm(o(XB, 0, 128), o("DM", 0, 128), q, True, False)
         mm(o(XB, 0, 128), o("E15", p1=1), o("LC", 128 * h, 128 * h + 128, p1=1), False, True)
-        mm(o(XA, 0, 128, p0=96, p1=120), o("CT", 64 * i + 1, 64 * i + 48, 2), o("ID"))
-        (cp if R0V else lin)(o("S" + H, p0=96, p1=120), o(XA, 0, 128, p0=96, p1=120))
-        mm(o(XA, 0, 128, p1=96), o("WM", 0, 96), s)
+        mm(o(XB, 256, 384), o("E15", p1=1), o("LC", 128 * h, 128 * h + 128, p1=1), True, False)
+        mm(o(XB, 256, 384), o("LN", p1=1), o("CB", c, c + 128, p1=1), False, False)
+        mm(o(XB, 256, 384), o("DM", 128, 256), q, False, t == NS)
+        mm(o(XA, 0, 128, p0=96, p1=120), o("CT", 240 * i + 1, 240 * i + 240, 10), o("ID"))
+        (cp if ON["S"] == "V" else lin)(tile(t - 1, h, p0=96, p1=120), o(XA, 0, 128, p0=96, p1=120))
         mm(o(XA, 128, 256), o("BC", 0, 128), s)
         mm(o(XA, 256, 384), o("BC", 128, 256), s)
-        act(o("S" + H, p1=96), o(XA, 0, 128, p1=96), AF.Relu)
-        mask(o("M" + H), o(XA, 128, 384))
+        mm(o(XA, 0, 128, p1=96), o("WM", 0, 96), s)
         m1, m2 = o("M" + H, 0, 128), o("M" + H, 128, 256)
+        mask(m1, o(XA, 128, 256))
+        if t < NS:
+            mask(m2, o(XA, 256, 384), cB2)
+        act(tile(t, h, p1=96), o(XA, 0, 128, p1=96), AF.Relu)
+        s = tile(t, h)
         if t == NS:
-            mm(o(XB, 256, 384), o("IDh"), q, True, False)
-            mm(o(XB, 256, 384), o("LN", p1=1), o("CB", p1=1), False, True)
+            ts(m2, o(XA, 256, 384), cB2, None, AL.is_lt)
             tt(o("T1" + H), m1, o(XB, 0, 128), AL.mult)
             mm(o(XA, 384, 512, p1=24), o("XV", 0, 24), s)
             lin(o("YP", 128 * h, 128 * h + 128, p1=24), o(XA, 384, 512, p1=24))
@@ -424,61 +428,52 @@ def build():
             tt(y, o("QF" + H), m2, AL.mult)
             dma("S", ("ext", "yq", (128 * h, 128 * h + 128)), y, [y], [], 65536)
             return
-        mm(o(XB, 256, 384), o("IDh"), q, True, False)
-        mm(o(XB, 256, 384), sid(-256), m2, False, True)
+        mm(o(XB, 256, 384), sid(-128), m2, False, True)
         tt(o("T1" + H), m1, o(XB, 0, 128), AL.mult)
         tt(q, o("T1" + H), o(XB, 256, 384), AL.add)
         if t < NS - 1:
             mm(o(XA, 384, 512), o("BC", 256, 384), s)
-            if M3V:
-                ts(o("M3" + H), o(XA, 384, 512), cJ, None, AL.is_le)
-            else:
-                mask(o("M3" + H), o(XA, 384, 512))
+            mask(o("M3" + H), o(XA, 384, 512))
             offers(t, h, o("M3" + H))
 
     def start(h):
         H = str(h)
         ctx[3] = "start" + H
-        XA, XB, VC = "XA" + H, "XB" + H, "VC" + H
-        s, q = o("S" + H), o("Q" + H)
+        XA, XB = "XA" + H, "XB" + H
+        s, q = tile(0, h), o("Q" + H)
         hs = lambda b, **k: o(b, 128 * h, 128 * h + 128, **k)
         lin(s, one, n8(15))
-        ts(o("S" + H, p1=24), hs("STi", p1=24), cS1[:2] + (24,) + cS1[3:], None, AL.mult)
-        cp(o("S" + H, p0=32, p1=40), hs("STi", p0=32, p1=40))
-        if h == 0:
-            cp(o("S0f", p1=16), o("STi", p1=16))
-            for a in range(16):
-                mm(o("KY0", 0, 16), o("WS", 15 - a, 143 - a, p1=16), o("S0f", a, 256, 16, p1=16), a == 0, a == 15)
-            cp(o("SO"), o("KY0", 0, 16))
-        cp(o("CU" + H), o("CLs"), o("SO", 8 * h, 8 * h + 8))
+        ts(tile(0, h, p1=40), hs("STi", p1=40), cS1[:2] + (40,) + cS1[3:], None, AL.mult)
+        cp(o("CU" + H), o("CLs"), o("BOu", 256 + 8 * h, 264 + 8 * h))
         cp(o("CW", 4096 + 256 * h, 4352 + 256 * h, 2), o("CU" + H))
-        fill(o(VC, 0, 136), 2 ** 20)
-        fill(o(VC, 136, 168), 2048)
-        fill(o("VB" + H), 2048)
-        iota(o(VC, 0, 136, 17), [[0, 8]], 4096 + 256 * h, 2)
+        for x in (o("VB" + H), o("RS" + H, 143, 1488, 17)):
+            fill(x, 0)
+            fill(x[:5] + (10 * x[5],), -1)
+        lin(o("Y" + H, 1, 80, 10), o("ONE", 0, 8), cK, 2048.0 + 256 * h)
         mm(o(XA, 128, 256), o("BC", 0, 128), s)
         mm(o(XA, 256, 384), o("BC", 128, 256), s)
-        mask(o("M" + H), o(XA, 128, 384))
+        mask(o("M" + H, 0, 128), o(XA, 128, 256))
+        mask(o("M" + H, 128, 256), o(XA, 256, 384), cB2)
         mm(o(XB, 0, 128), o("LN", p1=1), hs("LC", p1=1), True, False)
-        mm(o(XB, 0, 128), sid(-4096), o("M" + H, 128, 256), False, True)
+        mm(o(XB, 0, 128), o("LN", p1=1), o("CB", 256, 384, p1=1), False, False)
+        mm(o(XB, 0, 128), sid(-2048), o("M" + H, 128, 256), False, True)
         ts(o("CH" + H), hs("Qi"), -384.0, None, AL.add)
         tt(q, o("CH" + H), o(XB, 0, 128), AL.max)
         offers(0, h, o("M" + H, 0, 128))
-        scan(o(VC, 144, 160), o("AL01"), o(XB, 384, 400), 0.0, AL.mult, AL.add)
-        ts(o(VC, 144, 160), o(VC, 144, 160), 2047.0, None, AL.min)
-        message(0, h, to_b(1, h, False)[1])
+        message(0, h, to_b(1, h, False, o("F2", 0, 80), o(XB, 384, 464), 2047.0))
         mm(o(XA, 0, 128, p1=96), o("WM", 96, 192), s)
-        act(o("S" + H, p1=96), o(XA, 0, 128, p1=96), AF.Relu)
+        act(tile(0, h, p1=96), o(XA, 0, 128, p1=96), AF.Relu)
         mm(o(XA, 384, 512), o("BC", 256, 384), s)
         mask(o("M3" + H), o(XA, 384, 512))
         offers(0, h, o("M3" + H))
 
     def tables():
-        for r in range(8):
-            if r < CA:
-                act(o("CW", 512 * r, 512 * r + 512), o("CLs"), AF.Copy, ind=o("GSu", 32 * r, 32 * r + 32))
+        for (a, b) in zip(CC, CC[1:]):
+            if b <= CA:
+                act(o("CW", 16 * a, 16 * b), o("CLs"), AF.Copy, ind=o("GSu", a, b))
             else:
-                cp(o("CW", 512 * r, 512 * r + 512), o("CLs"), o("GSu", 32 * r, 32 * r + 32))
+                cp(o("CW", 16 * a, 16 * b), o("CLs"), o("GSu", a, b))
+        for r in range(8):
             x, f = o("BW", 512 * r, 512 * r + 512), o("BOu", 32 * r, 32 * r + 32)
             if r < BV:
                 ts(x, o("PW"), -1.0, None, AL.mult, None, f)
@@ -491,72 +486,69 @@ def build():
     def wide(t, h):
         H = str(h)
         P, EQ, KY = "P" + H, "EQ" + H, "KY" + H
-        if CHA:
-            lin(o("CH" + H), o("CU" + H), 1.0, -2048.0)
-        else:
-            ts(o("CH" + H), o("CU" + H), -2048.0, None, AL.add)
+        shift(ON["CH"], o("CH" + H), o("CU" + H), -2048.0)
         mm(o(KY, 0, 136), o("CH" + H), o("IX"), True, False)
-        pv = PV if t >= PT else 0
+        mm(o(KY, 16, 136, 17), o("IDh"), o("Y" + H, 1, 80, 10), False, False)
+        pv = PV[t]
         for a in range(128 - pv, 128, PS):
-            cp(o(P, 16 * a, 16 * (a + PS)), o("PW"), o("CU" + H, a, a + PS))
-        for (a, b) in GP:
-            b = min(b, 128 - pv)
+            cp(o(P, 16 * a, 16 * min(a + PS, 128)), o("PW"), o("CU" + H, a, min(a + PS, 128)))
+        cut = [2 * int((128 - pv) * k / 2) for k in GP]
+        for (a, b) in zip(cut, cut[1:]):
             chain["A"] = [act(o(P, 16 * a, 16 * b), o("PW"), AF.Copy, ind=o("CU" + H, a, b), after=chain["A"])]
         for (a, b) in PIECES:
             for k in range(16):
-                m = o("MP" + H, a, b)
-                if k < NM and a == 0:
-                    m = o("MS" + H, 128 * (t % 2) + a, 128 * (t % 2) + b)
-                chain["V"] = [tt(o(EQ, 128 * k + a, 128 * k + b), o(P, 16 * a + k, 16 * b, 16), m, AL.is_equal, after=chain["V"])]
+                chain["V"] = [tt(o(EQ, 128 * k + a, 128 * k + b), o(P, 16 * a + k, 16 * b, 16), o("MP" + H, a, b), AL.not_equal, after=chain["V"])]
         for k in range(16):
             mm(o(KY, k, 136, 17), o(P, k, 2048, 16), o("INp"), False, False)
-        mm(o(KY, 0, 136), o("S" + H), o("PN"), False, False)
+        mm(o(KY, 0, 136), tile(t, h), o("PN"), False, False)
         for k in range(16):
             mm(o(KY, k, 136, 17), o(EQ, 128 * k, 128 * k + 128), o("INe"), False, k == 15)
 
     def choose(t, h):
         H = str(h)
         i = 2 * t + h
-        VC = "VC" + H
-        scan(o("RS" + H, 0, 136), o(VC, 0, 136), o("KY" + H, 0, 136), BIG, AL.min, AL.max)
-        rs, z = o("RS" + H, 15, 136, 17), o("RS" + H, 136, 144)
-        nf, u = o("CT", 64 * i + 1, 64 * i + 16, 2), o("CT", 64 * i + 33, 64 * i + 48, 2)
+        last = t == NS - 1
+        scan(o("RS" + H, 0, 1360, 10), o("RD"), o("KY" + H, 0, 136), 0.0, AL.add, AL.max)
+        rs = o("RS" + H, 160, 1360, 170)
+        rv = o("RS" + H, 143, 1488, 17)
+        nf, u = o("CT", 240 * i + 1, 240 * i + 80, 10), o("CT", 240 * i + 81, 240 * i + 160, 10)
+        land, x, ub = o("CT", 240 * i + 160, 240 * i + 240), o("CT", 240 * i, 240 * i + 80), o("CT", 240 * i + 80, 240 * i + 160)
         ts(u, rs, MAG, MAG, AL.add, AL.subtract)
-        ts(z, rs, 4608.0, None, AL.max)
+        if last:
+            ts(o("VB" + H, 1, 80, 10), rs, 2560.0, None, AL.max)
+        fb = to_b(t, h, True, ub, o("VB" + H) if last else rv)
         ts(nf, rs, 8192.0, None, AL.is_lt)
-        tt(o("VB" + H, 136, 144), z, u, AL.subtract)
-        fb = to_b(t, h, True)
-        land, x = o("CT", 64 * i + 16, 64 * i + 32), o("CT", 64 * i, 64 * i + 16)
+        f = to_b(t, h, False, ub, rv) if last else to_b(t, h, False, x, o("XB" + H, 384, 464))
         j = add("G", "rdma", (land, x, t, "af%d" % i), [x], [], 500.0, 0.0)
         add("X", "arr", ("af%d" % i, j), [], [land], 0.0, 2600.0, after=[j])
-        tt(o(VC, 0, 136, 17), rs, u, AL.subtract)
-        if t < NS - 1:
-            scan(o(VC, 144, 160), x, o("XB" + H, 384, 400), 0.0, AL.mult, AL.add)
-        f = to_b(t, h, False)
-        if t < NS - 1:
-            if CUA:
-                act(o("CU" + H), o("CW"), AF.Copy, ind=f[0])
-            else:
-                cp(o("CU" + H), o("CW"), f[0])
-        if i == 2 * NS - 3:
-            dma("S", ("rows", "CW", 0, 4096), ("ext", "gs", None), [], [o("CW", 0, 4096)], 131072)
-            cp(o("CW", 4096, 4608, 2), o("GW"))
         snd = o("SND", 128 * i, 128 * i + 128)
-        tt(snd, o("BW"), o("MS" + H, 128 * (t % 2), 128 * (t % 2) + 128), AL.min, fb[0])
+        tt(snd, o("BW"), o("MS" + H, 128 * (t % 2), 128 * (t % 2) + 128), AL.min, fb)
         land = o("MW", 2048 + 128 * i, 2048 + 128 * i + 128)
         j = add("G", "rdma", (land, snd, t, "ad%d" % i), [snd], [], 500.0, 0.0)
         add("X", "arr", ("ad%d" % i, j), [], [land], 0.0, 3200.0, after=[j])
-        if t < NS - 1:
-            message(t + 1, h, f[1])
-        else:
+        if not last:
+            act(o("CU" + H), o("CW"), AF.Copy, ind=fb)
+            message(t + 1, h, f)
+        if i == 2 * NS - 3:
+            dma("S", ("rows", "CW", 0, 4096), ("ext", "gs", None), [], [o("CW", 0, 4096)], 131072)
+            cp(o("CW", 4096, 4608, 2), o("GW"))
+        if last:
             y = o("YS", 128 * h, 128 * h + 128)
-            cp(y, o("CW"), f[0])
+            cp(y, o("CW"), f)
             dma("S", ("ext", "ys", (128 * h, 128 * h + 128)), ("rows", "YS", 128 * h, 128 * h + 128), [y], [], 4096)
-        if t == NS - 1 or h == 1:
-            a = i if t == NS - 1 else i - 1
-            x = o("MO", 128 * a, 128 * i + 128)
-            act(x, o("MW", 2048 + 128 * a, 2048 + 128 * i + 128), AF.Abs)
-            dma("S", ("ext", "mn", (128 * a, 128 * i + 128)), x, [x], [], 32768 * (i - a + 1))
+            x = o("MO", 128 * i, 128 * i + 128)
+            act(x, land, AF.Abs)
+            dma("S", ("ext", "mn", (128 * i, 128 * i + 128)), x, [x], [], 32768)
+
+    def arrived():
+        for t in range(NS - 1):
+            act(o("MO", 256 * t, 256 * t + 256), o("MW", 2048 + 256 * t, 2304 + 256 * t), AF.Abs)
+        for t in range(NS - 1):
+            x, y = o("MO", 256 * t, 256 * t + 256), o(("MP0", "KY0")[t % 2], 256, 512)
+            for h in range(2):
+                mm(o(y[0], 256 + 128 * h, 384 + 128 * h), o("BS"), tile(t, h))
+            tt(x, x, y, AL.min)
+            dma("S", ("ext", "mn", (256 * t, 256 * t + 256)), x, [x], [], 65536)
 
     start(0)
     start(1)
@@ -566,31 +558,35 @@ def build():
             ctx[0], ctx[1], ctx[2] = ("step" if t < NS - 1 else "last%d" % h), {}, (t, h)
             wide(t, h)
             choose(t, h)
+            if t == NS - 1 and h == 0:
+                arrived()
             update(t + 1, h)
     prune(ops)
     return ops
 
 
-CASES = ((0.83, 1.1, 160.0, 0.7, 71.8), (0.85, 1.45, 190.0, 0.8, 79.0), (0.9, 2.0, 170.0, 0.7, 86.4), (1.2, 1.1, 190.0, 0.7, 94.9),
-         (1.2, 2.0, 150.0, 0.75, 108.4), (0.9, 1.3, 160.0, 1.2, 85.0))
-MID = (0.87, 1.45, 180.0, 0.85)
-PERIOD, FIRST, BUS = 8200.0, 13000.0, 250.0
+CASES = ((0.83, 1.1, 160.0, 0.35, 0.7, 62.0), (0.87, 1.35, 180.0, 0.45, 0.8, 67.0), (0.9, 2.0, 170.0, 0.5, 1.0, 80.0), (1.2, 1.1, 190.0, 0.5, 1.0, 87.0),
+         (1.2, 2.0, 170.0, 0.5, 1.0, 102.0), (0.9, 1.3, 200.0, 0.8, 0.8, 74.0))
+MID = (0.87, 1.4, 180.0, 0.5, 0.85)
+PERIOD, FIRST, BUS = 7500.0, 13300.0, 250.0
 HAND = True
-SEED, HEAT, AHEAD = 1, 2.0, 8000.0
+SEED, HEAT, AHEAD = 1, 2.0, 2000.0
 SHIFT = {}
-DUE = {("V", "CH"): -2100, ("P", "KY", 1): -1900, ("A", "P", 1): -3750, ("A", "P", 2): -3090, ("A", "P", 3): -2430, ("A", "P", 4): -1200,
-       ("V", "P", 1): -700, ("V", "P", 2): -700, ("V", "RS", 1): 2150, ("V", "CT", 1): 2440, ("V", "RS", 2): 2490, ("V", "CT", 2): 2545,
-       ("G", "CT"): 2750, ("V", "VB"): 2730, ("V", "VC", 1): 2780, ("V", "VC", 2): 2840, ("V", "Y", 1): 2960, ("V", "Y", 2): 3090,
-       ("V", "OF", 1): 3610, ("V", "OF", 2): 3790, ("V", "SND"): 3850, ("G", "MW"): 4230, ("A", "CU"): 4100, ("P", "MP"): 3470,
-       ("P", "XB", 1): 4600, ("P", "XB", 2): 4650, ("P", "XB", 3): 4700, ("P", "XA", 1): 5450, ("V", "S"): 5900, ("P", "XA", 2): 6180,
-       ("P", "XA", 3): 6200, ("P", "XA", 4): 6220, ("A", "M"): 6680, ("A", "S"): 6890, ("P", "XB", 4): 7010, ("P", "XA", 5): 7080,
-       ("A", "MS"): 7360, ("V", "T1"): 7400, ("A", "M3"): 7580, ("V", "M3"): 7420, ("A", "MO"): 7690, ("P", "MP", 9): 7700, ("V", "Q"): 7770,
-       ("P", "XB", 5): 8050, ("V", "ZX"): 9900, ("P", "XB"): 10180, ("S", "ext"): 9000, ("X", "af"): 2800, ("X", "ad"): 4300}
-EARLY = {"variables": 500, "BOu": 3000, "start0": 4000, "GSu": 5000, "start1": 6000, "CT": 9000, "CW": 15500, "BW": 11500, "GW": 12000,
-         "MS1": 13200, "CU0": 100, "CU1": 200}
+EQ0 = 0.0
+DUE = {("V", "CH"): -1800, ("A", "CH"): -1800, ("P", "KY", 1): -1500, ("P", "KY", 2): -1400, ("A", "P", 1): -3600, ("A", "P", 2): -2600, ("A", "P", 3): -800,
+       ("V", "P", 1): -1480, ("V", "P"): -800, ("V", "RS", 1): 2180, ("V", "CT", 1): 2490, ("V", "VB"): 2520, ("V", "CT", 2): 2550,
+       ("G", "CT"): 2800, ("V", "Y"): 2730, ("V", "Z"): 3150, ("P", "MP", 1): 3450,
+       ("V", "OF"): 3310, ("V", "OM"): 6400, ("A", "OM"): 4700, ("V", "SND"): 3550, ("G", "MW"): 3940, ("A", "CU"): 3550, ("P", "MP"): 7000,
+       ("P", "XB", 1): 4500, ("P", "XB", 2): 4700, ("P", "XB", 3): 4750, ("P", "XB", 4): 4900, ("P", "XB", 5): 5000, ("P", "XA", 1): 5100,
+       ("V", "S"): 5600, ("A", "S", 1): 6450, ("A", "S", 2): 6450,
+       ("P", "XA", 2): 5880, ("P", "XA", 3): 5900, ("P", "XA", 4): 5920, ("A", "M"): 6220, ("P", "XB", 6): 6630,
+       ("P", "XA", 5): 7200, ("A", "MS"): 6600, ("V", "T1"): 6850, ("A", "M3"): 7600, ("A", "MO"): 4000, ("P", "MP", 9): 7000, ("V", "Q"): 7200,
+       ("P", "XB", 7): 7500, ("V", "ZX"): 9500, ("P", "XB"): 9800, ("S", "ext"): 9000, ("X", "af"): 2900, ("X", "ad"): 4000}
+EARLY = {"variables": 500, "BOu": 3000, "start0": 4000, "GSu": 7000, "start1": 8000, "CW": 10500, "BW": 7500, "CU0": 100, "CU1": 200}
+GAP = {("V", "CW"): 800.0, ("A", "CW"): 900.0}
 
 
-def graph(ops, c, gt, l, f):
+def graph(ops, c, gt, l, f, pe=1.0, BUS=BUS):
     cost = []
     lat = []
     bus = 0.0
@@ -600,7 +596,7 @@ def graph(ops, c, gt, l, f):
         if p["eng"] in "VAP" and p["kind"] != "dma":
             if k is not None and p["args"][k] is not None:
                 v += nel(p["args"][0]) * (gt - GTH) * CYC
-            v *= c / CYC
+            v *= c / CYC * (pe if p["eng"] == "P" else 1.0)
         cost.append(v)
         v = p["lat"] * (f if p["eng"] == "X" else 1.0)
         if p["kind"] == "dma":
@@ -682,10 +678,10 @@ def once(eng, g, succ, due, slack):
     return order
 
 
-def plan(ops, climbs=1000, tries=0, polish=(9500, 3000)):
+def plan(ops, climbs=500, tries=0, polish=(6000, 9000)):
     n = len(ops)
     eng = [p["eng"] for p in ops]
-    sets = [(graph(ops, c, gt, l, f), w) for (c, gt, l, f, w) in CASES]
+    sets = [(graph(ops, *c[:-1]), c[-1]) for c in CASES]
     mid = graph(ops, *MID)
     succ = [[] for _ in range(n)]
     for i, p in enumerate(ops):
@@ -702,15 +698,17 @@ def plan(ops, climbs=1000, tries=0, polish=(9500, 3000)):
             if p["kind"] == "dma" and nm != "rows":
                 base[i] = -20000.0
             elif nm in EARLY or p["part"] in EARLY:
-                base[i] = EARLY.get(nm, EARLY.get(p["part"])) + 0.1 * i
+                base[i] = EARLY.get(nm, EARLY.get(p["part"])) + 0.1 * i + GAP.get((e, nm), 0.0) * k
+                if (e, nm) in GAP:
+                    cls[-1] = names.setdefault((p["part"], e, nm, k), len(names))
             continue
         t, h = p["at"]
         if (e, nm) == ("V", "EQ"):
-            v, k = 1700.0 * k / (16 * len(PIECES)), (k - 1) // 4
-        elif (e, nm) == ("P", "KY") and k > 1:
-            v, k = (-400.0 + 42 * k, 2) if k < 18 else (450.0, 3) if k == 18 else (53.0 * k + 80.0, 4 + (k - 19) // 4) if k < 35 else (3220.0 + k, 9)
+            v, k = EQ0 + 1780.0 * (k - 1) / (16 * len(PIECES)), (k - 1) // 4
+        elif (e, nm) == ("P", "KY") and 2 < k < 44:
+            v, k = (42.0 * k, 3) if k < 19 else (800.0, 4) if k == 19 else (75.0 * k - 675.0, 5 + (k - 20) // 4) if k < 36 else (2950.0 + k, 9)
         elif (e, nm) == ("P", "MP") and k < 9:
-            v, k = DUE[e, nm] + k, 1
+            v, k = DUE[e, nm, 1] + k, 1
         else:
             v = DUE.get((e, nm, k), DUE.get((e, nm), 7000.0)) + k
         base[i] = FIRST + PERIOD * (t + 0.5 * h) + v
@@ -756,7 +754,7 @@ def plan(ops, climbs=1000, tries=0, polish=(9500, 3000)):
     beg = starts(eng, mid, best[1])
     per = [i for i in range(n) if ops[i]["at"] == (2, 0) and ops[i]["cls"][1:] == ("V", "RS", 1)][0]
     nxt = [i for i in range(n) if ops[i]["at"] == (2, 1) and ops[i]["cls"][1:] == ("V", "RS", 1)][0]
-    half = beg[nxt] - beg[per]
+    half = PERIOD / 2 if HAND else beg[nxt] - beg[per]
     names = {}
     cls = np.array([names.setdefault(p["cls"] if p["at"] and 1 <= p["at"][0] < NS - 1 else i, len(names)) for i, p in enumerate(ops)])
     ref = {p["cls"]: beg[i] for i, p in enumerate(ops) if p["at"] == (2, 0)}
@@ -967,7 +965,7 @@ def rank_program(g, core, T, topo):
             else:
                 r = q.iota(ap(a[0]), a[1], a[2], a[3], allow_small_or_imprecise_dtypes=True)
         elif kind == "asel":
-            r = q.affine_select(ap(a[0]), ap(a[1]), a[2], AL.is_equal, 0.0, a[3], a[4])
+            r = q.affine_select(ap(a[0]), ap(a[1]), a[2], a[5], a[6], a[3], a[4])
         elif kind == "dma":
             r = q.dma_start(ap(a[0]), ap(a[1]))
         elif kind == "rdma":

@@ -7,29 +7,33 @@ AL = AluOpType
 AF = ActivationFunctionType
 NS = 6
 PIECES = ((0, 128),)
-GP = (0, 0.45, 0.85, 1)
+GP = (0, 1)
 CC = (0, 32, 64, 96, 128, 160, 192, 208, 224, 240, 256)
 CA = 128
 LV = ("SID", "BC", "BT", "S0", "S1", "ZP", "SH0", "IDh", "IX", "WS")
-PS = 10
+PS = 14
 ON = {"CH": "V", "OM": "V", "S": "V", "BOu": "V", "GSu": "V"}
-PV = (30, 20, 20, 20, 20, 20)
+PV = (28, 22, 22, 22, 22, 14)
 BV = 4
 FIXV = (5, 7)
+EV = ()
+NM = 0
+TWICE = True
+OPEN = 1000.0
+LOADS = (("Qi", "q0"), ("GSi", "gs"), ("CLs", "cl"))
 HH = float(2 ** 60)
-BIG = 2 ** 20
-MAG = 1.5 * 2.0 ** 37
+BIG = 2 ** 21
 F32, BF, F16, I32, U16 = "float32", "bfloat16", "float16", "int32", "uint16"
 BYTES = {F32: 4, BF: 2, F16: 2, I32: 4, U16: 2}
 
 SCRATCH = {}
 for _d, _l in (
-        (BF, (("PW", 4096), ("BW", 4624), ("MW", 3584), ("SND", 1536), ("MO", 1536), ("CT", 2880), ("ONE", 160), ("ZB", 160), ("ZER", 192),
-              ("IXb", 136), ("SID", 1280), ("SH0", 128), ("INe", 8), ("INp", 8), ("F2", 160), ("FT", 160), ("G8", 128), ("RD", 136),
+        (BF, (("PW", 4096), ("BW", 4624), ("MW", 3584), ("SND", 1536), ("MO", 1536), ("CT", 2000), ("ONE", 384), ("ZB", 160), ("ZER", 192),
+              ("IXb", 136), ("SID", 1280), ("SH0", 128), ("INe", 8), ("INp", 8), ("F2", 80), ("FT", 80), ("G8", 128), ("RD", 136),
               ("BC", 384), ("BS", 128), ("PN", 136), ("XV", 40), ("WM", 192), ("WO", 400), ("IOG", 128), ("IOH", 136), ("IOK", 136))),
-        (I32, (("CW", 4608), ("CLs", 2048), ("GW", 256), ("BOi", 288), ("GSi", 256), ("Qi", 256), ("STi", 256), ("PI", 16))),
+        (I32, (("CW", 4608), ("CLs", 2048), ("BOi", 288), ("GSi", 256), ("Qi", 256), ("STi", 256), ("PI", 16))),
         (U16, (("BOu", 272), ("GSu", 256))),
-        (F16, (("IDh", 128), ("X2", 288), ("X3", 288), ("ZP", 320), ("ZF", 272), ("IX", 136), ("DM", 256), ("D3", 128), ("E15", 128),
+        (F16, (("IDh", 128), ("X2", 288), ("X3", 288), ("ZP", 320), ("IX", 136), ("DM", 256), ("D3", 128), ("E15", 128),
                ("LN", 128), ("CB", 384), ("LC", 256), ("FW", 48), ("WQ", 80))),
         (F32, (("CC", 40), ("IO16", 16), ("LP", 256), ("IN8", 16), ("IN16", 8), ("D8", 8), ("WZ", 80),
                ("YQ", 256), ("YS", 256), ("YP", 256)))):
@@ -37,12 +41,14 @@ for _d, _l in (
         SCRATCH[_n] = ("sbuf", [128, _c], _d)
 for _h in range(2):
     for _n, _c, _d in (("P", 2048, BF), ("EQ", 2048, BF), ("CU", 128, U16), ("CH", 128, F16), ("MS", 256, BF), ("RS", 1488, F32),
-                       ("VB", 80, F32), ("Y", 80, F16), ("Z", 80, F16), ("OF", 16, U16), ("OM", 16, U16), ("S", 896, BF),
+                       ("RU", 1488, BF), ("VB", 80, F32), ("Y", 80, F16), ("Z", 80, F16), ("OF", 16, U16), ("OM", 16, U16), ("S", 896, BF),
                        ("Q", 128, F16), ("M", 256, BF),
                        ("M3", 128, BF), ("T1", 128, F32), ("ZX", 128, F32), ("QF", 128, F32)):
         SCRATCH["%s%d" % (_n, _h)] = ("sbuf", [128, _c], _d)
-    for _n in ("MP", "KY", "XA", "XB"):
+    for _n in ("MP", "KY", "XB"):
         SCRATCH["%s%d" % (_n, _h)] = ("psum", [128, 512], F32)
+SCRATCH["XA"] = ("psum", [128, 512], F32)
+SCRATCH["TP"] = ("psum", [128, 256], BF)
 
 SEMAPHORES = ["cV", "cA", "cP", "cG", "loc"] + ["d%d" % i for i in range(48)] + ["ad%d" % i for i in range(12)] + ["af%d" % i for i in range(12)]
 
@@ -84,7 +90,7 @@ def build():
     hist = {}
     bank = {}
     lastpe = {}
-    ctx = ["", {}, None, "constants"]
+    ctx = ["", {}, None, "constants", False]
 
     def add(eng, kind, args, reads, writes, cost, lat=0.0, after=()):
         i = len(ops)
@@ -127,9 +133,10 @@ def build():
             deps[j] = deps.get(j, False)
         nm = args[0][0] if isinstance(args[0], tuple) else args[0][:2]
         key = (ctx[0], eng, nm[:-1] if nm[-1] in "01" and nm[:-1] + "1" in SCRATCH and nm[:-1] + "0" in SCRATCH and ctx[0] else nm)
-        ctx[1][key] = ctx[1].get(key, 0) + 1
+        ctx[1][key] = ctx[1].get(key, 0) + (0 if ctx[4] else 1)
         ops.append({"eng": eng, "kind": kind, "args": args, "deps": deps, "cost": cost, "lat": lat, "cls": key + (ctx[1][key],), "at": ctx[2],
-                    "part": ctx[3]})
+                    "part": ctx[3], "join": ctx[4]})
+        ctx[4] = False
         return i
 
     def aps(*xs):
@@ -170,9 +177,10 @@ def build():
             return ts(out, a, scale, bias, AL.mult, AL.add)
         return act(out, a, AF.Copy if bias == 0.0 else AF.Identity, scale, bias)
 
-    def mm(out, l, r, s0=True, s1=True):
+    def mm(out, l, r, s0=True, s1=True, join=False):
         same = ops[-1]["kind"] == "mm" and ops[-1]["args"][1] == l and ops[-1]["args"][0][0] == out[0]
         c = max(16 if same else min(64, nel(l)), nel(r)) * (1 if two(l) else 4)
+        ctx[4] = join
         return add("P", "mm", (out, l, r, s0, s1), [l, r], [out], c * PCYC)
 
     def iota(out, pat, base, cm):
@@ -198,30 +206,34 @@ def build():
             (o("STi", p0=8 * k, p1=8 * k + 8), nm) for k, nm in enumerate(("p0", "p0", "n0", "n0", "w0"))]:
         la = [dma("A", x, ("ext", nm, None), [], [x], 8192, la)]
     ld = []
-    for k in range(4):
-        x = o("PW", 1024 * k, 1024 * k + 1024)
-        ld = [dma("S", x, ("ext", "pt", (1024 * k, 1024 * k + 1024)), [], [x], 262144, ld)]
-    for (b, nm) in (("Qi", "q0"), ("GSi", "gs")):
-        ld = [dma("S", o(b), ("ext", nm, None), [], [o(b)], 131072, ld)]
-    ld = [dma("S", o("CLs"), ("ext", "cl", None), [], [o("CLs")], 1048576, ld)]
+    for (a, b) in ((0, 512), (512, 1024), (1024, 2048), (2048, 3072), (3072, 4096)):
+        ld = [dma("S", o("PW", a, b), ("ext", "pt", (a, b)), [], [o("PW", a, b)], 256 * (b - a), ld)]
+    for (b, nm) in LOADS:
+        ld = [dma("S", o(b), ("ext", nm, None), [], [o(b)], 512 * nel(o(b)), ld)]
     ld = [dma("S", o("MW", 0, 2048), ("ext", "m0", None), [], [o("MW", 0, 2048)], 524288, ld)]
 
     ms(o("ONE"), 1.0)
     one = o("ONE", 0, 128)
     iota(col("PI", 0), [[0, 1]], 0, 1)
-    asel(o("ZB"), o("ONE"), [[1, 160]], -16, -1)
+    for x, y in ((o("CW", 4096, 4352), ("ext", "q0", None)), (o("CW", 4352, 4608), ("ext", "q0", None)), (o("BW", 4096, 4608), ("ext", "pt", (0, 512)))):
+        ld = [dma("S", x, y, [], [x], 131072, ld)]
+    for k in range(4):
+        x, y = o("S%d" % (k % 2), 128 + 384 * (k // 2), 512 + 384 * (k // 2), p0=96), o("ONE", p0=96)
+        ld = [dma("S", x, y, [y], [x], 24576, ld)]
+    asel(o("ZB"), o("ONE", 0, 160), [[1, 160]], -16, -1)
     iota(o("IO16"), [[1, 16]], 0, 0)
     iota(o("IOG"), [[1, 8], [0, 16]], 0, 0)
     iota(o("IOH"), [[1, 8], [0, 17]], 0, 0)
-    iota(o("IOK"), [[0, 8], [-1, 17]], 16, 0)
+    iota(o("IOK"), [[0, 8], [-1, 17]], 81, 0)
     iota(o("LP", p1=1), [[1, 256]], 1664, 0)
     asel(o("IXb"), o("ONE", 0, 136), [[-16, 8], [-1, 17]], 0, 1)
     fill(o("RD"), 0)
     fill(o("RD", 0, 136, 17), -BIG)
-    asel(o("FT"), o("ONE"), [[0, 16], [-16, 10]], 16, 1, AL.is_ge, 2.0 ** 40)
-    asel(o("F2"), o("FT"), [[0, 16], [-16, 10]], 32, 1, AL.is_ge)
-    ms(o("F2", 0, 160, 10), 0.0)
-    ts(o("F2", 2, 160, 10), o("F2", 2, 160, 10), 2.0 ** -40, None, AL.mult)
+    asel(o("FT"), o("ONE", 0, 80), [[0, 8], [-16, 10]], 16, 1, AL.is_ge, 2.0 ** 40)
+    asel(o("F2"), o("FT"), [[0, 8], [-16, 10]], 32, 1, AL.is_ge)
+    ms(o("F2", 0, 80, 10), 0.0)
+    ts(o("F2", 2, 80, 10), o("F2", 2, 80, 10), 2.0 ** -40, None, AL.mult)
+    fill(o("CT", 0, 80), 0)
     for c, (s, op) in enumerate(((15, AL.bitwise_and), (4, AL.arith_shift_right), (3, AL.arith_shift_right), (7, AL.bitwise_and),
                                  (16, AL.bitwise_and), (8, AL.bitwise_and))):
         ts(col("PI", c + 1), col("PI", 0), s, None, op)
@@ -232,7 +244,6 @@ def build():
     lin(cJ16, cP32, -1.0 / 16, 1.0)
     lin(o("ZP", 0, 160), o("ZB"), cJ16)
     ts(o("ZP", 160, 320), o("ZB"), cP32, 1.0 / 16, AL.mult, AL.mult)
-    ms(o("ZF"), 0.0)
     lin(cBias, cJ, 1.0, 0.5)
     lin(cB2, cJ, -1.0, -0.5)
     lin(cK, cP, 2.0)
@@ -251,7 +262,7 @@ def build():
     lin(o("IX"), o("IXb"))
     ms(o("IX", 16, 136, 17), 0.0)
     lin(o("LC", p1=1), o("LP", p1=1))
-    lin(o("LN", p1=1), o("ONE", 0, 128, p1=1))
+    ms(o("LN", p1=1), 1.0)
     ts(cS1, cQ8, 0.0, None, AL.is_equal)
     ts(o("G8"), o("IOG"), cM8, None, AL.is_equal)
     ms(o("FW"), 0.0)
@@ -263,8 +274,8 @@ def build():
     red(vw, o("IN8", 7, 12))
     for k, v in enumerate((vp, vn, n8(4), vr, vw)):
         lin(o("XV", 8 * k, 8 * k + 8), o("D8"), v)
-    lin(c1, n8(12), 64.0, vp)
-    ts(c2a, n8(14), n8(12), vn, AL.subtract, AL.subtract)
+    lin(c1, n8(13), 64.0, vp)
+    ts(c2a, n8(14), n8(13), vn, AL.subtract, AL.subtract)
     ts(c3, n8(15), vp, vr, AL.add, AL.subtract)
     lin(c3b, n8(15), 15.0, vp)
     ts(cpn, vr, vw, -2.0 ** 23, AL.add, AL.mult)
@@ -292,11 +303,11 @@ def build():
     fill(o("WO", p1=1), 0)
     iota(o("WO", 1, 400, 10, p1=1), [[256, 5], [0, 8]], 384 - 2048, 0)
     var = {"p": o("XV", 0, 8), "n": o("XV", 8, 16), "w": o("XV", 16, 24), "r": o("XV", 24, 32), "a": o("XV", 32, 40),
-           "f": o("ID", 96, 104), "u": o("ID", 104, 112), "s": o("ID", 112, 120), "1": o("ID", 120, 128)}
+           "u": o("ID", 96, 104), "f": o("ID", 104, 112), "s": o("ID", 112, 120), "1": o("ID", 120, 128)}
     ell = [("w", 1), ("a", -16), ("f", -1), ("u", -2.0 ** -14), ("r", -128)]
     layer = ([("p", 1), ("f", 64), ("1", -64)], [("r", -1), ("a", -1), ("f", 64), ("1", -63)],
              [("n", 1), ("f", 1), ("s", -1)], [("n", 1), ("f", 1), ("s", -1), ("1", -16)],
-             ell + [("1", 17)], ell + [("1", -30)], ell + [("1", -31)],
+             ell + [("1", 82)], ell + [("1", 35)], ell + [("1", 34)],
              [("1", 1), ("n", -1), ("f", -65), ("s", 1)],
              [("p", 1), ("r", -1), ("n", -1), ("f", 63), ("s", 1), ("a", -64), ("1", -62)],
              [("a", 1), ("s", 1), ("1", -1)],
@@ -304,7 +315,7 @@ def build():
              [("p", 1), ("n", 1), ("f", 1), ("s", -1), ("1", -32)],
              [("p", 1)], [], [("n", 1)], [], [("w", 1)], [("w", 1), ("1", -31), ("1", -16)], [("w", 1), ("1", -32), ("1", -16)],
              [("p", 1), ("n", -1), ("1", 1)], [], [], [], [])
-    parts = {17: (16, 1), -30: (-16, -16, 1, 1), -31: (-16, -16, 1), -32: (-16, -16), -63: (-64, 1), -65: (-64, -1),
+    parts = {82: (64, 16, 1, 1), 35: (16, 16, 1, 1, 1), 34: (16, 16, 1, 1), -31: (-16, -16, 1), -32: (-16, -16), -63: (-64, 1), -65: (-64, -1),
              63: (64, -1), 65: (64, 1), -62: (-64, 1, 1), -95: (-64, -16, -16, 1)}
     ent = sorted([(v != 1, v, 8 * so, nm) for so, lst in enumerate(layer) for (nm, v0) in lst for v in parts.get(v0, (v0,))])
     vals = sorted(set(e[1] for e in ent) - {1}) + [-2048, 0.5, -0.5]
@@ -312,10 +323,10 @@ def build():
     for v in vals:
         lin(sid(v), o("ID"), float(v))
     ms(o("ZER"), 0.0)
-    mm(o("KY1", 0, 192), o("ID"), o("ZER"), True, False)
+    mm(o("XA", 0, 192), o("ID"), o("ZER"), True, False)
     for k, (_, v, c, nm) in enumerate(ent):
-        mm(o("KY1", c, c + 8), sid(v), var[nm], False, k == len(ent) - 1)
-    lin(o("WM"), o("KY1", 0, 192))
+        mm(o("XA", c, c + 8), sid(v), var[nm], False, k == len(ent) - 1, k and v == ent[k - 1][1])
+    lin(o("WM"), o("XA", 0, 192))
     for k, v in enumerate((-0.5, 0.5)):
         mm(o("XB0", 128 * k, 128 * k + 128), o("ID"), o("SH0"), True, False)
         mm(o("XB0", 128 * k, 128 * k + 128), sid(v), o("ID"), False, True)
@@ -323,37 +334,31 @@ def build():
     cp(o("D3"), o("DM", 0, 128))
     cp(o("D3", 15, 128, 16), o("DM", 0, 128, 16))
     for i in range(2 * NS):
-        asel(o("CT", 240 * i, 240 * i + 160), o("F2"), [[0, 160]], 0, 0)
-    for k in range(3):
-        for h in range(2):
-            fill(o("S%d" % h, 128 + 256 * k, 384 + 256 * k), 1)
+        asel(o("CT", 160 * i + 80, 160 * i + 160), o("F2"), [[0, 80]], 0, 0)
 
     ctx[3] = "variables"
     for k in range(8):
-        x, y, z = o("PW", 512 * k, 512 * k + 512), o(("MP0", "MP1", "XA1", "XB1")[k % 4]), o("EQ%d" % (k // 4), 512 * (k % 4), 512 * (k % 4) + 512)
+        x, y, z = o("PW", 512 * k, 512 * k + 512), o(("MP0", "MP1", "KY1", "XB1")[k % 4]), o("EQ%d" % (k // 4), 512 * (k % 4), 512 * (k % 4) + 512)
         if k in FIXV:
             act(y, x, AF.Relu, HH, -254.0 * HH)
             tt(x, x, y, AL.subtract)
         else:
             ts(z, x, 255.0, -HH, AL.is_equal, AL.mult)
             mm(y, o("ID"), x, True, False)
-            mm(y, o("ID"), z, False, True)
-            lin(x, y)
+            mm(y, o("ID"), z, False, True, True)
+            (cp if k in EV else lin)(x, y)
     ctx[3] = "fills"
-    fill(o("BW", 4096, 4624), 0)
-    fill(o("CW", 4096, 4608), 0)
-    fill(o("GW"), 0)
+    fill(o("BW", 4608, 4624), 0)
     for (a, b, ps, n) in (("BOi", "BOu", "KY0", 288), ("GSi", "GSu", "KY1", 256)):
         ctx[3] = b
         lin(o("X2", 0, n), o(a), 1.0, -2048.0)
         add("V", "tr", (o("X3", 0, n), o("X2", 0, n)), [o("X2", 0, n)], [o("X3", 0, n)], n / 2 * CYC)
-        mm(o(ps, 0, nel(o(b))), o("IDh"), o("ZF", 0, nel(o(b))), True, False)
         for m0 in range(2):
-            for g0 in range(2):
-                c = 160 * m0 + 16 + 16 * (m0 - g0)
-                for m in range(8 if m0 else n // 32):
+            for m in range(8 if m0 else n // 32):
+                for g0 in range(2):
+                    c = 160 * m0 + 16 + 16 * (m0 - g0)
                     mm(o(ps, 2 * m + m0, 256, 16) if m < 8 else o(ps, 256, 272), o("ZP", c, c + 128),
-                       o("X3", 32 * m + 16 * g0, 32 * m + 16 * g0 + 16), False, m0 + g0 + m == 9 and m0 == 1)
+                       o("X3", 32 * m + 16 * g0, 32 * m + 16 * g0 + 16), g0 == 0, g0 == 1, m % 4 + g0 > 0)
         shift(ON[b], o(b), o(ps, 0, nel(o(b))), 2048.0)
 
     def to_b(t, h, first, fac, x, top=None):
@@ -362,7 +367,7 @@ def build():
         scan(o(y), fac, x, 0.0, AL.mult, AL.add)
         for gq in range(8):
             mm(o(ps, 160, 168, p0=32 * (gq // 2), p1=32 * (gq // 2) + 32), o("FW", 16 - 16 * (gq % 2), 48 - 16 * (gq % 2)),
-               o(y, 10 * gq + 2, 10 * gq + 10), gq % 2 == 0, gq % 2 == 1)
+               o(y, 10 * gq + 2, 10 * gq + 10), gq % 2 == 0, gq % 2 == 1, gq > 0)
         f = o(f, 8 * (t % 2), 8 * (t % 2) + 8)
         if top:
             ts(f, o(ps, 160, 168), 2048.0, top, AL.add, AL.min)
@@ -395,7 +400,7 @@ def build():
 
     def update(t, h):
         H = str(h)
-        XA, XB = "XA" + H, "XB" + H
+        XA, XB = "XA", "XB" + H
         s, q = tile(t - 1, h), o("Q" + H)
         i = 2 * (t - 1) + h
         c = 128 if t == NS else 0
@@ -404,27 +409,39 @@ def build():
         mm(o(XB, 256, 384), o("E15", p1=1), o("LC", 128 * h, 128 * h + 128, p1=1), True, False)
         mm(o(XB, 256, 384), o("LN", p1=1), o("CB", c, c + 128, p1=1), False, False)
         mm(o(XB, 256, 384), o("DM", 128, 256), q, False, t == NS)
-        mm(o(XA, 0, 128, p0=96, p1=120), o("CT", 240 * i + 1, 240 * i + 240, 10), o("ID"))
-        (cp if ON["S"] == "V" else lin)(tile(t - 1, h, p0=96, p1=120), o(XA, 0, 128, p0=96, p1=120))
-        mm(o(XA, 128, 256), o("BC", 0, 128), s)
-        mm(o(XA, 256, 384), o("BC", 128, 256), s)
-        mm(o(XA, 0, 128, p1=96), o("WM", 0, 96), s)
         m1, m2 = o("M" + H, 0, 128), o("M" + H, 128, 256)
-        mask(m1, o(XA, 128, 256))
+        if t == NS:
+            x = o("TP", 128 * h, 128 * h + 128, p0=96, p1=112)
+            y = o("CT", 160 * i + 1, 160 * i + 160, 10)
+            add("P", "pt", (x, y, o("ID")), [y, o("ID")], [x], 128 * PCYC)
+            cp(tile(t - 1, h, p0=96, p1=112), x)
+            mm(o(XA, 128, 256), o("BC", 0, 128), s)
+            mask(m1, o(XA, 128, 256))
+            tt(o("T1" + H), m1, o(XB, 0, 128), AL.mult)
+            tt(o("QF" + H), o("T1" + H), o(XB, 256, 384), AL.add)
+        x = o("TP", 128 * h, 128 * h + 128, p0=96, p1=120)
+        for (z, y) in ((x, o("CT", 160 * i + 1, 160 * i + 240, 10)), (x[:2] + (104,) + x[3:], o("RU" + H, 160, 1360, 170))):
+            ctx[4] = z != x
+            add("P", "pt", (z, y, o("ID")), [y, o("ID")], [z], 128 * PCYC)
+        (cp if ON["S"] == "V" else lin)(tile(t - 1, h, p0=96, p1=120), x)
         if t < NS:
+            mm(o(XA, 128, 256), o("BC", 0, 128), s)
+        mm(o(XA, 256, 384) if t < NS else o(XB, 128, 256), o("BC", 128, 256), s)
+        mm(o(XA, 0, 128, p1=96), o("WM", 0, 96), s)
+        if t < NS:
+            mask(m1, o(XA, 128, 256))
             mask(m2, o(XA, 256, 384), cB2)
         act(tile(t, h, p1=96), o(XA, 0, 128, p1=96), AF.Relu)
         s = tile(t, h)
         if t == NS:
-            ts(m2, o(XA, 256, 384), cB2, None, AL.is_lt)
-            tt(o("T1" + H), m1, o(XB, 0, 128), AL.mult)
+            m2 = o(XB, 128, 256)
+            ts(m2, m2, cB2, None, AL.is_lt)
             mm(o(XA, 384, 512, p1=24), o("XV", 0, 24), s)
             lin(o("YP", 128 * h, 128 * h + 128, p1=24), o(XA, 384, 512, p1=24))
             for k in range(3):
                 x = o("YP", 128 * h, 128 * h + 128, p0=8 * k, p1=8 * k + 8)
                 dma("S", ("ext", "ys", (256 * (k + 1) + 128 * h, 256 * (k + 1) + 128 * h + 128)), x, [x], [], 4096)
             y = o("YQ", 128 * h, 128 * h + 128)
-            tt(o("QF" + H), o("T1" + H), o(XB, 256, 384), AL.add)
             tt(y, o("QF" + H), m2, AL.mult)
             dma("S", ("ext", "yq", (128 * h, 128 * h + 128)), y, [y], [], 65536)
             return
@@ -439,7 +456,7 @@ def build():
     def start(h):
         H = str(h)
         ctx[3] = "start" + H
-        XA, XB = "XA" + H, "XB" + H
+        XA, XB = "XA", "XB" + H
         s, q = tile(0, h), o("Q" + H)
         hs = lambda b, **k: o(b, 128 * h, 128 * h + 128, **k)
         lin(s, one, n8(15))
@@ -449,6 +466,7 @@ def build():
         for x in (o("VB" + H), o("RS" + H, 143, 1488, 17)):
             fill(x, 0)
             fill(x[:5] + (10 * x[5],), -1)
+        asel(o("RU" + H, 143, 1488, 17), o("F2"), [[0, 80]], 0, 0)
         lin(o("Y" + H, 1, 80, 10), o("ONE", 0, 8), cK, 2048.0 + 256 * h)
         mm(o(XA, 128, 256), o("BC", 0, 128), s)
         mm(o(XA, 256, 384), o("BC", 128, 256), s)
@@ -479,9 +497,9 @@ def build():
                 ts(x, o("PW"), -1.0, None, AL.mult, None, f)
             else:
                 act(x, o("PW"), AF.Copy, -1.0, ind=f)
-        dma("S", ("rows", "GW", 0, 256), ("ext", "s0", None), [], [o("GW")], 8192)
+        dma("S", ("rows", "Qi", 0, 256), ("ext", "s0", None), [], [o("Qi")], 8192)
 
-    chain = {"A": [], "V": []}
+    chain = {"A": [], "V": [], "G": [], "X": []}
 
     def wide(t, h):
         H = str(h)
@@ -497,12 +515,13 @@ def build():
             chain["A"] = [act(o(P, 16 * a, 16 * b), o("PW"), AF.Copy, ind=o("CU" + H, a, b), after=chain["A"])]
         for (a, b) in PIECES:
             for k in range(16):
-                chain["V"] = [tt(o(EQ, 128 * k + a, 128 * k + b), o(P, 16 * a + k, 16 * b, 16), o("MP" + H, a, b), AL.not_equal, after=chain["V"])]
+                m = o("MP" + H, a, b) if k >= NM else o("MS" + H, 128 * (t % 2) + a, 128 * (t % 2) + b)
+                chain["V"] = [tt(o(EQ, 128 * k + a, 128 * k + b), o(P, 16 * a + k, 16 * b, 16), m, AL.not_equal, after=chain["V"])]
         for k in range(16):
-            mm(o(KY, k, 136, 17), o(P, k, 2048, 16), o("INp"), False, False)
+            mm(o(KY, k, 136, 17), o(P, k, 2048, 16), o("INp"), False, False, k % 4 > 0)
         mm(o(KY, 0, 136), tile(t, h), o("PN"), False, False)
         for k in range(16):
-            mm(o(KY, k, 136, 17), o(EQ, 128 * k, 128 * k + 128), o("INe"), False, k == 15)
+            mm(o(KY, k, 136, 17), o(EQ, 128 * k, 128 * k + 128), o("INe"), False, k == 15, k % 2 and k < 12)
 
     def choose(t, h):
         H = str(h)
@@ -511,27 +530,31 @@ def build():
         scan(o("RS" + H, 0, 1360, 10), o("RD"), o("KY" + H, 0, 136), 0.0, AL.add, AL.max)
         rs = o("RS" + H, 160, 1360, 170)
         rv = o("RS" + H, 143, 1488, 17)
-        nf, u = o("CT", 240 * i + 1, 240 * i + 80, 10), o("CT", 240 * i + 81, 240 * i + 160, 10)
-        land, x, ub = o("CT", 240 * i + 160, 240 * i + 240), o("CT", 240 * i, 240 * i + 80), o("CT", 240 * i + 80, 240 * i + 160)
-        ts(u, rs, MAG, MAG, AL.add, AL.subtract)
+        if TWICE:
+            scan(o("RU" + H, 0, 1360, 10), o("RD"), o("KY" + H, 0, 136), 0.0, AL.add, AL.max)
+        else:
+            cp(o("RU" + H, 160, 1360, 170), rs)
+        nf, ub = o("CT", 160 * i + 81, 160 * i + 160, 10), o("RU" + H, 143, 1488, 17)
+        land, x = o("CT", 160 * i + 160, 160 * i + 240), o("CT", 160 * i + 80, 160 * i + 160)
         if last:
-            ts(o("VB" + H, 1, 80, 10), rs, 2560.0, None, AL.max)
+            ts(o("VB" + H, 1, 80, 10), rs, 65 * 16384.0 + 2560.0, None, AL.max)
         fb = to_b(t, h, True, ub, o("VB" + H) if last else rv)
-        ts(nf, rs, 8192.0, None, AL.is_lt)
+        ts(nf, rs, 65.5 * 16384.0, None, AL.is_lt)
         f = to_b(t, h, False, ub, rv) if last else to_b(t, h, False, x, o("XB" + H, 384, 464))
-        j = add("G", "rdma", (land, x, t, "af%d" % i), [x], [], 500.0, 0.0)
-        add("X", "arr", ("af%d" % i, j), [], [land], 0.0, 2600.0, after=[j])
         snd = o("SND", 128 * i, 128 * i + 128)
         tt(snd, o("BW"), o("MS" + H, 128 * (t % 2), 128 * (t % 2) + 128), AL.min, fb)
-        land = o("MW", 2048 + 128 * i, 2048 + 128 * i + 128)
-        j = add("G", "rdma", (land, snd, t, "ad%d" % i), [snd], [], 500.0, 0.0)
-        add("X", "arr", ("ad%d" % i, j), [], [land], 0.0, 3200.0, after=[j])
+        sends = [(land, x, "af%d" % i, 2600.0), (o("MW", 2048 + 128 * i, 2048 + 128 * i + 128), snd, "ad%d" % i, 3200.0)]
+        land = sends[1][0]
+        for (a, b, sem, way) in sends:
+            j = [add("G", "rdma", (a, b, t, sem), [b], [], 500.0 + (0.0 if chain["G"] else OPEN), 0.0, chain["G"])]
+            add("X", "arr", (sem, j[0]), [], [a], 0.0, way, after=j + chain["X"])
+            chain["G"], chain["X"] = j, [add("X", "busy", ("bu",), [], [], 0.0, way - 1400.0, after=j)]
         if not last:
             act(o("CU" + H), o("CW"), AF.Copy, ind=fb)
             message(t + 1, h, f)
         if i == 2 * NS - 3:
             dma("S", ("rows", "CW", 0, 4096), ("ext", "gs", None), [], [o("CW", 0, 4096)], 131072)
-            cp(o("CW", 4096, 4608, 2), o("GW"))
+            lin(o("CW", 4096, 4608, 2), o("Qi"))
         if last:
             y = o("YS", 128 * h, 128 * h + 128)
             cp(y, o("CW"), f)
@@ -561,28 +584,47 @@ def build():
             if t == NS - 1 and h == 0:
                 arrived()
             update(t + 1, h)
-    prune(ops)
     return ops
 
 
-CASES = ((0.83, 1.1, 160.0, 0.35, 0.7, 62.0), (0.87, 1.35, 180.0, 0.45, 0.8, 67.0), (0.9, 2.0, 170.0, 0.5, 1.0, 80.0), (1.2, 1.1, 190.0, 0.5, 1.0, 87.0),
-         (1.2, 2.0, 170.0, 0.5, 1.0, 102.0), (0.9, 1.3, 200.0, 0.8, 0.8, 74.0))
-MID = (0.87, 1.4, 180.0, 0.5, 0.85)
-PERIOD, FIRST, BUS = 7500.0, 13300.0, 250.0
+def knots(ops):
+    res = []
+    home = []
+    for i, p in enumerate(ops):
+        if p["join"]:
+            q = res[-1]
+            q["cost"] += p["cost"]
+            q["calls"].append(i)
+        else:
+            q = dict(p)
+            q["deps"], q["calls"] = {}, [i]
+            res.append(q)
+        home.append(len(res) - 1)
+        for j, w in p["deps"].items():
+            if home[j] != home[i]:
+                q["deps"][home[j]] = q["deps"].get(home[j], False) or w
+    prune(res)
+    return res
+
+
+CASES = ((0.83, 1.1, 155.0, 0.4, 0.65, 300.0, 58.5), (0.83, 1.56, 165.0, 0.44, 0.65, 250.0, 63.0), (0.9, 2.0, 180.0, 0.5, 0.7, 260.0, 75.3),
+         (1.2, 1.15, 190.0, 0.55, 0.7, 230.0, 81.5), (1.2, 2.0, 180.0, 0.6, 0.7, 330.0, 97.5), (0.9, 1.4, 190.0, 0.56, 0.65, 230.0, 68.3))
+MID = (0.85, 1.5, 170.0, 0.46, 0.65, 250.0)
+PERIOD, FIRST, BUS = 6848.0, 13300.0, 250.0
+OWN = 1.0
 HAND = True
 SEED, HEAT, AHEAD = 1, 2.0, 2000.0
 SHIFT = {}
-EQ0 = 0.0
-DUE = {("V", "CH"): -1800, ("A", "CH"): -1800, ("P", "KY", 1): -1500, ("P", "KY", 2): -1400, ("A", "P", 1): -3600, ("A", "P", 2): -2600, ("A", "P", 3): -800,
-       ("V", "P", 1): -1480, ("V", "P"): -800, ("V", "RS", 1): 2180, ("V", "CT", 1): 2490, ("V", "VB"): 2520, ("V", "CT", 2): 2550,
-       ("G", "CT"): 2800, ("V", "Y"): 2730, ("V", "Z"): 3150, ("P", "MP", 1): 3450,
-       ("V", "OF"): 3310, ("V", "OM"): 6400, ("A", "OM"): 4700, ("V", "SND"): 3550, ("G", "MW"): 3940, ("A", "CU"): 3550, ("P", "MP"): 7000,
-       ("P", "XB", 1): 4500, ("P", "XB", 2): 4700, ("P", "XB", 3): 4750, ("P", "XB", 4): 4900, ("P", "XB", 5): 5000, ("P", "XA", 1): 5100,
-       ("V", "S"): 5600, ("A", "S", 1): 6450, ("A", "S", 2): 6450,
-       ("P", "XA", 2): 5880, ("P", "XA", 3): 5900, ("P", "XA", 4): 5920, ("A", "M"): 6220, ("P", "XB", 6): 6630,
-       ("P", "XA", 5): 7200, ("A", "MS"): 6600, ("V", "T1"): 6850, ("A", "M3"): 7600, ("A", "MO"): 4000, ("P", "MP", 9): 7000, ("V", "Q"): 7200,
-       ("P", "XB", 7): 7500, ("V", "ZX"): 9500, ("P", "XB"): 9800, ("S", "ext"): 9000, ("X", "af"): 2900, ("X", "ad"): 4000}
-EARLY = {"variables": 500, "BOu": 3000, "start0": 4000, "GSu": 7000, "start1": 8000, "CW": 10500, "BW": 7500, "CU0": 100, "CU1": 200}
+DUE = {("V", "CH"): (-380,), ("V", "P"): (-770, -1660), ("A", "P"): (-3090,), ("V", "EQ"): tuple(range(0, 1650, 106)),
+       ("P", "KY"): (-160, -100, -80, 210, 320, 630, 740, 800, 850, 910, 1010, 1230, 1440, 1550, 1650, 1760, 1860, 2710),
+       ("V", "RS"): (2090,), ("V", "RU"): (2200,), ("V", "CT"): (2370,), ("V", "VB"): (2380,), ("V", "Y"): (2480,), ("V", "OF"): (2990,),
+       ("V", "SND"): (3210,), ("G", "CT"): (2580,), ("X", "af"): (2600,), ("X", "bu"): (2600, 3600), ("G", "MW"): (3590,), ("X", "ad"): (3600,),
+       ("A", "CU"): (3210,), ("A", "MO"): (4000,), ("V", "Z"): (5120,), ("P", "MP"): (5360, 6620), ("V", "OM"): (5740,), ("A", "MS"): (6220,),
+       ("P", "TP"): (5460,), ("V", "S"): (5840,), ("P", "XA"): (6360, 6410, 6460, 7420), ("A", "M"): (6860, 6970), ("A", "S"): (7080,),
+       ("A", "M3"): (9440,), ("P", "XB"): (6300, 6580, 6920, 6970, 7920, 7970, 9670, 10310, 10450, 10710), ("V", "T1"): (8830,),
+       ("V", "Q"): (9390,), ("V", "ZX"): (9940,)}
+EARLY = {"variables": 500, "BOu": 3000, "start0": 4000, "GSu": 7000, "start1": 8000, "CW": 13000, "BW": 7500, "CU0": 100, "CU1": 200}
+STRETCHES = ((0.0, 0.4, 0.45), (0.72, 2.0, 0.2), (0.3, 0.55, 0.1), (0.5, 0.8, 0.1), (0.15, 0.4, 0.15))
 GAP = {("V", "CW"): 800.0, ("A", "CW"): 900.0}
 
 
@@ -593,7 +635,7 @@ def graph(ops, c, gt, l, f, pe=1.0, BUS=BUS):
     for p in ops:
         k = {"ts": 6, "tt": 4, "cp": 2, "act": 5}.get(p["kind"])
         v = p["cost"]
-        if p["eng"] in "VAP" and p["kind"] != "dma":
+        if p["eng"] in "VAPG" and p["kind"] not in ("dma", "rdma"):
             if k is not None and p["args"][k] is not None:
                 v += nel(p["args"][0]) * (gt - GTH) * CYC
             v *= c / CYC * (pe if p["eng"] == "P" else 1.0)
@@ -603,7 +645,7 @@ def graph(ops, c, gt, l, f, pe=1.0, BUS=BUS):
             bus = p["args"][2] / BUS + (bus - 60.0 if p["args"][1][0] == "ext" and p["args"][0][0] != "rows" else 0.0)
             v += bus
         lat.append(v)
-    fw = [[(j, cost[j] + (lat[j] + l if p["deps"][j] or ops[j]["eng"] != p["eng"] else 0.0)) for j in p["near"]] for p in ops]
+    fw = [[(j, cost[j] + (lat[j] + l if ops[j]["eng"] != p["eng"] or p["eng"] == "X" else lat[j] + OWN * l if p["deps"][j] else 0.0)) for j in p["near"]] for p in ops]
     return cost, lat, fw
 
 
@@ -678,7 +720,7 @@ def once(eng, g, succ, due, slack):
     return order
 
 
-def plan(ops, climbs=500, tries=0, polish=(6000, 9000)):
+def plan(ops, climbs=200, tries=0, polish=(300, 160000)):
     n = len(ops)
     eng = [p["eng"] for p in ops]
     sets = [(graph(ops, *c[:-1]), c[-1]) for c in CASES]
@@ -703,14 +745,8 @@ def plan(ops, climbs=500, tries=0, polish=(6000, 9000)):
                     cls[-1] = names.setdefault((p["part"], e, nm, k), len(names))
             continue
         t, h = p["at"]
-        if (e, nm) == ("V", "EQ"):
-            v, k = EQ0 + 1780.0 * (k - 1) / (16 * len(PIECES)), (k - 1) // 4
-        elif (e, nm) == ("P", "KY") and 2 < k < 44:
-            v, k = (42.0 * k, 3) if k < 19 else (800.0, 4) if k == 19 else (75.0 * k - 675.0, 5 + (k - 20) // 4) if k < 36 else (2950.0 + k, 9)
-        elif (e, nm) == ("P", "MP") and k < 9:
-            v, k = DUE[e, nm, 1] + k, 1
-        else:
-            v = DUE.get((e, nm, k), DUE.get((e, nm), 7000.0)) + k
+        v = DUE.get((e, nm), ())
+        v = float(v[k - 1]) if k <= len(v) else 7000.0 + k
         base[i] = FIRST + PERIOD * (t + 0.5 * h) + v
         table[p["cls"]] = v
         cls.append(names.setdefault((c, e, nm, k), len(names)))
@@ -759,7 +795,7 @@ def plan(ops, climbs=500, tries=0, polish=(6000, 9000)):
     cls = np.array([names.setdefault(p["cls"] if p["at"] and 1 <= p["at"][0] < NS - 1 else i, len(names)) for i, p in enumerate(ops)])
     ref = {p["cls"]: beg[i] for i, p in enumerate(ops) if p["at"] == (2, 0)}
     if HAND:
-        ref = {c: beg[per] + (table[c] - DUE["V", "RS", 1]) * 2 * half / PERIOD for c in ref}
+        ref = {c: beg[per] + (table[c] - DUE["V", "RS"][0]) * 2 * half / PERIOD for c in ref}
     base = np.array([ref[p["cls"]] + half * (2 * p["at"][0] + p["at"][1] - 4) if p["at"] and 1 <= p["at"][0] < NS - 1 and p["cls"] in ref
                      else beg[i] for i, p in enumerate(ops)])
     near = [p["near"] for p in ops]
@@ -776,30 +812,146 @@ def plan(ops, climbs=500, tries=0, polish=(6000, 9000)):
         v = [x if k == c else replay(eng, g, r) / w for k, (g, w) in enumerate(sets)]
         return (sum(v) / len(v) + max(v)) / 2, r, d, due, v, {}
     cur = top = rank(base.tolist(), np.zeros(len(names)), 0, 1e9)
-    for stage in range(2):
-        if stage:
-            base, cls = np.array(starts(eng, mid, top[1] if top[0] < best[0] else best[1])), np.arange(n)
-            cur = top = rank(base.tolist(), np.zeros(n), 0, 1e9)
-        for it in range(polish[stage]):
-            c = int(rng.integers(len(sets)))
-            if c not in cur[5]:
-                cur[5][c] = [(i, y) for (i, y) in waits(ops, eng, sets[c][0], cur[1]) if cls[i] != cls[y]]
-            i, y = cur[5][c][int(rng.integers(len(cur[5][c])))]
-            d = cur[2].copy()
-            far = 1.0 + (0.0, 60.0, 300.0)[it % 3] * float(rng.random())
-            if it % 7 == 0:
-                d[cls[y]] = cur[3][y] + 1500.0 * float(rng.normal()) - base[y]
-            elif it % 2:
-                d[cls[i]] = cur[3][y] - far - base[i]
+    for it in range(polish[0]):
+        c = int(rng.integers(len(sets)))
+        if c not in cur[5]:
+            cur[5][c] = [(i, y) for (i, y) in waits(ops, eng, sets[c][0], cur[1]) if cls[i] != cls[y]]
+        i, y = cur[5][c][int(rng.integers(len(cur[5][c])))]
+        d = cur[2].copy()
+        far = 1.0 + (0.0, 60.0, 300.0)[it % 3] * float(rng.random())
+        if it % 7 == 0:
+            d[cls[y]] = cur[3][y] + 1500.0 * float(rng.normal()) - base[y]
+        elif it % 2:
+            d[cls[i]] = cur[3][y] - far - base[i]
+        else:
+            d[cls[y]] = cur[3][i] + far - base[y]
+        heat = HEAT * float(rng.random()) * (1.0 - it / polish[0])
+        v = rank((base + d[cls]).tolist(), d, c, cur[4][c] + 2.0 * heat + 1.0)
+        if v and v[0] <= cur[0] + heat:
+            cur = v
+            if v[0] < top[0]:
+                top = v
+    order, v = top[1], top[0]
+    for (a, b, share) in STRETCHES:
+        beg = starts(eng, mid, order)
+        order = sorted(order, key=lambda i: beg[i])
+        end = beg[order[-1]]
+        lo, hi = [len([1 for x in beg if x < z * end]) for z in (a, b)]
+        order, v = stretch(ops, eng, sets, succ, order, lo, hi, int(share * polish[1]), rng)
+    return order, v, top[0], best[0]
+
+
+def stretch(ops, eng, sets, succ, order, lo, hi, tries, rng):
+    n = len(ops)
+    seg = order[lo:hi]
+    where = [0] * n
+    for i in seg:
+        where[i] = 1
+    for i in order[hi:]:
+        where[i] = 2
+    fix = []
+    for (g, w) in sets:
+        cost, lat, fw = g
+        beg = starts(eng, g, order)
+        tail = [cost[i] + lat[i] for i in range(n)]
+        nxt = {}
+        for i in reversed(order[hi:]):
+            if eng[i] != "X":
+                tail[i] = max(tail[i], cost[i] + nxt.get(eng[i], 0.0))
+                nxt[eng[i]] = tail[i]
+            for j, d in fw[i]:
+                tail[j] = max(tail[j], d + tail[i])
+        free = {e: 0.0 for e in "VAPGSX"}
+        end = 0.0
+        for i in order[:lo]:
+            end = max(end, beg[i] + tail[i])
+            if eng[i] != "X":
+                free[eng[i]] = beg[i] + cost[i]
+        row = {i: (eng[i], max([0.0] + [beg[j] + d for j, d in fw[i] if where[j] == 0]), [(j, d) for j, d in fw[i] if where[j]],
+                   0.0 if eng[i] == "X" else cost[i], tail[i]) for i in seg}
+        fix.append((row, free, end, nxt, w, beg))
+
+    def run(c, r):
+        row, free, end, nxt, w, beg = fix[c]
+        free = dict(free)
+        for i in r:
+            e, s, fw, co, ta = row[i]
+            if co and free[e] > s:
+                s = free[e]
+            for j, d in fw:
+                if beg[j] + d > s:
+                    s = beg[j] + d
+            beg[i] = s
+            free[e] = s + co
+            if s + ta > end:
+                end = s + ta
+        for e, x in nxt.items():
+            if free[e] + x > end:
+                end = free[e] + x
+        return end / w
+
+    def held(c, r):
+        row, free, end, nxt, w, beg = fix[c]
+        run(c, r)
+        before = {}
+        last = {}
+        for i in r:
+            before[i] = last.get(eng[i])
+            last[eng[i]] = i
+        i = max(r, key=lambda k: beg[k] + max(row[k][4], row[k][3] + nxt.get(eng[k], 0.0) if last[eng[k]] == k else 0.0))
+        res = []
+        while i is not None:
+            j = max(row[i][2] + [(None, row[i][1])], key=lambda x: x[1] + (0.0 if x[0] is None else beg[x[0]]))
+            y = before[i]
+            if row[i][3] and y is not None and beg[y] + row[y][3] > j[1] + (0.0 if j[0] is None else beg[j[0]]):
+                res.append((i, y))
+                i = y
             else:
-                d[cls[y]] = cur[3][i] + far - base[y]
-            heat = HEAT * float(rng.random()) * (1.0 - it / polish[stage]) / (1 + 3 * stage)
-            v = rank((base + d[cls]).tolist(), d, c, cur[4][c] + 2.0 * heat + 1.0)
-            if v and v[0] <= cur[0] + heat:
-                cur = v
-                if v[0] < top[0]:
-                    top = v
-    return top[1], top[0], best[0]
+                i = j[0]
+        return res
+
+    def moved(r, i, y, early):
+        a, b = r.index(y), r.index(i)
+        part = r[a:b + 1]
+        go = {i if early else y}
+        for k in (reversed(part) if early else part):
+            if k in go:
+                go.update(ops[k]["near"] if early else succ[k])
+        if (y if early else i) in go:
+            return None
+        x, z = [k for k in part if k in go], [k for k in part if k not in go]
+        return r[:a] + (x + z if early else z + x) + r[b + 1:]
+    v = [run(c, seg) for c in range(len(sets))]
+    cur = top = ((sum(v) / len(v) + max(v)) / 2, seg, v, {})
+    for it in range(tries):
+        c = int(rng.integers(len(sets)))
+        if c not in cur[3]:
+            cur[3][c] = held(c, cur[1])
+        if not cur[3][c]:
+            continue
+        i, y = cur[3][c][int(rng.integers(len(cur[3][c])))]
+        early = it % 2 == 0
+        if it % 3:
+            q = [k for k in cur[1] if eng[k] == eng[i]]
+            k = 1 + int(8 * float(rng.random()) ** 2)
+            if early:
+                y = q[max(0, q.index(y) - k)]
+            else:
+                i = q[min(len(q) - 1, q.index(i) + k)]
+        r = moved(cur[1], i, y, early)
+        if r is None:
+            continue
+        heat = 0.5 * HEAT * float(rng.random()) * (1.0 - it / tries)
+        x = run(c, r)
+        if x > cur[2][c] + 2.0 * heat + 1.0:
+            continue
+        v = [x if k == c else run(k, r) for k in range(len(sets))]
+        s = (sum(v) / len(v) + max(v)) / 2
+        if s <= cur[0] + heat:
+            cur = (s, r, v, {})
+            if s < top[0]:
+                top = cur
+    return order[:lo] + top[1] + order[hi:], top[0]
 
 
 def starts(eng, g, order):
@@ -847,7 +999,8 @@ def rank_program(g, core, T, topo):
         return
     if "ops" not in CACHE:
         CACHE["ops"] = build()
-        CACHE["order"] = plan(CACHE["ops"])[0]
+        nodes = knots(CACHE["ops"])
+        CACHE["order"] = [i for k in plan(nodes)[0] for i in nodes[k]["calls"]]
     ops, order = CACHE["ops"], CACHE["order"]
     nr = len(T.cores)
     qs = {"V": g.vector, "A": g.scalar, "P": g.tensor, "G": g, "S": g.sync}
@@ -959,6 +1112,8 @@ def rank_program(g, core, T, topo):
                 r = q.activation(ap(a[0]), src(a[1], a[5]), a[2])
         elif kind == "mm":
             r = q.matmul(ap(a[0]), ap(a[1]), ap(a[2]), a[3], a[4])
+        elif kind == "pt":
+            r = q.transpose(ap(a[0]), ap(a[1]), ap(a[2]))
         elif kind == "iota":
             if SCRATCH[a[0][0]][2] == I32:
                 r = q.iota(ap(a[0]), a[1], a[2], a[3])

import math
import numpy as np
from concourse.bass import DstId, RemoteDMATransfer
from concourse.mybir import dt, AluOpType, AxisListType, ActivationFunctionType

AL = AluOpType
AF = ActivationFunctionType
NS = 6
PIECES = ((0, 128),)
GP = (0, 1)
CC = (0, 32, 64, 96, 128, 160, 192, 208, 224, 240, 256)
CA = 128
LV = ("SID", "BC", "BT", "S0", "S1", "ZP", "SH0", "IDh", "IX", "WS")
PS = 14
ON = {"CH": "V", "OM": "V", "S": "V", "BOu": "V", "GSu": "V"}
PV = (28, 22, 22, 22, 22, 14)
BV = 4
FIXV = (5, 7)
EV = ()
NM = 0
TWICE = True
OPEN = 1000.0
LOADS = (("Qi", "q0"), ("GSi", "gs"), ("CLs", "cl"))
HH = float(2 ** 60)
BIG = 2 ** 21
F32, BF, F16, I32, U16 = "float32", "bfloat16", "float16", "int32", "uint16"
BYTES = {F32: 4, BF: 2, F16: 2, I32: 4, U16: 2}

SCRATCH = {}
for _d, _l in (
        (BF, (("PW", 4096), ("BW", 4624), ("MW", 3584), ("SND", 1536), ("MO", 1536), ("CT", 2000), ("ONE", 384), ("ZB", 160), ("ZER", 192),
              ("IXb", 136), ("SID", 1280), ("SH0", 128), ("INe", 8), ("INp", 8), ("F2", 80), ("FT", 80), ("G8", 128), ("RD", 136),
              ("BC", 384), ("BS", 128), ("PN", 136), ("XV", 40), ("WM", 192), ("WO", 400), ("IOG", 128), ("IOH", 136), ("IOK", 136))),
        (I32, (("CW", 4608), ("CLs", 2048), ("BOi", 288), ("GSi", 256), ("Qi", 256), ("STi", 256), ("PI", 16))),
        (U16, (("BOu", 272), ("GSu", 256))),
        (F16, (("IDh", 128), ("X2", 288), ("X3", 288), ("ZP", 320), ("IX", 136), ("DM", 256), ("D3", 128), ("E15", 128),
               ("LN", 128), ("CB", 384), ("LC", 256), ("FW", 48), ("WQ", 80))),
        (F32, (("CC", 40), ("IO16", 16), ("LP", 256), ("IN8", 16), ("IN16", 8), ("D8", 8), ("WZ", 80),
               ("YQ", 256), ("YS", 256), ("YP", 256)))):
    for _n, _c in _l:
        SCRATCH[_n] = ("sbuf", [128, _c], _d)
for _h in range(2):
    for _n, _c, _d in (("P", 2048, BF), ("EQ", 2048, BF), ("CU", 128, U16), ("CH", 128, F16), ("MS", 256, BF), ("RS", 1488, F32),
                       ("RU", 1488, BF), ("VB", 80, F32), ("Y", 80, F16), ("Z", 80, F16), ("OF", 16, U16), ("OM", 16, U16), ("S", 896, BF),
                       ("Q", 128, F16), ("M", 256, BF),
                       ("M3", 128, BF), ("T1", 128, F32), ("ZX", 128, F32), ("QF", 128, F32)):
        SCRATCH["%s%d" % (_n, _h)] = ("sbuf", [128, _c], _d)
    for _n in ("MP", "KY", "XB"):
        SCRATCH["%s%d" % (_n, _h)] = ("psum", [128, 512], F32)
SCRATCH["XA"] = ("psum", [128, 512], F32)
SCRATCH["TP"] = ("psum", [128, 256], BF)

SEMAPHORES = ["cV", "cA", "cP", "cG", "loc"] + ["d%d" % i for i in range(48)] + ["ad%d" % i for i in range(12)] + ["af%d" % i for i in range(12)]

CYC, PCYC, GTH = 1.0, 0.8, 1.9


def o(b, c0=0, c1=None, st=1, p0=0, p1=128):
    if b == "ID":
        return ("ZB", p0, p1, 16 + c0, 16 + (c1 or 128), st)
    if c1 is None:
        c1 = SCRATCH[b][1][1]
    return (b, p0, p1, c0, c1, st)


def nel(x):
    return len(range(x[3], x[4], x[5]))


def two(x):
    return BYTES[SCRATCH[x[0]][2]] == 2


def isps(x):
    return SCRATCH[x[0]][0] == "psum"


def span(x):
    return (x[1], x[2], x[3], x[3] + (nel(x) - 1) * x[5] + 1, x[5])


def meet(a, b):
    if (a[2] - b[2]) % math.gcd(a[4], b[4]):
        return False
    return a[0] < b[1] and b[0] < a[1] and a[2] < b[3] and b[2] < a[3]


def build():
    ops = []
    hist = {}
    bank = {}
    lastpe = {}
    ctx = ["", {}, None, "constants", False]

    def add(eng, kind, args, reads, writes, cost, lat=0.0, after=()):
        i = len(ops)
        deps = {}
        dma = kind in ("dma", "rdma")

        def dep(j, raw):
            if j == i:
                return
            pj = ops[j]
            w = not (pj["eng"] == "P" and eng == "P")
            deps[j] = deps.get(j, False) or w
        for x, wr in [(x, False) for x in reads] + [(x, True) for x in writes]:
            s = span(x)
            hl = hist.setdefault(x[0], [])
            for (j, s2, w2) in hl:
                if (wr or w2) and meet(s, s2):
                    dep(j, w2)
            if isps(x):
                b = bank.setdefault(x[0], [None, [], []])
                if b[0] != eng:
                    b[0], b[2], b[1] = eng, b[1], []
                for j in b[2]:
                    dep(j, True)
                if i not in b[1]:
                    b[1].append(i)
                if eng == "P":
                    if x[0] in lastpe:
                        dep(lastpe[x[0]], False)
                    lastpe[x[0]] = i
        for x in writes:
            s = span(x)
            hist[x[0]] = [e for e in hist[x[0]] if not (s[0] <= e[1][0] and e[1][1] <= s[1] and s[2] <= e[1][2] and e[1][3] <= s[3]
                                                        and (s[4] == 1 or (s[4] == e[1][4] and (s[2] - e[1][2]) % s[4] == 0)))]
        for x in reads:
            hist[x[0]].append((i, span(x), False))
        for x in writes:
            hist[x[0]].append((i, span(x), True))
        for j in after:
            deps[j] = deps.get(j, False)
        nm = args[0][0] if isinstance(args[0], tuple) else args[0][:2]
        key = (ctx[0], eng, nm[:-1] if nm[-1] in "01" and nm[:-1] + "1" in SCRATCH and nm[:-1] + "0" in SCRATCH and ctx[0] else nm)
        ctx[1][key] = ctx[1].get(key, 0) + (0 if ctx[4] else 1)
        ops.append({"eng": eng, "kind": kind, "args": args, "deps": deps, "cost": cost, "lat": lat, "cls": key + (ctx[1][key],), "at": ctx[2],
                    "part": ctx[3], "join": ctx[4]})
        ctx[4] = False
        return i

    def aps(*xs):
        return [x for x in xs if isinstance(x, tuple)]

    def ts(out, a, s1, s2, op0, op1=None, ind=None):
        n = nel(out)
        c = 60 + n * GTH if ind else max(64, n * (0.5 if two(out) and two(a) else 1))
        return add("V", "ts", (out, a, s1, s2, op0, op1, ind), aps(a, s1, s2, ind), [out], c * CYC)

    def tt(out, a, b, op, ind=None, after=()):
        n = nel(out)
        c = 60 + n * GTH if ind else max(64, n * (1 if isps(a) or isps(b) else 2))
        return add("V", "tt", (out, a, b, op, ind), aps(a, b, ind), [out], c * CYC, after=after)

    def cp(out, a, ind=None):
        n = nel(out)
        c = 60 + n * GTH if ind else max(64, n * (0.5 if two(out) and two(a) else 1))
        return add("V", "cp", (out, a, ind), aps(a, ind), [out], c * CYC)

    def ms(out, v):
        return add("V", "ms", (out, v), [], [out], max(64, nel(out) * (0.5 if two(out) else 1)) * CYC)

    def red(out, a):
        return add("V", "red", (out, a), [a], [out], max(64, nel(a)) * CYC)

    def scan(out, a, b, init, op0, op1):
        return add("V", "scan", (out, a, b, init, op0, op1), [a, b], [out],
                   max(64, nel(out) * (0.5 if two(out) and two(a) and two(b) else 1)) * CYC)

    def act(out, a, f, scale=1.0, bias=0.0, ind=None, after=()):
        n = nel(out)
        c = 78 + n * GTH if ind else max(64, n)
        return add("A", "act", (out, a, f, scale, bias, ind), aps(a, ind, bias, scale), [out], c * CYC, after=after)

    def lin(out, a, scale=1.0, bias=0.0):
        if out[0] in LV and not ctx[0] and not isps(a):
            return ts(out, a, scale, bias, AL.mult, AL.add)
        return act(out, a, AF.Copy if bias == 0.0 else AF.Identity, scale, bias)

    def mm(out, l, r, s0=True, s1=True, join=False):
        same = ops[-1]["kind"] == "mm" and ops[-1]["args"][1] == l and ops[-1]["args"][0][0] == out[0]
        c = max(16 if same else min(64, nel(l)), nel(r)) * (1 if two(l) else 4)
        ctx[4] = join
        return add("P", "mm", (out, l, r, s0, s1), [l, r], [out], c * PCYC)

    def iota(out, pat, base, cm):
        return add("G", "iota", (out, pat, base, cm), [], [out], 160 + 2 * nel(out) * CYC)

    def fill(out, v):
        return iota(out, [[0, nel(out)]], v, 0)

    def asel(out, a, pat, base, cm, op=AL.is_equal, v=0.0):
        return add("G", "asel", (out, a, pat, base, cm, op, v), [a], [out], 210 + 2 * nel(out) * CYC)

    def shift(e, out, a, v):
        return ts(out, a, v, None, AL.add) if e == "V" else act(out, a, AF.Identity, 1.0, v)

    def dma(eng, out, src, rd, wr, nbytes, after=()):
        return add(eng, "dma", (out, src, nbytes), rd, wr, 60.0, 1300.0, after)

    def col(b, c):
        return o(b, c, c + 1)

    la = [dma("A", o("BOi", 0, 256), ("ext", "bo", None), [], [o("BOi", 0, 256)], 131072)]
    for x, nm in [(o("BOi", 256 + 16 * k, 272 + 16 * k), "s0") for k in range(2)] + [
            (o("STi", p0=8 * k, p1=8 * k + 8), nm) for k, nm in enumerate(("p0", "p0", "n0", "n0", "w0"))]:
        la = [dma("A", x, ("ext", nm, None), [], [x], 8192, la)]
    ld = []
    for (a, b) in ((0, 512), (512, 1024), (1024, 2048), (2048, 3072), (3072, 4096)):
        ld = [dma("S", o("PW", a, b), ("ext", "pt", (a, b)), [], [o("PW", a, b)], 256 * (b - a), ld)]
    for (b, nm) in LOADS:
        ld = [dma("S", o(b), ("ext", nm, None), [], [o(b)], 512 * nel(o(b)), ld)]
    ld = [dma("S", o("MW", 0, 2048), ("ext", "m0", None), [], [o("MW", 0, 2048)], 524288, ld)]

    ms(o("ONE"), 1.0)
    one = o("ONE", 0, 128)
    iota(col("PI", 0), [[0, 1]], 0, 1)
    for x, y in ((o("CW", 4096, 4352), ("ext", "q0", None)), (o("CW", 4352, 4608), ("ext", "q0", None)), (o("BW", 4096, 4608), ("ext", "pt", (0, 512)))):
        ld = [dma("S", x, y, [], [x], 131072, ld)]
    for k in range(4):
        x, y = o("S%d" % (k % 2), 128 + 384 * (k // 2), 512 + 384 * (k // 2), p0=96), o("ONE", p0=96)
        ld = [dma("S", x, y, [y], [x], 24576, ld)]
    asel(o("ZB"), o("ONE", 0, 160), [[1, 160]], -16, -1)
    iota(o("IO16"), [[1, 16]], 0, 0)
    iota(o("IOG"), [[1, 8], [0, 16]], 0, 0)
    iota(o("IOH"), [[1, 8], [0, 17]], 0, 0)
    iota(o("IOK"), [[0, 8], [-1, 17]], 81, 0)
    iota(o("LP", p1=1), [[1, 256]], 1664, 0)
    asel(o("IXb"), o("ONE", 0, 136), [[-16, 8], [-1, 17]], 0, 1)
    fill(o("RD"), 0)
    fill(o("RD", 0, 136, 17), -BIG)
    asel(o("FT"), o("ONE", 0, 80), [[0, 8], [-16, 10]], 16, 1, AL.is_ge, 2.0 ** 40)
    asel(o("F2"), o("FT"), [[0, 8], [-16, 10]], 32, 1, AL.is_ge)
    ms(o("F2", 0, 80, 10), 0.0)
    ts(o("F2", 2, 80, 10), o("F2", 2, 80, 10), 2.0 ** -40, None, AL.mult)
    fill(o("CT", 0, 80), 0)
    for c, (s, op) in enumerate(((15, AL.bitwise_and), (4, AL.arith_shift_right), (3, AL.arith_shift_right), (7, AL.bitwise_and),
                                 (16, AL.bitwise_and), (8, AL.bitwise_and))):
        ts(col("PI", c + 1), col("PI", 0), s, None, op)
    cp(o("CC", 0, 7), o("PI", 0, 7))
    cP, cJ, cP16, cP8, cM8, cP32, cQ8 = [col("CC", c) for c in range(7)]
    cJ16, cBias, cN0, cJ15, cJd, cBS, cJe, cJ1, cB2 = [col("CC", c) for c in range(7, 16)]
    vp, vn, vr, vw, c1, c2a, c3, c3b, cpn, cA, cK, cJ0, cS1 = [col("CC", c) for c in range(16, 29)]
    lin(cJ16, cP32, -1.0 / 16, 1.0)
    lin(o("ZP", 0, 160), o("ZB"), cJ16)
    ts(o("ZP", 160, 320), o("ZB"), cP32, 1.0 / 16, AL.mult, AL.mult)
    lin(cBias, cJ, 1.0, 0.5)
    lin(cB2, cJ, -1.0, -0.5)
    lin(cK, cP, 2.0)
    ts(cJ0, cJ, 0.0, None, AL.is_equal)
    ts(cJ1, cJ, 1.0, None, AL.is_equal)
    ts(cJ15, cJ, 15.0, None, AL.is_equal)
    lin(cN0, cJ0, -0.5, 0.5)
    ts(cJd, cJ15, cJ1, 0.5, AL.subtract, AL.mult)
    ts(cJe, cJ0, cJ1, 0.5, AL.add, AL.mult)
    ts(o("IN8"), o("IO16"), cP8, None, AL.is_equal)
    ts(o("IN16"), o("IO16", 0, 8), cP16, None, AL.is_equal)
    ts(o("D8"), o("IO16", 0, 8), cM8, None, AL.is_equal)
    lin(o("INe"), o("IN16"), -float(2 ** 19))
    lin(o("INp"), o("IN16"), -float(2.0 ** -41))
    lin(o("IDh"), o("ID"))
    lin(o("IX"), o("IXb"))
    ms(o("IX", 16, 136, 17), 0.0)
    lin(o("LC", p1=1), o("LP", p1=1))
    ms(o("LN", p1=1), 1.0)
    ts(cS1, cQ8, 0.0, None, AL.is_equal)
    ts(o("G8"), o("IOG"), cM8, None, AL.is_equal)
    ms(o("FW"), 0.0)
    ts(o("FW", 16, 32), o("IO16"), cJ, None, AL.is_equal)
    n8 = lambda s: col("IN8", s)
    lin(vp, n8(0), 1.0, n8(1))
    lin(vn, n8(3), -1.0, n8(2))
    lin(vr, n8(6), -1.0, n8(5))
    red(vw, o("IN8", 7, 12))
    for k, v in enumerate((vp, vn, n8(4), vr, vw)):
        lin(o("XV", 8 * k, 8 * k + 8), o("D8"), v)
    lin(c1, n8(13), 64.0, vp)
    ts(c2a, n8(14), n8(13), vn, AL.subtract, AL.subtract)
    ts(c3, n8(15), vp, vr, AL.add, AL.subtract)
    lin(c3b, n8(15), 15.0, vp)
    ts(cpn, vr, vw, -2.0 ** 23, AL.add, AL.mult)
    lin(o("BC", 0, 128), o("G8"), c1)
    lin(o("BC", 128, 256), o("G8"), c2a)
    lin(o("BC", 256, 384), o("G8"), c3)
    lin(o("BC", 271, 384, 16), o("D8"), c3b)
    lin(cA, o("ID", 121, 122), 16384.0)
    ts(o("PN"), o("IOH"), cM8, cpn, AL.is_equal, AL.mult)
    ms(o("PN", 16, 136, 17), 0.0)
    lin(o("PN", p0=96), o("IOK", p0=96), o("CC", 25, 26, p0=96))
    ts(cBS, n8(15), n8(14), 256.0, AL.subtract, AL.mult)
    lin(o("BS"), o("G8"), cBS)
    for k, v in enumerate((-128.0, 1664.0, -2048.0)):
        ms(o("CB", 128 * k, 128 * k + 128, p1=1), v)
    lin(o("SH0"), o("ZB", 17, 145), cN0)
    ms(o("E15", p1=1), 0.0)
    ms(o("E15", 15, 128, 16, p1=1), 0.5)
    ms(o("WZ"), 0.0)
    ms(o("WQ"), 0.0)
    lin(o("WZ", 0, 80, 10), o("IN16"), -1.0)
    lin(o("WZ", 1, 80, 10), o("IN16"), cJ15)
    lin(o("WQ", 0, 80, 10), o("IN16"), cJd)
    lin(o("WQ", 1, 80, 10), o("IN16"), cJe)
    fill(o("WO", p1=1), 0)
    iota(o("WO", 1, 400, 10, p1=1), [[256, 5], [0, 8]], 384 - 2048, 0)
    var = {"p": o("XV", 0, 8), "n": o("XV", 8, 16), "w": o("XV", 16, 24), "r": o("XV", 24, 32), "a": o("XV", 32, 40),
           "u": o("ID", 96, 104), "f": o("ID", 104, 112), "s": o("ID", 112, 120), "1": o("ID", 120, 128)}
    ell = [("w", 1), ("a", -16), ("f", -1), ("u", -2.0 ** -14), ("r", -128)]
    layer = ([("p", 1), ("f", 64), ("1", -64)], [("r", -1), ("a", -1), ("f", 64), ("1", -63)],
             [("n", 1), ("f", 1), ("s", -1)], [("n", 1), ("f", 1), ("s", -1), ("1", -16)],
             ell + [("1", 82)], ell + [("1", 35)], ell + [("1", 34)],
             [("1", 1), ("n", -1), ("f", -65), ("s", 1)],
             [("p", 1), ("r", -1), ("n", -1), ("f", 63), ("s", 1), ("a", -64), ("1", -62)],
             [("a", 1), ("s", 1), ("1", -1)],
             [("p", 1), ("n", 1), ("f", 65), ("s", -1), ("r", -1), ("a", -64), ("1", -95)],
             [("p", 1), ("n", 1), ("f", 1), ("s", -1), ("1", -32)],
             [("p", 1)], [], [("n", 1)], [], [("w", 1)], [("w", 1), ("1", -31), ("1", -16)], [("w", 1), ("1", -32), ("1", -16)],
             [("p", 1), ("n", -1), ("1", 1)], [], [], [], [])
    parts = {82: (64, 16, 1, 1), 35: (16, 16, 1, 1, 1), 34: (16, 16, 1, 1), -31: (-16, -16, 1), -32: (-16, -16), -63: (-64, 1), -65: (-64, -1),
             63: (64, -1), 65: (64, 1), -62: (-64, 1, 1), -95: (-64, -16, -16, 1)}
    ent = sorted([(v != 1, v, 8 * so, nm) for so, lst in enumerate(layer) for (nm, v0) in lst for v in parts.get(v0, (v0,))])
    vals = sorted(set(e[1] for e in ent) - {1}) + [-2048, 0.5, -0.5]
    sid = lambda v: o("ID") if v == 1 else o("SID", 128 * vals.index(v), 128 * vals.index(v) + 128)
    for v in vals:
        lin(sid(v), o("ID"), float(v))
    ms(o("ZER"), 0.0)
    mm(o("XA", 0, 192), o("ID"), o("ZER"), True, False)
    for k, (_, v, c, nm) in enumerate(ent):
        mm(o("XA", c, c + 8), sid(v), var[nm], False, k == len(ent) - 1, k and v == ent[k - 1][1])
    lin(o("WM"), o("XA", 0, 192))
    for k, v in enumerate((-0.5, 0.5)):
        mm(o("XB0", 128 * k, 128 * k + 128), o("ID"), o("SH0"), True, False)
        mm(o("XB0", 128 * k, 128 * k + 128), sid(v), o("ID"), False, True)
    lin(o("DM"), o("XB0", 0, 256))
    cp(o("D3"), o("DM", 0, 128))
    cp(o("D3", 15, 128, 16), o("DM", 0, 128, 16))
    for i in range(2 * NS):
        asel(o("CT", 160 * i + 80, 160 * i + 160), o("F2"), [[0, 80]], 0, 0)

    ctx[3] = "variables"
    for k in range(8):
        x, y, z = o("PW", 512 * k, 512 * k + 512), o(("MP0", "MP1", "KY1", "XB1")[k % 4]), o("EQ%d" % (k // 4), 512 * (k % 4), 512 * (k % 4) + 512)
        if k in FIXV:
            act(y, x, AF.Relu, HH, -254.0 * HH)
            tt(x, x, y, AL.subtract)
        else:
            ts(z, x, 255.0, -HH, AL.is_equal, AL.mult)
            mm(y, o("ID"), x, True, False)
            mm(y, o("ID"), z, False, True, True)
            (cp if k in EV else lin)(x, y)
    ctx[3] = "fills"
    fill(o("BW", 4608, 4624), 0)
    for (a, b, ps, n) in (("BOi", "BOu", "KY0", 288), ("GSi", "GSu", "KY1", 256)):
        ctx[3] = b
        lin(o("X2", 0, n), o(a), 1.0, -2048.0)
        add("V", "tr", (o("X3", 0, n), o("X2", 0, n)), [o("X2", 0, n)], [o("X3", 0, n)], n / 2 * CYC)
        for m0 in range(2):
            for m in range(8 if m0 else n // 32):
                for g0 in range(2):
                    c = 160 * m0 + 16 + 16 * (m0 - g0)
                    mm(o(ps, 2 * m + m0, 256, 16) if m < 8 else o(ps, 256, 272), o("ZP", c, c + 128),
                       o("X3", 32 * m + 16 * g0, 32 * m + 16 * g0 + 16), g0 == 0, g0 == 1, m % 4 + g0 > 0)
        shift(ON[b], o(b), o(ps, 0, nel(o(b))), 2048.0)

    def to_b(t, h, first, fac, x, top=None):
        H = str(h)
        y, ps, f = ("Y" + H, "KY" + H, "OF" + H) if first else ("Z" + H, "MP" + H, "OM" + H)
        scan(o(y), fac, x, 0.0, AL.mult, AL.add)
        for gq in range(8):
            mm(o(ps, 160, 168, p0=32 * (gq // 2), p1=32 * (gq // 2) + 32), o("FW", 16 - 16 * (gq % 2), 48 - 16 * (gq % 2)),
               o(y, 10 * gq + 2, 10 * gq + 10), gq % 2 == 0, gq % 2 == 1, gq > 0)
        f = o(f, 8 * (t % 2), 8 * (t % 2) + 8)
        if top:
            ts(f, o(ps, 160, 168), 2048.0, top, AL.add, AL.min)
        else:
            shift("V" if first else ON["OM"], f, o(ps, 160, 168), 2048.0)
        return f

    def message(t, h, off):
        H = str(h)
        m = o("MS" + H, 128 * (t % 2), 128 * (t % 2) + 128)
        top = 2048 if t == 0 else 2048 + 128 * (2 * (t - 1) + h + 1)
        act(m, o("MW", 0, top), AF.Abs, ind=off)
        mm(o("MP" + H, 0, 128), o("ID"), m)

    def tile(t, h, **k):
        return o("S%d" % h, 128 * t, 128 * t + 128, **k)

    def mask(out, x, b=cBias):
        act(out, x, AF.Sign, -1.0, b)

    def offers(t, h, m):
        H = str(h)
        XB = "XB" + H
        mm(o(XB, 128, 256), o("D3"), o("Q" + H))
        tt(o("ZX" + H), m, o(XB, 128, 256), AL.mult)
        x = o(XB, 384, 464)
        mm(x, o("ONE", 0, 128, p1=1), o("WO", 80 * t, 80 * t + 80, p1=1), True, False)
        mm(x, o("Q" + H), o("WQ"), False, False)
        mm(x, o("ZX" + H), o("WZ"), False, True)

    def update(t, h):
        H = str(h)
        XA, XB = "XA", "XB" + H
        s, q = tile(t - 1, h), o("Q" + H)
        i = 2 * (t - 1) + h
        c = 128 if t == NS else 0
        mm(o(XB, 0, 128), o("DM", 0, 128), q, True, False)
        mm(o(XB, 0, 128), o("E15", p1=1), o("LC", 128 * h, 128 * h + 128, p1=1), False, True)
        mm(o(XB, 256, 384), o("E15", p1=1), o("LC", 128 * h, 128 * h + 128, p1=1), True, False)
        mm(o(XB, 256, 384), o("LN", p1=1), o("CB", c, c + 128, p1=1), False, False)
        mm(o(XB, 256, 384), o("DM", 128, 256), q, False, t == NS)
        m1, m2 = o("M" + H, 0, 128), o("M" + H, 128, 256)
        if t == NS:
            x = o("TP", 128 * h, 128 * h + 128, p0=96, p1=112)
            y = o("CT", 160 * i + 1, 160 * i + 160, 10)
            add("P", "pt", (x, y, o("ID")), [y, o("ID")], [x], 128 * PCYC)
            cp(tile(t - 1, h, p0=96, p1=112), x)
            mm(o(XA, 128, 256), o("BC", 0, 128), s)
            mask(m1, o(XA, 128, 256))
            tt(o("T1" + H), m1, o(XB, 0, 128), AL.mult)
            tt(o("QF" + H), o("T1" + H), o(XB, 256, 384), AL.add)
        x = o("TP", 128 * h, 128 * h + 128, p0=96, p1=120)
        for (z, y) in ((x, o("CT", 160 * i + 1, 160 * i + 240, 10)), (x[:2] + (104,) + x[3:], o("RU" + H, 160, 1360, 170))):
            ctx[4] = z != x
            add("P", "pt", (z, y, o("ID")), [y, o("ID")], [z], 128 * PCYC)
        (cp if ON["S"] == "V" else lin)(tile(t - 1, h, p0=96, p1=120), x)
        if t < NS:
            mm(o(XA, 128, 256), o("BC", 0, 128), s)
        mm(o(XA, 256, 384) if t < NS else o(XB, 128, 256), o("BC", 128, 256), s)
        mm(o(XA, 0, 128, p1=96), o("WM", 0, 96), s)
        if t < NS:
            mask(m1, o(XA, 128, 256))
            mask(m2, o(XA, 256, 384), cB2)
        act(tile(t, h, p1=96), o(XA, 0, 128, p1=96), AF.Relu)
        s = tile(t, h)
        if t == NS:
            m2 = o(XB, 128, 256)
            ts(m2, m2, cB2, None, AL.is_lt)
            mm(o(XA, 384, 512, p1=24), o("XV", 0, 24), s)
            lin(o("YP", 128 * h, 128 * h + 128, p1=24), o(XA, 384, 512, p1=24))
            for k in range(3):
                x = o("YP", 128 * h, 128 * h + 128, p0=8 * k, p1=8 * k + 8)
                dma("S", ("ext", "ys", (256 * (k + 1) + 128 * h, 256 * (k + 1) + 128 * h + 128)), x, [x], [], 4096)
            y = o("YQ", 128 * h, 128 * h + 128)
            tt(y, o("QF" + H), m2, AL.mult)
            dma("S", ("ext", "yq", (128 * h, 128 * h + 128)), y, [y], [], 65536)
            return
        mm(o(XB, 256, 384), sid(-128), m2, False, True)
        tt(o("T1" + H), m1, o(XB, 0, 128), AL.mult)
        tt(q, o("T1" + H), o(XB, 256, 384), AL.add)
        if t < NS - 1:
            mm(o(XA, 384, 512), o("BC", 256, 384), s)
            mask(o("M3" + H), o(XA, 384, 512))
            offers(t, h, o("M3" + H))

    def start(h):
        H = str(h)
        ctx[3] = "start" + H
        XA, XB = "XA", "XB" + H
        s, q = tile(0, h), o("Q" + H)
        hs = lambda b, **k: o(b, 128 * h, 128 * h + 128, **k)
        lin(s, one, n8(15))
        ts(tile(0, h, p1=40), hs("STi", p1=40), cS1[:2] + (40,) + cS1[3:], None, AL.mult)
        cp(o("CU" + H), o("CLs"), o("BOu", 256 + 8 * h, 264 + 8 * h))
        cp(o("CW", 4096 + 256 * h, 4352 + 256 * h, 2), o("CU" + H))
        for x in (o("VB" + H), o("RS" + H, 143, 1488, 17)):
            fill(x, 0)
            fill(x[:5] + (10 * x[5],), -1)
        asel(o("RU" + H, 143, 1488, 17), o("F2"), [[0, 80]], 0, 0)
        lin(o("Y" + H, 1, 80, 10), o("ONE", 0, 8), cK, 2048.0 + 256 * h)
        mm(o(XA, 128, 256), o("BC", 0, 128), s)
        mm(o(XA, 256, 384), o("BC", 128, 256), s)
        mask(o("M" + H, 0, 128), o(XA, 128, 256))
        mask(o("M" + H, 128, 256), o(XA, 256, 384), cB2)
        mm(o(XB, 0, 128), o("LN", p1=1), hs("LC", p1=1), True, False)
        mm(o(XB, 0, 128), o("LN", p1=1), o("CB", 256, 384, p1=1), False, False)
        mm(o(XB, 0, 128), sid(-2048), o("M" + H, 128, 256), False, True)
        ts(o("CH" + H), hs("Qi"), -384.0, None, AL.add)
        tt(q, o("CH" + H), o(XB, 0, 128), AL.max)
        offers(0, h, o("M" + H, 0, 128))
        message(0, h, to_b(1, h, False, o("F2", 0, 80), o(XB, 384, 464), 2047.0))
        mm(o(XA, 0, 128, p1=96), o("WM", 96, 192), s)
        act(tile(0, h, p1=96), o(XA, 0, 128, p1=96), AF.Relu)
        mm(o(XA, 384, 512), o("BC", 256, 384), s)
        mask(o("M3" + H), o(XA, 384, 512))
        offers(0, h, o("M3" + H))

    def tables():
        for (a, b) in zip(CC, CC[1:]):
            if b <= CA:
                act(o("CW", 16 * a, 16 * b), o("CLs"), AF.Copy, ind=o("GSu", a, b))
            else:
                cp(o("CW", 16 * a, 16 * b), o("CLs"), o("GSu", a, b))
        for r in range(8):
            x, f = o("BW", 512 * r, 512 * r + 512), o("BOu", 32 * r, 32 * r + 32)
            if r < BV:
                ts(x, o("PW"), -1.0, None, AL.mult, None, f)
            else:
                act(x, o("PW"), AF.Copy, -1.0, ind=f)
        dma("S", ("rows", "Qi", 0, 256), ("ext", "s0", None), [], [o("Qi")], 8192)

    chain = {"A": [], "V": [], "G": [], "X": []}

    def wide(t, h):
        H = str(h)
        P, EQ, KY = "P" + H, "EQ" + H, "KY" + H
        shift(ON["CH"], o("CH" + H), o("CU" + H), -2048.0)
        mm(o(KY, 0, 136), o("CH" + H), o("IX"), True, False)
        mm(o(KY, 16, 136, 17), o("IDh"), o("Y" + H, 1, 80, 10), False, False)
        pv = PV[t]
        for a in range(128 - pv, 128, PS):
            cp(o(P, 16 * a, 16 * min(a + PS, 128)), o("PW"), o("CU" + H, a, min(a + PS, 128)))
        cut = [2 * int((128 - pv) * k / 2) for k in GP]
        for (a, b) in zip(cut, cut[1:]):
            chain["A"] = [act(o(P, 16 * a, 16 * b), o("PW"), AF.Copy, ind=o("CU" + H, a, b), after=chain["A"])]
        for (a, b) in PIECES:
            for k in range(16):
                m = o("MP" + H, a, b) if k >= NM else o("MS" + H, 128 * (t % 2) + a, 128 * (t % 2) + b)
                chain["V"] = [tt(o(EQ, 128 * k + a, 128 * k + b), o(P, 16 * a + k, 16 * b, 16), m, AL.not_equal, after=chain["V"])]
        for k in range(16):
            mm(o(KY, k, 136, 17), o(P, k, 2048, 16), o("INp"), False, False, k % 4 > 0)
        mm(o(KY, 0, 136), tile(t, h), o("PN"), False, False)
        for k in range(16):
            mm(o(KY, k, 136, 17), o(EQ, 128 * k, 128 * k + 128), o("INe"), False, k == 15, k % 2 and k < 12)

    def choose(t, h):
        H = str(h)
        i = 2 * t + h
        last = t == NS - 1
        scan(o("RS" + H, 0, 1360, 10), o("RD"), o("KY" + H, 0, 136), 0.0, AL.add, AL.max)
        rs = o("RS" + H, 160, 1360, 170)
        rv = o("RS" + H, 143, 1488, 17)
        if TWICE:
            scan(o("RU" + H, 0, 1360, 10), o("RD"), o("KY" + H, 0, 136), 0.0, AL.add, AL.max)
        else:
            cp(o("RU" + H, 160, 1360, 170), rs)
        nf, ub = o("CT", 160 * i + 81, 160 * i + 160, 10), o("RU" + H, 143, 1488, 17)
        land, x = o("CT", 160 * i + 160, 160 * i + 240), o("CT", 160 * i + 80, 160 * i + 160)
        if last:
            ts(o("VB" + H, 1, 80, 10), rs, 65 * 16384.0 + 2560.0, None, AL.max)
        fb = to_b(t, h, True, ub, o("VB" + H) if last else rv)
        ts(nf, rs, 65.5 * 16384.0, None, AL.is_lt)
        f = to_b(t, h, False, ub, rv) if last else to_b(t, h, False, x, o("XB" + H, 384, 464))
        snd = o("SND", 128 * i, 128 * i + 128)
        tt(snd, o("BW"), o("MS" + H, 128 * (t % 2), 128 * (t % 2) + 128), AL.min, fb)
        sends = [(land, x, "af%d" % i, 2600.0), (o("MW", 2048 + 128 * i, 2048 + 128 * i + 128), snd, "ad%d" % i, 3200.0)]
        land = sends[1][0]
        for (a, b, sem, way) in sends:
            j = [add("G", "rdma", (a, b, t, sem), [b], [], 500.0 + (0.0 if chain["G"] else OPEN), 0.0, chain["G"])]
            add("X", "arr", (sem, j[0]), [], [a], 0.0, way, after=j + chain["X"])
            chain["G"], chain["X"] = j, [add("X", "busy", ("bu",), [], [], 0.0, way - 1400.0, after=j)]
        if not last:
            act(o("CU" + H), o("CW"), AF.Copy, ind=fb)
            message(t + 1, h, f)
        if i == 2 * NS - 3:
            dma("S", ("rows", "CW", 0, 4096), ("ext", "gs", None), [], [o("CW", 0, 4096)], 131072)
            lin(o("CW", 4096, 4608, 2), o("Qi"))
        if last:
            y = o("YS", 128 * h, 128 * h + 128)
            cp(y, o("CW"), f)
            dma("S", ("ext", "ys", (128 * h, 128 * h + 128)), ("rows", "YS", 128 * h, 128 * h + 128), [y], [], 4096)
            x = o("MO", 128 * i, 128 * i + 128)
            act(x, land, AF.Abs)
            dma("S", ("ext", "mn", (128 * i, 128 * i + 128)), x, [x], [], 32768)

    def arrived():
        for t in range(NS - 1):
            act(o("MO", 256 * t, 256 * t + 256), o("MW", 2048 + 256 * t, 2304 + 256 * t), AF.Abs)
        for t in range(NS - 1):
            x, y = o("MO", 256 * t, 256 * t + 256), o(("MP0", "KY0")[t % 2], 256, 512)
            for h in range(2):
                mm(o(y[0], 256 + 128 * h, 384 + 128 * h), o("BS"), tile(t, h))
            tt(x, x, y, AL.min)
            dma("S", ("ext", "mn", (256 * t, 256 * t + 256)), x, [x], [], 65536)

    start(0)
    start(1)
    tables()
    for t in range(NS):
        for h in range(2):
            ctx[0], ctx[1], ctx[2] = ("step" if t < NS - 1 else "last%d" % h), {}, (t, h)
            wide(t, h)
            choose(t, h)
            if t == NS - 1 and h == 0:
                arrived()
            update(t + 1, h)
    return ops


def knots(ops):
    res = []
    home = []
    for i, p in enumerate(ops):
        if p["join"]:
            q = res[-1]
            q["cost"] += p["cost"]
            q["calls"].append(i)
        else:
            q = dict(p)
            q["deps"], q["calls"] = {}, [i]
            res.append(q)
        home.append(len(res) - 1)
        for j, w in p["deps"].items():
            if home[j] != home[i]:
                q["deps"][home[j]] = q["deps"].get(home[j], False) or w
    prune(res)
    return res


CASES = ((0.83, 1.1, 155.0, 0.4, 0.65, 300.0, 58.5), (0.83, 1.56, 165.0, 0.44, 0.65, 250.0, 63.0), (0.9, 2.0, 180.0, 0.5, 0.7, 260.0, 75.3),
         (1.2, 1.15, 190.0, 0.55, 0.7, 230.0, 81.5), (1.2, 2.0, 180.0, 0.6, 0.7, 330.0, 97.5), (0.9, 1.4, 190.0, 0.56, 0.65, 230.0, 68.3))
MID = (0.85, 1.5, 170.0, 0.46, 0.65, 250.0)
PERIOD, FIRST, BUS = 6848.0, 13300.0, 250.0
OWN = 1.0
HAND = True
SEED, HEAT, AHEAD = 1, 2.0, 2000.0
SHIFT = {}
DUE = {("V", "CH"): (-380,), ("V", "P"): (-770, -1660), ("A", "P"): (-3090,), ("V", "EQ"): tuple(range(0, 1650, 106)),
       ("P", "KY"): (-160, -100, -80, 210, 320, 630, 740, 800, 850, 910, 1010, 1230, 1440, 1550, 1650, 1760, 1860, 2710),
       ("V", "RS"): (2090,), ("V", "RU"): (2200,), ("V", "CT"): (2370,), ("V", "VB"): (2380,), ("V", "Y"): (2480,), ("V", "OF"): (2990,),
       ("V", "SND"): (3210,), ("G", "CT"): (2580,), ("X", "af"): (2600,), ("X", "bu"): (2600, 3600), ("G", "MW"): (3590,), ("X", "ad"): (3600,),
       ("A", "CU"): (3210,), ("A", "MO"): (4000,), ("V", "Z"): (5120,), ("P", "MP"): (5360, 6620), ("V", "OM"): (5740,), ("A", "MS"): (6220,),
       ("P", "TP"): (5460,), ("V", "S"): (5840,), ("P", "XA"): (6360, 6410, 6460, 7420), ("A", "M"): (6860, 6970), ("A", "S"): (7080,),
       ("A", "M3"): (9440,), ("P", "XB"): (6300, 6580, 6920, 6970, 7920, 7970, 9670, 10310, 10450, 10710), ("V", "T1"): (8830,),
       ("V", "Q"): (9390,), ("V", "ZX"): (9940,)}
EARLY = {"variables": 500, "BOu": 3000, "start0": 4000, "GSu": 7000, "start1": 8000, "CW": 13000, "BW": 7500, "CU0": 100, "CU1": 200}
STRETCHES = ((0.0, 0.4, 0.45), (0.72, 2.0, 0.2), (0.3, 0.55, 0.1), (0.5, 0.8, 0.1), (0.15, 0.4, 0.15))
GAP = {("V", "CW"): 800.0, ("A", "CW"): 900.0}


def graph(ops, c, gt, l, f, pe=1.0, BUS=BUS):
    cost = []
    lat = []
    bus = 0.0
    for p in ops:
        k = {"ts": 6, "tt": 4, "cp": 2, "act": 5}.get(p["kind"])
        v = p["cost"]
        if p["eng"] in "VAPG" and p["kind"] not in ("dma", "rdma"):
            if k is not None and p["args"][k] is not None:
                v += nel(p["args"][0]) * (gt - GTH) * CYC
            v *= c / CYC * (pe if p["eng"] == "P" else 1.0)
        cost.append(v)
        v = p["lat"] * (f if p["eng"] == "X" else 1.0)
        if p["kind"] == "dma":
            bus = p["args"][2] / BUS + (bus - 60.0 if p["args"][1][0] == "ext" and p["args"][0][0] != "rows" else 0.0)
            v += bus
        lat.append(v)
    fw = [[(j, cost[j] + (lat[j] + l if ops[j]["eng"] != p["eng"] or p["eng"] == "X" else lat[j] + OWN * l if p["deps"][j] else 0.0)) for j in p["near"]] for p in ops]
    return cost, lat, fw


def prune(ops):
    anc = []
    for p in ops:
        hard = 0
        a = 0
        for j, w in p["deps"].items():
            a |= anc[j] | (1 << j)
            if w or ops[j]["eng"] != p["eng"]:
                hard |= anc[j]
        anc.append(a)
        p["near"] = [j for j in p["deps"] if ops[j]["lat"] or not hard >> j & 1]


def replay(eng, g, order):
    cost, lat, fw = g
    beg = [0.0] * len(eng)
    free = {}
    end = 0.0
    for i in order:
        e = eng[i]
        s = free.get(e, 0.0)
        for j, d in fw[i]:
            if beg[j] + d > s:
                s = beg[j] + d
        beg[i] = s
        if e != "X":
            free[e] = s + cost[i]
        if s + cost[i] + lat[i] > end:
            end = s + cost[i] + lat[i]
    return end


def once(eng, g, succ, due, slack):
    cost, lat, fw = g
    n = len(eng)
    left = [len(x) for x in fw]
    beg = [0.0] * n
    ready = {e: {} for e in "VAPGSX"}
    free = {e: 0.0 for e in ready}
    nxt = {}
    order = []
    for i in range(n):
        if left[i] == 0:
            ready[eng[i]][i] = 0.0
            nxt[eng[i]] = 0.0
    while nxt:
        e = min(nxt, key=nxt.get)
        r = ready[e]
        lim = nxt[e] + slack[e]
        i = min([k for k in r if r[k] <= lim], key=lambda k: due[k])
        s = max(r.pop(i), free[e])
        beg[i] = s
        if e != "X":
            free[e] = s + cost[i]
        order.append(i)
        if r:
            nxt[e] = max(min(r.values()), free[e])
        else:
            del nxt[e]
        for k in succ[i]:
            left[k] -= 1
            if left[k] == 0:
                v = max([beg[j] + d for j, d in fw[k]])
                x = eng[k]
                ready[x][k] = v
                v = max(v, free[x])
                if v < nxt.get(x, 1e18):
                    nxt[x] = v
    return order


def plan(ops, climbs=200, tries=0, polish=(300, 160000)):
    n = len(ops)
    eng = [p["eng"] for p in ops]
    sets = [(graph(ops, *c[:-1]), c[-1]) for c in CASES]
    mid = graph(ops, *MID)
    succ = [[] for _ in range(n)]
    for i, p in enumerate(ops):
        for j in p["near"]:
            succ[j].append(i)
    names = {}
    cls = []
    base = [None] * n
    table = {}
    for i, p in enumerate(ops):
        c, e, nm, k = p["cls"]
        if not c:
            cls.append(names.setdefault((p["part"], e, nm), len(names)))
            if p["kind"] == "dma" and nm != "rows":
                base[i] = -20000.0
            elif nm in EARLY or p["part"] in EARLY:
                base[i] = EARLY.get(nm, EARLY.get(p["part"])) + 0.1 * i + GAP.get((e, nm), 0.0) * k
                if (e, nm) in GAP:
                    cls[-1] = names.setdefault((p["part"], e, nm, k), len(names))
            continue
        t, h = p["at"]
        v = DUE.get((e, nm), ())
        v = float(v[k - 1]) if k <= len(v) else 7000.0 + k
        base[i] = FIRST + PERIOD * (t + 0.5 * h) + v
        table[p["cls"]] = v
        cls.append(names.setdefault((c, e, nm, k), len(names)))
    for i in range(n - 1, -1, -1):
        if base[i] is None:
            base[i] = min([base[k] - d - (AHEAD if ops[k]["at"] else 0.0) for k in succ[i] for j, d in mid[2][k] if j == i] + [60000.0])
    cls = np.array(cls)
    base = np.array(base) + 0.001 * np.arange(n)
    slack = {"V": 150.0, "A": 250.0, "P": 300.0, "G": 200.0, "S": 0.0, "X": 0.0}

    def score(d):
        r = once(eng, mid, succ, (base + d[cls]).tolist(), slack)
        v = [replay(eng, g, r) / w for (g, w) in sets]
        return (sum(v) / len(v) + max(v)) / 2, r
    rng = np.random.default_rng(SEED)
    delta = np.array([float(SHIFT.get(" ".join(str(x) for x in c), 0)) for c in names])
    first = best = cur = score(delta) + (delta,)
    rep = [k for c, k in names.items() if c[0] == "step"]
    for it in range(climbs * (tries + 1)):
        if it % climbs == 0:
            cur = first if it < climbs * tries else best
        d = cur[2].copy()
        if it % 2:
            held = waits(ops, eng, sets[int(rng.integers(len(sets)))][0], cur[1])
            held = [(i, y) for (i, y) in held if cls[i] != cls[y]]
            i, y = held[int(rng.integers(len(held)))]
            gap = max(0.0, base[i] + d[cls[i]] - base[y] - d[cls[y]]) + 10.0 + 300.0 * float(rng.random()) ** 2
            if it % 4 == 1:
                d[cls[i]] -= gap
            else:
                d[cls[y]] += gap
        else:
            for k in range(1 + it % 3):
                x = rep[int(rng.integers(len(rep)))] if it % 4 else int(rng.integers(len(names)))
                d[x] += float(rng.normal()) * (200.0, 700.0, 2500.0)[(it // 4) % 3]
        v = score(d)
        if v[0] <= cur[0] + HEAT * float(rng.random()) * (1.0 - it % climbs / climbs):
            cur = v + (d,)
            if v[0] < best[0]:
                best = cur
    beg = starts(eng, mid, best[1])
    per = [i for i in range(n) if ops[i]["at"] == (2, 0) and ops[i]["cls"][1:] == ("V", "RS", 1)][0]
    nxt = [i for i in range(n) if ops[i]["at"] == (2, 1) and ops[i]["cls"][1:] == ("V", "RS", 1)][0]
    half = PERIOD / 2 if HAND else beg[nxt] - beg[per]
    names = {}
    cls = np.array([names.setdefault(p["cls"] if p["at"] and 1 <= p["at"][0] < NS - 1 else i, len(names)) for i, p in enumerate(ops)])
    ref = {p["cls"]: beg[i] for i, p in enumerate(ops) if p["at"] == (2, 0)}
    if HAND:
        ref = {c: beg[per] + (table[c] - DUE["V", "RS"][0]) * 2 * half / PERIOD for c in ref}
    base = np.array([ref[p["cls"]] + half * (2 * p["at"][0] + p["at"][1] - 4) if p["at"] and 1 <= p["at"][0] < NS - 1 and p["cls"] in ref
                     else beg[i] for i, p in enumerate(ops)])
    near = [p["near"] for p in ops]

    def rank(due, d, c, bound):
        for i in range(n):
            for j in near[i]:
                if due[j] >= due[i]:
                    due[i] = due[j] + 0.01
        r = sorted(range(n), key=lambda i: due[i])
        x = replay(eng, sets[c][0], r) / sets[c][1]
        if x > bound:
            return None
        v = [x if k == c else replay(eng, g, r) / w for k, (g, w) in enumerate(sets)]
        return (sum(v) / len(v) + max(v)) / 2, r, d, due, v, {}
    cur = top = rank(base.tolist(), np.zeros(len(names)), 0, 1e9)
    for it in range(polish[0]):
        c = int(rng.integers(len(sets)))
        if c not in cur[5]:
            cur[5][c] = [(i, y) for (i, y) in waits(ops, eng, sets[c][0], cur[1]) if cls[i] != cls[y]]
        i, y = cur[5][c][int(rng.integers(len(cur[5][c])))]
        d = cur[2].copy()
        far = 1.0 + (0.0, 60.0, 300.0)[it % 3] * float(rng.random())
        if it % 7 == 0:
            d[cls[y]] = cur[3][y] + 1500.0 * float(rng.normal()) - base[y]
        elif it % 2:
            d[cls[i]] = cur[3][y] - far - base[i]
        else:
            d[cls[y]] = cur[3][i] + far - base[y]
        heat = HEAT * float(rng.random()) * (1.0 - it / polish[0])
        v = rank((base + d[cls]).tolist(), d, c, cur[4][c] + 2.0 * heat + 1.0)
        if v and v[0] <= cur[0] + heat:
            cur = v
            if v[0] < top[0]:
                top = v
    order, v = top[1], top[0]
    for (a, b, share) in STRETCHES:
        beg = starts(eng, mid, order)
        order = sorted(order, key=lambda i: beg[i])
        end = beg[order[-1]]
        lo, hi = [len([1 for x in beg if x < z * end]) for z in (a, b)]
        order, v = stretch(ops, eng, sets, succ, order, lo, hi, int(share * polish[1]), rng)
    return order, v, top[0], best[0]


def stretch(ops, eng, sets, succ, order, lo, hi, tries, rng):
    n = len(ops)
    seg = order[lo:hi]
    where = [0] * n
    for i in seg:
        where[i] = 1
    for i in order[hi:]:
        where[i] = 2
    fix = []
    for (g, w) in sets:
        cost, lat, fw = g
        beg = starts(eng, g, order)
        tail = [cost[i] + lat[i] for i in range(n)]
        nxt = {}
        for i in reversed(order[hi:]):
            if eng[i] != "X":
                tail[i] = max(tail[i], cost[i] + nxt.get(eng[i], 0.0))
                nxt[eng[i]] = tail[i]
            for j, d in fw[i]:
                tail[j] = max(tail[j], d + tail[i])
        free = {e: 0.0 for e in "VAPGSX"}
        end = 0.0
        for i in order[:lo]:
            end = max(end, beg[i] + tail[i])
            if eng[i] != "X":
                free[eng[i]] = beg[i] + cost[i]
        row = {i: (eng[i], max([0.0] + [beg[j] + d for j, d in fw[i] if where[j] == 0]), [(j, d) for j, d in fw[i] if where[j]],
                   0.0 if eng[i] == "X" else cost[i], tail[i]) for i in seg}
        fix.append((row, free, end, nxt, w, beg))

    def run(c, r):
        row, free, end, nxt, w, beg = fix[c]
        free = dict(free)
        for i in r:
            e, s, fw, co, ta = row[i]
            if co and free[e] > s:
                s = free[e]
            for j, d in fw:
                if beg[j] + d > s:
                    s = beg[j] + d
            beg[i] = s
            free[e] = s + co
            if s + ta > end:
                end = s + ta
        for e, x in nxt.items():
            if free[e] + x > end:
                end = free[e] + x
        return end / w

    def held(c, r):
        row, free, end, nxt, w, beg = fix[c]
        run(c, r)
        before = {}
        last = {}
        for i in r:
            before[i] = last.get(eng[i])
            last[eng[i]] = i
        i = max(r, key=lambda k: beg[k] + max(row[k][4], row[k][3] + nxt.get(eng[k], 0.0) if last[eng[k]] == k else 0.0))
        res = []
        while i is not None:
            j = max(row[i][2] + [(None, row[i][1])], key=lambda x: x[1] + (0.0 if x[0] is None else beg[x[0]]))
            y = before[i]
            if row[i][3] and y is not None and beg[y] + row[y][3] > j[1] + (0.0 if j[0] is None else beg[j[0]]):
                res.append((i, y))
                i = y
            else:
                i = j[0]
        return res

    def moved(r, i, y, early):
        a, b = r.index(y), r.index(i)
        part = r[a:b + 1]
        go = {i if early else y}
        for k in (reversed(part) if early else part):
            if k in go:
                go.update(ops[k]["near"] if early else succ[k])
        if (y if early else i) in go:
            return None
        x, z = [k for k in part if k in go], [k for k in part if k not in go]
        return r[:a] + (x + z if early else z + x) + r[b + 1:]
    v = [run(c, seg) for c in range(len(sets))]
    cur = top = ((sum(v) / len(v) + max(v)) / 2, seg, v, {})
    for it in range(tries):
        c = int(rng.integers(len(sets)))
        if c not in cur[3]:
            cur[3][c] = held(c, cur[1])
        if not cur[3][c]:
            continue
        i, y = cur[3][c][int(rng.integers(len(cur[3][c])))]
        early = it % 2 == 0
        if it % 3:
            q = [k for k in cur[1] if eng[k] == eng[i]]
            k = 1 + int(8 * float(rng.random()) ** 2)
            if early:
                y = q[max(0, q.index(y) - k)]
            else:
                i = q[min(len(q) - 1, q.index(i) + k)]
        r = moved(cur[1], i, y, early)
        if r is None:
            continue
        heat = 0.5 * HEAT * float(rng.random()) * (1.0 - it / tries)
        x = run(c, r)
        if x > cur[2][c] + 2.0 * heat + 1.0:
            continue
        v = [x if k == c else run(k, r) for k in range(len(sets))]
        s = (sum(v) / len(v) + max(v)) / 2
        if s <= cur[0] + heat:
            cur = (s, r, v, {})
            if s < top[0]:
                top = cur
    return order[:lo] + top[1] + order[hi:], top[0]


def starts(eng, g, order):
    cost, lat, fw = g
    beg = [0.0] * len(eng)
    free = {}
    for i in order:
        s = max([free.get(eng[i], 0.0)] + [beg[j] + d for j, d in fw[i]])
        beg[i] = s
        if eng[i] != "X":
            free[eng[i]] = s + cost[i]
    return beg


def waits(ops, eng, g, order):
    cost, lat, fw = g
    beg = [0.0] * len(eng)
    why = [-1] * len(eng)
    last = {}
    for i in order:
        e = eng[i]
        y = last.get(e, -1)
        s = beg[y] + cost[y] if y >= 0 else 0.0
        for j, d in fw[i]:
            if beg[j] + d >= s:
                s, y = beg[j] + d, j
        beg[i], why[i] = s, y
        if e != "X":
            last[e] = i
    i = max(order, key=lambda k: beg[k] + cost[k] + lat[k])
    res = []
    while why[i] >= 0:
        if why[i] not in ops[i]["deps"]:
            res.append((i, why[i]))
        i = why[i]
    return res


CACHE = {}


def rank_program(g, core, T, topo):
    rank = T.rank_of(core)
    if rank is None:
        return
    if "ops" not in CACHE:
        CACHE["ops"] = build()
        nodes = knots(CACHE["ops"])
        CACHE["order"] = [i for k in plan(nodes)[0] for i in nodes[k]["calls"]]
    ops, order = CACHE["ops"], CACHE["order"]
    nr = len(T.cores)
    qs = {"V": g.vector, "A": g.scalar, "P": g.tensor, "G": g, "S": g.sync}
    dest = [T.cores[(rank + 1 + t % (nr - 1)) % nr] for t in range(NS)]
    engs = set(range(16))
    for a in T.cores:
        for b in T.cores:
            if a != b:
                assert topo.may_write(a, b)
                engs &= set(topo.engines(a, b))
    engs = sorted(engs)
    ne = len(engs)
    mask = sum(1 << e for e in engs)

    def ap(x):
        if not isinstance(x, tuple):
            return x
        if x[0] == "ext":
            return T[x[1]][:] if x[2] is None else T[x[1]][:, x[2][0]:x[2][1]]
        if x[0] == "rows":
            return T[x[1]][0:128:16, x[2]:x[3]]
        if x[5] == 1:
            return T[x[0]][x[1]:x[2], x[3]:x[4]]
        return T[x[0]][x[1]:x[2], x[3]:x[4]:x[5]]

    def src(x, ind):
        return ap(x) if ind is None else ap(x).indirect(ap(ind))

    pos = {}
    for k, i in enumerate(order):
        pos[i] = k
    seen = {}
    need = set()
    for i in order:
        e = ops[i]["eng"]
        if e == "X":
            continue
        best = {}
        for j, w in ops[i]["deps"].items():
            pj = ops[j]
            if w and pj["kind"] not in ("dma", "rdma", "arr") and pos[j] > seen.get((e, pj["eng"]), -1):
                best[pj["eng"]] = max(best.get(pj["eng"], -1), pos[j])
        for k, v in best.items():
            seen[e, k] = v
            need.add(order[v])
    mark = {}
    cnt = {}
    nd = 0
    for i in order:
        p = ops[i]
        if p["kind"] == "dma":
            mark[i] = ("d%d" % nd, 16)
            nd += 1
        elif p["kind"] == "arr":
            mark[i] = (p["args"][0], ne)
        elif i in need:
            cnt[p["eng"]] = cnt.get(p["eng"], 0) + 1
            mark[i] = ("c" + p["eng"], cnt[p["eng"]])
    waited = {}
    seen = {}
    nloc = 0
    for i in order:
        p = ops[i]
        e, kind, a = p["eng"], p["kind"], p["args"]
        if e == "X":
            continue
        q = qs[e]
        want = {}
        for j, w in p["deps"].items():
            pj = ops[j]
            if not w or pj["kind"] == "rdma":
                continue
            if pj["kind"] in ("dma", "arr"):
                want[mark[j][0]] = mark[j][1]
            elif pos[j] > seen.get((e, pj["eng"]), -1):
                key = "c" + pj["eng"]
                if key not in want or pos[j] > want[key][0]:
                    want[key] = (pos[j], pj["eng"])
        for s, v in sorted(want.items()):
            if isinstance(v, tuple):
                seen[e, v[1]] = v[0]
                v = mark[order[v[0]]][1]
            if waited.get((e, s), 0) < v:
                waited[e, s] = v
                q.wait_ge(T.sem[s], v)
        if kind == "ts":
            if a[5] is None:
                r = q.tensor_scalar(ap(a[0]), src(a[1], a[6]), ap(a[2]), None, a[4])
            else:
                r = q.tensor_scalar(ap(a[0]), src(a[1], a[6]), ap(a[2]), ap(a[3]), a[4], a[5])
        elif kind == "tt":
            r = q.tensor_tensor(ap(a[0]), src(a[1], a[4]), ap(a[2]), a[3])
        elif kind == "cp":
            r = q.tensor_copy(ap(a[0]), src(a[1], a[2]))
        elif kind == "ms":
            r = q.memset(ap(a[0]), a[1])
        elif kind == "red":
            r = q.tensor_reduce(ap(a[0]), ap(a[1]), AxisListType.X, AL.add)
        elif kind == "tr":
            r = q.transpose(ap(a[0]), ap(a[1]))
        elif kind == "scan":
            r = q.tensor_tensor_scan(ap(a[0]), ap(a[1]), ap(a[2]), a[3], a[4], a[5])
        elif kind == "act":
            if a[4] != 0.0:
                r = q.activation(ap(a[0]), src(a[1], a[5]), a[2], bias=ap(a[4]), scale=ap(a[3]))
            elif a[3] != 1.0:
                r = q.activation(ap(a[0]), src(a[1], a[5]), a[2], scale=ap(a[3]))
            else:
                r = q.activation(ap(a[0]), src(a[1], a[5]), a[2])
        elif kind == "mm":
            r = q.matmul(ap(a[0]), ap(a[1]), ap(a[2]), a[3], a[4])
        elif kind == "pt":
            r = q.transpose(ap(a[0]), ap(a[1]), ap(a[2]))
        elif kind == "iota":
            if SCRATCH[a[0][0]][2] == I32:
                r = q.iota(ap(a[0]), a[1], a[2], a[3])
            else:
                r = q.iota(ap(a[0]), a[1], a[2], a[3], allow_small_or_imprecise_dtypes=True)
        elif kind == "asel":
            r = q.affine_select(ap(a[0]), ap(a[1]), a[2], a[5], a[6], a[3], a[4])
        elif kind == "dma":
            r = q.dma_start(ap(a[0]), ap(a[1]))
        elif kind == "rdma":
            rid, pid, _ = topo.addr(dest[a[2]])
            q.remote_dma(ap(a[0]), ap(a[1]), T.sem[a[3]], T.sem.loc, pid, rid, mask)
            nloc += ne
            continue
        if i in mark:
            r.then_inc(T.sem[mark[i][0]], 16 if kind == "dma" else 1)
    g.wait_ge(T.sem.loc, nloc)
    top = {}
    for i, (s, v) in mark.items():
        top[s] = max(top.get(s, 0), v)
    for s, v in sorted(top.items()):
        if ("S", s) not in waited or waited["S", s] < v:
            g.sync.wait_ge(T.sem[s], v)
